import numpy as np, ml_dtypes
CORES = [2,6,10,14,18,22,26,30]
N = 8
import mx_ref
BF = ml_dtypes.bfloat16
def gentries(a):
    return np.ascontiguousarray(a.reshape(8, 16, -1).transpose(0, 2, 1)).reshape(8, -1)
def gtable(e):
    e = np.asarray(e); return np.ascontiguousarray(e.reshape(8, -1, 16).transpose(0, 2, 1)).reshape(128, -1).astype(np.int32)
def gcols(t, e):
    v = np.concatenate([t.reshape(8, 16, -1, 4), np.zeros((8, 16, 1, 4), BF)], axis=2)
    return np.ascontiguousarray(np.stack([v[g][:, e[g]] for g in range(8)])).reshape(128, -1)
def tile(rs):
    return np.stack(rs, axis=2).reshape(128, -1).astype(BF)
def pick(q, e):
    c = np.concatenate([q[0].reshape(128, -1, 4), np.zeros((128, 1, 4), np.uint8)], axis=1); s = np.concatenate([q[1], np.ones((16, 1), np.uint8)], axis=1)
    return (np.ascontiguousarray(c[:, e].reshape(128, -1)), np.ascontiguousarray(s[:, e]))
def join(*qs):
    return (np.concatenate([q[0] for q in qs], axis=1), np.concatenate([q[1] for q in qs], axis=1))
def put(q, e, v):
    c, s = q[0].reshape(128, -1, 4).copy(), q[1].copy(); c[:, e] = v[0].reshape(128, -1, 4); s[:, e] = v[1]
    return (c.reshape(128, -1), s)
def pk(c, s):
    return (np.ascontiguousarray(c), mx_ref.live(s))
def emit(q):
    return q[0], q[1]
def packed(v, rng):
    q = [mx_ref.quantize(np.ascontiguousarray(v[r])) for r in range(N)]
    return np.stack([a for a, b in q]), np.stack([mx_ref.plane(b, rng) for a, b in q])
def values_of_codes():
    e, c = np.zeros((128, 128, 4), np.float32), np.zeros((128, 2, 4), np.uint8)
    e[np.arange(128), np.arange(128), 0] = 1
    c[:127, :, 0] = np.arange(256).reshape(2, 128).T[:127]
    return mx_ref.matmul(mx_ref.quantize(e.reshape(128, 512).astype(BF)), (c.reshape(128, 8), np.full((16, 2), 127, np.uint8))).T.reshape(-1).astype(np.float64)
CODE_VALUE, SCALE_VALUE = values_of_codes(), 2.0 ** (np.arange(256) - 127.0)
def decode(q):
    return (CODE_VALUE[q[0]].reshape(16, 8, -1, 4) * SCALE_VALUE[q[1]][:, None, :, None] + 0.0).reshape(128, -1).astype(np.float32)
def f(rng, *shape):
    return mx_ref.flush((rng.standard_normal(shape, dtype=np.float32) * np.exp2(rng.integers(-2, 3, shape[:-1] + (1,)))).astype(BF))
def wide(rng, *shape, cols=0):
    v = rng.standard_normal(shape, dtype=np.float32) * np.exp2(rng.integers(-12, 13, shape)).astype(np.float32)
    if cols: v *= np.repeat(np.exp2(rng.integers(-cols, cols + 1, shape[:-2] + (1, shape[-1] // 4))) * (rng.random(shape[:-2] + (1, shape[-1] // 4)) > 0.0625), 4, axis=-1).astype(np.float32)
    return mx_ref.flush(v.astype(BF))
C = 256
TURN = [1, 2, 4]
def numbers_of(rng):
    return {"x": np.array(f(rng, N, 128, 4 * C)), "u": np.array(f(rng, N, 128, 512)), "v": np.array(f(rng, N, 128, 512))}
def rotors(rng):
    return np.argsort(rng.random((N, 8, C)), axis=2)
def stored(e):
    return np.stack([gtable(e[r]) for r in range(N)])
def layers(rng):
    return 2.0 * rng.random((N, 128, 4, 128, 4)) - 1.0
def kept(rng):
    w, i = layers(rng), np.arange(16)
    w[:, :, :, :16] = 0
    for b in range(4): w[:, i, b, i, b] = 1
    return w
def weights(rng, w):
    c, s = packed(np.ascontiguousarray(w).reshape(N, 128, 2048).astype(np.float32).astype(BF), rng)
    return {"wc": c, "ws": s}
def setup_inputs(rng):
    return {**numbers_of(rng), "p": stored(rotors(rng)), **weights(rng, layers(rng))}
def setup_inputs_ties(rng):
    d = numbers_of(rng)
    o = rng.permutation(N)
    k = rng.integers(-2, 3, (N, C))
    k[o[0]] = 1
    k[o[1]] = 0
    k[o[2]] = -1 - rng.integers(0, 2, C)
    x = d["x"].reshape(N, 128, C, 4)
    x[:, :16] = 0
    x[:, 0, :, 0] = k.astype(np.float32).astype(BF)
    u = d["u"].reshape(N, 128, 128, 4)
    u[:, :, 0] = 0
    u[:, :, 1::16] = 0
    for r in range(N):
        u[r, 0, 0, 0] = 1.0 if o[r] % 2 == 0 else -1.0
        u[r, 0, 1::16, 0] = rng.permutation([1, 1, 1, -1, -1, -1, 0, 0]).astype(np.float32).astype(BF)
    return {"x": x.reshape(N, 128, 4 * C), "u": u.reshape(N, 128, 512), "v": d["v"], "p": stored(rotors(rng)), **weights(rng, kept(rng))}
def setup_inputs_near(rng):
    d = numbers_of(rng)
    s = rng.integers(0, 16, (N, C))
    size = np.where(np.arange(N) // 2 % 2 == rng.integers(2), 2.0 ** 9, 2.0 ** -7)[:, None]
    x = d["x"].astype(np.float32).reshape(N, 128, C, 4)
    x[:, :16] = 0
    x[:, 0, :, 0] = rng.integers(-1, 2, (N, C)) * size
    x[:, 8] = ((s[:, :, None] >> np.arange(4)) & 1) * np.exp2(np.arange(4) - 23.0) * size[:, :, None]
    x[:, 11, :, 0] = 2.0 ** -10 * size
    u = d["u"].reshape(N, 128, 128, 4)
    u[:, :, 0] = 0
    u[:, :, 1::16] = 0
    w = kept(rng)
    odd = int(rng.integers(2))
    for r in range(N):
        k = 1.0 if r % 2 == odd else 2.0 ** -30
        if r % 2 != odd: w[r, :, :, :16] *= 0.0625
        u[r, 0, 0, 0] = k
        u[r, 8, 0] = k
        u[r, 11, 0, 0] = k
        h = rng.permutation(8)
        for g in range(8):
            if h[g] < 4: u[r, 8, 16 * g + 1] = k
            else: u[r, 0, 16 * g + 1, 0] = -k
    return {"x": x.reshape(N, 128, 4 * C).astype(BF), "u": u.reshape(N, 128, 512), "v": d["v"], "p": stored(rotors(rng)), **weights(rng, w)}
def setup_inputs_huge(rng):
    d = numbers_of(rng)
    o = rng.permutation(N)
    e = rotors(rng)
    e[o < N // 2, 1:] = np.arange(C)
    x = 2.0 ** 25 * (0.75 + 0.25 * rng.random((N, 128, C, 4)))
    x[o == 0] = 2.0 ** 25
    u = d["u"].reshape(N, 128, 128, 4)
    for r in range(N):
        k = rng.permutation(C)
        t = 1.0 - 0.125 * (k // 2 % 2)
        t = t * (k % 2 * 2.0 - 1.0) if o[r] < N // 2 else t * (o[r] % 2 * 2.0 - 1.0)
        x[r] *= t[None, :, None]
        u[r, :, 0] = ((rng.integers(2) * 2.0 - 1.0) * 2.0 ** 30 * (1.0 - 0.1 * rng.random((128, 4)))).astype(np.float32).astype(BF)
        u[r, :, 1::16] = ((rng.permutation(8) % 2 * 2.0 - 1.0)[None, :, None] * 2.0 ** 30 * (1.0 - 0.1 * rng.random((128, 8, 4)))).astype(np.float32).astype(BF)
    return {"x": x.astype(np.float32).reshape(N, 128, 4 * C).astype(BF), "u": u.reshape(N, 128, 512), "v": d["v"], "p": stored(e), **weights(rng, np.ones((N, 128, 4, 128, 4)))}
def setup_inputs_ends(rng):
    d = numbers_of(rng)
    o = rng.permutation(N)
    e = rotors(rng)
    i = np.arange(C)
    x = np.full((N, 128, C, 4), 2.0 ** 25)
    w = np.ones((N, 128, 4, 128, 4))
    u = d["u"].reshape(N, 128, 128, 4)
    for r in range(N):
        k = o[r] % 4
        if k == 0:
            e[r, 1:] = i
            x[r, :, rng.integers(C)] *= -1.0
        elif k == 2: e[r] = (i + C - 1) % C
        else:
            if k == 1: e[r] = i[::-1]
            x[r, 32:] *= rng.integers(0, 2, (96, C, 4)) * 2.0 - 1.0
            x[r, 64:] *= 2.0 ** -55
        x[r] *= rng.integers(2) * 2.0 - 1.0
        a = 2.0 ** -30 if o[r] == 1 else 2.0 ** 30
        u[r, :, 0] = a * (rng.integers(2) * 2.0 - 1.0)
        t = rng.permutation([1, 1, 1, 1, -1, -1, -1, 0]) * a
        u[r, :, 1::16] = t.astype(np.float32).astype(BF)[None, :, None]
        if o[r] == 3: w[r, 64:] = (rng.integers(0, 2, (64, 4, 128, 4)) * 2.0 - 1.0) * 2.0 ** -30
    d["v"] = (np.where(d["v"] < 0, -1.0, 1.0) * np.where(rng.permutation(N) % 2, 2.0 ** -30, 2.0 ** 30)[:, None, None]).astype(np.float32).astype(BF)
    return {"x": x.astype(np.float32).reshape(N, 128, 4 * C).astype(BF), "u": u.reshape(N, 128, 512), "v": d["v"], "p": stored(e), **weights(rng, w)}
def setup_inputs_spread(rng):
    d = setup_inputs(rng)
    d["x"] = wide(rng, N, 128, 4 * C, cols=6)
    return d
def check_inputs(d):
    b = []
    for k, top in (("x", 2.0 ** 25), ("u", 2.0 ** 30), ("v", 2.0 ** 30)):
        a = np.abs(d[k].astype(np.float32))
        if not (np.isfinite(a).all() and ((a == 0) | (a >= 2.0 ** -30) & (a <= top)).all()): b.append("a value of " + k)
    none, least, most = [emit(mx_ref.quantize(np.full((128, 16), k, np.float32).astype(BF)))[1][0, 0] for k in (0.0, 2.0 ** -30, 1.0)]
    for r in range(N):
        if (np.sort(gentries(d["p"][r]), axis=1) != np.arange(C)).any(): b.append("p: a group without a permutation")
        if ((d["wc"][r] & 0x7F) == 0x7F).any(): b.append("wc: a code that is no number")
        s = mx_ref.live(d["ws"][r])
        if ((s != none) & ((s < least) | (s > most))).any(): b.append("ws: a scale out of range")
        elif (np.abs(decode(pk(d["wc"][r], d["ws"][r]))) > 1).any(): b.append("a number of W beyond 1")
    return b
def reference(x, u, v, p, wc, ws):
    qu = [mx_ref.quantize(u[r]) for r in range(N)]
    lay = [pk(wc[r], ws[r]) for r in range(N)]
    rho = np.stack([gentries(p[r]) for r in range(N)])
    now = [x[r] for r in range(N)]
    a = np.zeros((N, 8), np.int64)
    op = np.zeros((N, 8, C), np.float32)
    for h in TURN:
        e = np.zeros((N, 8, C), np.int64)
        j = np.zeros((N, 1), np.int64) + np.arange(C)
        for g in range(8):
            j = (np.take_along_axis(rho[:, g], (j + a[:, g:g + 1]) % C, axis=1) - a[:, g:g + 1]) % C
            e[:, g] = j
        back = np.argsort(e, axis=2)
        for r in range(N):
            b = r ^ h
            part = gcols(now[r], e[r])
            q = mx_ref.quantize(part)
            z = mx_ref.quantize(tile([mx_ref.matmul(pick(lay[b], np.arange(128 * k, 128 * k + 128)), q) * np.float32(0.0078125) for k in range(4)]))
            s = mx_ref.matmul(qu[b], z) + np.float32(0.0)
            o = np.argsort(-s[0], kind="stable")
            m = np.zeros(C, np.int64)
            m[o[::2]] = o[1::2]
            m[o[1::2]] = o[::2]
            mixed = ((part.astype(np.float32) + decode(z)) * np.float32(0.5)).astype(BF)
            come = m[back[r]]
            now[r] = gcols(mixed, come)
            a[r] = (a[r] + np.sum(s[1::16] > 0, axis=1)) % C
            op[r] = (np.take_along_axis(e[r], come, axis=1) + a[r][:, None]) % C
    y = np.zeros((N, 128, C), np.float32)
    oc, osc = np.zeros((N, 128, 4 * C), np.uint8), np.zeros((N, 16, C), np.uint8)
    for r in range(N):
        q = mx_ref.quantize(now[r])
        y[r] = mx_ref.matmul(mx_ref.quantize(v[r]), q)
        oc[r], osc[r] = emit(q)
    return {"y": y, "op": op, "oc": oc, "osc": osc}

@@ -1,0 +1,558 @@
+from concourse.bass import DstId, RemoteDMATransfer
+from concourse.mybir import dt, AluOpType, ActivationFunctionType
+
+A = AluOpType
+COPY = ActivationFunctionType.Copy
+SIGN = ActivationFunctionType.Sign
+C = 256
+TURN = [1, 2, 4]
+UP = 144
+X4 = "float8_e4m3fn_x4"
+OPT = {"offact": 0, "gm": 5, "cut": 42, "gaps": 0, "qc": 1, "slot": 3, "fin": 0}
+
+
+def _pair(name, n):
+    return {"q" + name: ("sbuf", [128, n], X4), "s" + name: ("sbuf", [128, n], "uint8")}
+
+
+def _of(dtype, n, *names):
+    return {k: ("sbuf", [128, n], dtype) for k in names}
+
+
+SCRATCH = {"ps": ("psum", [128, 4096], "float32")}
+for _d in (_of("bfloat16", 4 * C, "xb", "ft", "ht", "ct", "iot"), _of("bfloat16", 512, "ub", "vb"), _of("float32", 4 * C, "st"),
+           _of("bfloat16", 4 * 130, "gt"), _of("bfloat16", 2048, "et"), _of("bfloat16", 1536, "wt"),
+           _of("int32", 144, "lst"), _of("int32", 128, "li", "lj"), _of("uint16", 128, "off"),
+           _of("bfloat16", C, "rho", "ta", "tb", "ra", "rb", "m16", "m4", "sa", "sb", "sg2", "orow", "oswp", "mrow", "crow", "optab"),
+           _of("bfloat16", 2 * C, "come"),
+           _of("float32", C, "sf32", "oprow", "yb"), _of("bfloat16", 128, "tri"),
+           _of("uint16", 16, "rl", "moff"), _of("uint16", 48, "el"), _of("uint16", 64, "l4"), _of("uint16", 32, "ol"),
+           _of("uint16", 10, "uoff", "doff"), _of("int32", 16, "ei", "ej", "ident"), _of("int32", 32, "ip", "iq"),
+           _of("float32", 16, "col", "acol"), _of("float32", 32, "cc", "dm", "a1", "a2", "dcum", "acum", "zer"),
+           _of("bfloat16", 32, "msm"), _of("float32", 8, "scol")):
+    SCRATCH.update(_d)
+for _n, _k in (("w", 512), ("w0", 512), ("w1", 512), ("w2", 512), ("u", 128), ("up", UP), ("u0", UP), ("u1", UP), ("u2", UP),
+               ("v", 128), ("f", C), ("h", C), ("c", C), ("g", 130), ("e", 512), ("k", 384), ("x", C)):
+    SCRATCH.update(_pair(_n, _k))
+
+SEMAPHORES = ["cv", "ca", "ct", "cg", "lp", "lws", "lwc", "lu", "lx", "lv", "sent",
+              "aw0", "aw1", "aw2", "au0", "au1", "au2", "outs", "outa"]
+
+
+def rank_program(g, core, T, topo):
+    rank = T.rank_of(core)
+    if rank is None:
+        return
+    Q = {"v": g.vector, "a": g.scalar, "t": g.tensor, "g": g, "s": g.sync}
+    V, S, PE = g.vector, g.scalar, g.tensor
+    known = {q: {} for q in Q}
+    count = {}
+    wrote, read = {}, {}
+    serial = [0]
+
+    def need(q, evs):
+        for ev in sorted(evs, key=lambda e: -e[3]):
+            if known[q].get(ev[0], 0) < ev[1]:
+                Q[q].wait_ge(T.sem[ev[0]], ev[1])
+                for s, n in ev[2].items():
+                    known[q][s] = max(known[q].get(s, 0), n)
+
+    def op(q, make, r=(), w=(), sem=None, n=1, upto=None, inc=True):
+        evs = []
+        for k in r:
+            if k in wrote:
+                evs.append(wrote[k])
+            if k[0] == "P":
+                evs += [e for e in read.get(k, []) if e[4] != q]
+        for k in w:
+            if k in wrote:
+                evs.append(wrote[k])
+            evs += read.get(k, [])
+        need(q, evs)
+        ins = make()
+        sem = sem or "c" + q
+        count[sem] = count.get(sem, 0) + n
+        if inc:
+            ins.then_inc(T.sem[sem], n)
+        clock = dict(known[q])
+        clock[sem] = upto or count[sem]
+        serial[0] += 1
+        ev = (sem, clock[sem], clock, serial[0], q)
+        for k in r:
+            read.setdefault(k, []).append(ev)
+        for k in w:
+            wrote[k] = ev
+            read[k] = []
+
+    def arrives(key, sem, n):
+        count[sem] = n
+        wrote[key] = (sem, n, {sem: n}, 0, "x")
+
+    def bank(k, a=0, b=C):
+        return T.ps[:, 512 * k + a:512 * k + b]
+
+    def ts(out, in0, s1, s2, op0, op1, r, w):
+        if op1 is None:
+            op("v", lambda: V.tensor_scalar(out, in0, s1, None, op0), r, w)
+        else:
+            op("v", lambda: V.tensor_scalar(out, in0, s1, s2, op0, op1), r, w)
+
+    def cp(out, in_, r, w):
+        op("v", lambda: V.tensor_copy(out, in_), r, w)
+
+    def act(out, in_, r, w, scale=None):
+        if scale is None:
+            op("a", lambda: S.activation(out, in_, COPY), r, w)
+        else:
+            op("a", lambda: S.activation(out, in_, COPY, scale=scale), r, w)
+
+    def move(q, out, in_, r, w, scale=None):
+        if q == "a":
+            act(out, in_, r, w, scale)
+        elif scale is None:
+            cp(out, in_, r, w)
+        else:
+            ts(out, in_, scale, None, A.mult, None, r, w)
+
+    def fill(ap, c, w):
+        op("v", lambda: V.memset(ap, c), (), w)
+
+    def quant(name, tile, r):
+        op("v", lambda: V.quantize_mx(T["q" + name][:], T["s" + name][:], tile), r, ["q" + name])
+
+    def quant_half(name, tile, h, r):
+        a, b = 128 * h, 128 * h + 128
+        op("v", lambda: V.quantize_mx(T["q" + name][:, a:b], T["s" + name][:, a:b], tile[:, 4 * a:4 * b]), r, ["q%s%d" % (name, h)])
+
+    def mm(k, n, a, a0, b, b0, r):
+        op("t", lambda: PE.matmul_mx(bank(k, 0, n), T["q" + a][:, a0:a0 + 128], T["s" + a][:, a0:a0 + 128],
+                                     T["q" + b][:, b0:b0 + n], T["s" + b][:, b0:b0 + n], True, True), r, ["P%d" % k])
+
+    def scan(out, mask, row, r, w):
+        op("v", lambda: V.tensor_tensor_scan(out, mask, row, 0.0, A.add, A.min), r, w)
+
+    pcol, icol, qcol, tcol, c16, c4, tmp, tmq = [T.col[:, k:k + 1] for k in range(8)]
+
+    op("s", lambda: g.sync.dma_start(T.sw[:], T.ws[:]), (), ["sw"], "lws", 16)
+    op("s", lambda: g.sync.dma_start(T.qw[:].bitcast(dt.uint8), T.wc[:]), (), ["qw"], "lwc", 16)
+    for s in range(8):
+        op("a", lambda: S.dma_start(T.lst[16 * s:128, 16 * s:16 * s + 16], T.p[0:128 - 16 * s, :]), (), ["lp%d" % s], "lp", 16, 128)
+    op("s", lambda: g.sync.dma_start(T.ub[:], T.u[:]), (), ["ub"], "lu", 16)
+    op("s", lambda: g.sync.dma_start(T.xb[:], T.x[:]), (), ["xb"], "lx", 16)
+    op("s", lambda: g.sync.dma_start(T.vb[:], T.v[:]), (), ["vb"], "lv", 16)
+
+    op("g", lambda: g.iota(T.ip[:, 0:10], [[-16, 10]], 0, 1), (), ["ip0"])
+    op("g", lambda: g.iota(T.cc[:, 0:16], [[1, 16]], 0, 0, allow_small_or_imprecise_dtypes=True), (), ["cc0"])
+    op("g", lambda: g.iota(T.cc[:, 16:32], [[0, 4], [1, 4]], 0, 0, allow_small_or_imprecise_dtypes=True), (), ["cc1"])
+    op("g", lambda: g.iota(T.iot[:, 0:C], [[1, C]], 0, 0, allow_small_or_imprecise_dtypes=True), (), ["iot"])
+
+    fill(T.gt[:], 0.0, ["g0", "g1"])
+    fill(T.dcum[:], 0.0, ["dcum"])
+    fill(T.zer[:], 0.0, ["zer"])
+    ts(T.iq[:, 0:1], T.ip[:, 0:1], 15, None, A.bitwise_and, None, ["ip0"], ["iq0"])
+    ts(T.iq[:, 1:2], T.ip[:, 0:1], 2, 3, A.arith_shift_right, A.bitwise_and, ["ip0"], ["iq1"])
+    ts(T.iq[:, 2:3], T.ip[:, 0:1], 3, None, A.bitwise_and, None, ["ip0"], ["iq2"])
+    cp(pcol, T.ip[:, 0:1], ["ip0"], ["pcol"])
+    cp(T.col[:, 1:4], T.iq[:, 0:3], ["iq0", "iq1", "iq2"], ["icol"])
+    ts(T.dm[:, 0:16], T.cc[:, 0:16], icol, None, A.subtract, None, ["cc0", "icol"], ["dm0"])
+    ts(T.dm[:, 16:32], T.cc[:, 16:32], qcol, None, A.subtract, None, ["cc1", "icol"], ["dm1"])
+    ts(T.moff[:], T.cc[:, 0:16], 0.0, icol, A.mult, A.add, ["cc0", "icol"], ["moff"])
+    ts(T.ident[:], T.cc[:, 0:16], 16.0, icol, A.mult, A.add, ["cc0", "icol"], ["ident"])
+    ts(T.a1[:], T.dm[:], 0.0, 1024.0, A.is_equal, A.mult, ["dm0", "dm1"], ["a1"])
+    ts(T.a2[:], T.dm[:], 1.0, -256.0, A.is_equal, A.mult, ["dm0", "dm1"], ["a2"])
+    cp(T.lst[0:16, 16:32], T.ident[0:16, :], ["ident"], ["li1"])
+    op("v", lambda: V.tensor_tensor(T.msm[:], T.a1[:], T.a2[:], A.add), ["a1", "a2"], ["msm"])
+    act(T.m16[:], T.msm[:, 0:16].indirect(T.moff[:]), ["msm", "moff"], ["m16"])
+    for s in range(2, 9):
+        cp(T.lst[0:16 * s, 16 * s:16 * s + 16], T.ident[0:16 * s, :], ["ident"], ["li%d" % s])
+    base = ["lp%d" % s for s in range(8)] + ["li%d" % s for s in range(1, 9)]
+    cp(T.off[:], T.lst[:, 0:128], base, ["off"])
+
+    peers = [T.cores[rank ^ h] for h in TURN]
+    every = topo.engines(core, peers[0])
+    far = topo.engines(core, peers[1])
+    near = [e for e in every if e not in far]
+    ways = [near, far[:len(far) // 2], far[len(far) // 2:]]
+    aw, au = ["aw0", "aw1", "aw2"], ["au0", "au1", "au2"]
+
+    def bits(es):
+        return sum(1 << e for e in es)
+
+    def dst(c):
+        a = topo.addr(c)
+        return DstId(rid=a[0], pnc=a[1])
+
+    def send(src, lands, which, sems, r):
+        tr = [RemoteDMATransfer(dst_ids=[dst(peers[i])], dma_engine_mask=bits(ways[i]), remote_sem=T.sem[sems[i]],
+                                src=src, dst=lands[i]) for i in which]
+        op("g", lambda: g.remote_dma_fused(tr, local_sem=T.sem.sent), r, (), "sent", sum(len(ways[i]) for i in which), inc=False)
+
+    def write(out, src, i, es, r, sems):
+        a = topo.addr(peers[i])
+        op("g", lambda: g.remote_dma(out, src, T.sem[sems[i]], T.sem.sent, a[1], a[0], bits(es)), r, (), "sent", len(es), inc=False)
+
+    write(T.sw0[:], T.sw[:], 0, every, ["sw"], aw)
+    write(T.qw0[:].bitcast(dt.uint8), T.qw[:].bitcast(dt.uint8), 0, every, ["qw"], aw)
+    arrives("W0", "aw0", 2 * len(every))
+    arrives("W1", "aw1", len(ways[1]) + len(far))
+    arrives("W2", "aw2", len(ways[2]) + len(far))
+    for i in range(3):
+        arrives("U%d" % i, au[i], 2 * len(ways[i] if i else every))
+
+    def lists(s):
+        return T.off[:, 16 * s:16 * s + 16]
+
+    act(T.rho[:], T.iot[:, 0:C].indirect(lists(0)), ["iot", "off"], ["rho"])
+    cp(T.ra[:], T.iot[:, 0:C].indirect(lists(5)), ["iot", "off"], ["ra"])
+    ts(c16, icol, 15.0, 256.0, A.is_lt, A.mult, ["icol"], ["c16"])
+    act(T.ta[:], T.rho[:].indirect(lists(1)), ["rho", "off"], ["ta"])
+    cp(T.rb[:], T.ra[:].indirect(lists(6)), ["ra", "off"], ["rb"])
+    ts(tmp, icol, 7.0, 16.0, A.min, A.mult, ["icol"], ["tmp"])
+    act(T.tb[:], T.ta[:].indirect(lists(2)), ["ta", "off"], ["tb"])
+    cp(T.ra[:], T.rb[:].indirect(lists(7)), ["rb", "off"], ["ra"])
+    fill(T.uoff[:, 1:10], 0, ["uoff1"])
+    ts(T.uoff[:, 0:1], tmp, 1.0, None, A.add, None, ["tmp"], ["uoff0"])
+    scan(T.sa[:], T.m16[:], T.ra[:], ["m16", "ra"], ["sa"])
+    quant("u", T.ub[:], ["ub"])
+    ts(T.rl[:], T.sa[:, 15:C:16], c16, None, A.add, None, ["sa", "c16"], ["rl"])
+    act(T.ta[:], T.tb[:].indirect(lists(3)), ["tb", "off"], ["ta"])
+    act(T.tb[:], T.ta[:].indirect(lists(4)), ["ta", "off"], ["tb"])
+    cp(T.qup[:].bitcast(dt.uint32), T.qu[:].bitcast(dt.uint32).indirect(T.uoff[:, 0:9]), ["qu", "uoff0", "uoff1"], ["qup"])
+    cp(T.sup[:], T.su[:].indirect(T.uoff[:, 0:9]), ["qu", "uoff0", "uoff1"], ["sup"])
+    write(T.qu0[:].bitcast(dt.uint8), T.qup[:].bitcast(dt.uint8), 0, every, ["qup"], au)
+    write(T.su0[:], T.sup[:], 0, every, ["sup"], au)
+    write(T.qw1[:].bitcast(dt.uint8), T.qw[:].bitcast(dt.uint8), 1, far, ["qw"], aw)
+    send(T.sw[:], [T["sw%d" % i][:] for i in range(3)], (1, 2), aw, ["sw"])
+    send(T.qup[:].bitcast(dt.uint8), [T["qu%d" % i][:].bitcast(dt.uint8) for i in range(3)], (1, 2), au, ["qup"])
+    send(T.sup[:], [T["su%d" % i][:] for i in range(3)], (1, 2), au, ["sup"])
+    write(T.qw2[:].bitcast(dt.uint8), T.qw[:].bitcast(dt.uint8), 2, far, ["qw"], aw)
+    op("g", lambda: g.iota(T.iot[:, C:4 * C], [[0, 3], [1, C]], 0, 0, allow_small_or_imprecise_dtypes=True), (), ["iot2"])
+    act(T.m4[:], T.msm[:, 16:32].indirect(T.moff[:]), ["msm", "moff"], ["m4"])
+    act(T.crow[:], T.tb[:].indirect(T.rl[:]), ["tb", "rl"], ["cr0", "cr1"])
+    ts(tmq, qcol, 3.0, 1024.0, A.is_lt, A.mult, ["icol"], ["tmq"])
+    fill(T.et[:, 0:1024], 0.0, ["e0", "e1"])
+    ts(c4, tmq, tcol, None, A.add, None, ["tmq", "icol"], ["c4"])
+
+    def constants():
+        fill(T.et[:, 1024:2048], 0.0, ["e2", "e3"])
+        for t, c in enumerate((1.0, 0.5, -0.5, 1.0)):
+            fill(T.wt[:, t:512:4], c, ["k%d" % t])
+        fill(T.wt[:, 512:1024], -1.0, ["k4"])
+        for t, c in enumerate((0.5, 0.5, -0.5, 1.0)):
+            fill(T.wt[:, 1024 + t:1536:4], c, ["k%d" % (5 + t)])
+        scan(T.sa[:], T.m16[:], T.crow[:], ["m16", "cr0", "cr1"], ["sa"])
+        for b in range(4):
+            ts(T.et[:, 512 * b + b:512 * b + 512:4], T.iot[:, 0:128], pcol, None, A.is_equal, None, ["iot", "pcol"], ["e%d" % b])
+        ts(T.el[:, 0:16], T.sa[:, 15:C:16], c16, None, A.add, None, ["sa", "c16"], ["el0"])
+        quant("k", T.wt[:], ["k%d" % t for t in range(9)])
+        ts(T.tri[:], T.iot[:, 0:128], pcol, None, A.is_gt, None, ["iot", "pcol"], ["tri"])
+        ts(T.iq[:, 8:18], T.ip[:, 0:10], 4, None, A.arith_shift_right, None, ["ip0"], ["iq8"])
+        quant("e", T.et[:], ["e0", "e1", "e2", "e3"])
+        ts(T.iq[:, 20:27], T.iq[:, 9:16], 1.0, 2.0, A.add, A.mult, ["iq8"], ["iq20"])
+        ts(T.doff[:, 8:9], T.iq[:, 8:9], 2.0, None, A.mult, None, ["iq8"], ["aoff"])
+        fill(T.doff[:, 7:8], 0, ["doff7"])
+        ts(T.doff[:, 0:7], T.iq[:, 20:27], 1.0, None, A.max, None, ["iq20"], ["doff0"])
+        quant("v", T.vb[:], ["vb"])
+
+    fkeys = ["f0", "f1", "f2", "f3"]
+    nothing = lambda: None
+
+    def gather(first, row, keys, name, gap=(nothing, nothing)):
+        def scan4(h):
+            scan(T.sb[:, 128 * h:128 * h + 128], T.m4[:, 0:128], row[:, 128 * h:128 * h + 128], ["m4", keys[h]], ["sb%d" % h])
+
+        def list4(h):
+            ts(T.l4[:, 32 * h:32 * h + 32], T.sb[:, 128 * h + 3:128 * h + 128:4], 4.0, c4, A.mult, A.add, ["sb%d" % h, "c4"], ["l4%d" % h])
+
+        def part(q, a, b, key):
+            win, r = (T.xb, ["xb"]) if first else (T.st, ["s0", "s1", "s2", "s3"])
+            move(q, T.ft[:, 16 * a:16 * b], win[:].indirect(T.l4[:, a:b]), r + ["l4%d" % (a // 32)], [key], None if first else 0.5)
+        cut = OPT["cut"]
+        scan4(0)
+        scan4(1)
+        list4(0)
+        list4(1)
+        part("a", 16, 32, "f1")
+        part("v", 0, 16, "f0")
+        part("a", cut, 64, "f3")
+        gap[0]()
+        quant_half(name, T.ft, 0, ["f0", "f1"])
+        part("v", 32, cut, "f2")
+        gap[1]()
+        quant_half(name, T.ft, 1, ["f2", "f3"])
+
+    def cast(q, h, k):
+        move(q, T.ht[:, 512 * h + k:512 * h + 512:4], bank(4 * h + k, 0, 128), ["P%d" % (4 * h + k)], ["h%d%d" % (h, k)], 0.0078125)
+
+    def score(h):
+        cp(T.scol[:, 4 * h:4 * h + 1], bank(h, 16, 17), ["P%d" % h], ["sc%d" % h])
+
+    def flag(h):
+        ts(T.gt[:, 8 + 3 * h:72 + 3 * h:8], bank(h, 0, 8), 0.0, None, A.is_gt, None, ["P%d" % h], ["g%d" % h])
+
+    def sc(h):
+        return T.scol[:, 4 * h:4 * h + 1]
+
+    def equal(h):
+        ts(T.ct[:, 512 * h + 2:512 * h + 512:4], bank(2 + h, 0, 128), sc(h), None, A.is_equal, None, ["P%d" % (2 + h), "sc%d" % h], ["c2%d" % h])
+
+    def other(h):
+        ts(T.ct[:, 512 * h:512 * h + 512:4], bank(2 + h, 0, 128), sc(1 - h), None, A.is_le if h else A.is_lt, None,
+           ["P%d" % (2 + h), "sc%d" % (1 - h)], ["c0%d" % h])
+
+    def sign(h, k):
+        op("a", lambda: S.activation(T.ct[:, 512 * h + 1:512 * h + 512:4], bank(k, 0, 128), SIGN, bias=sc(h), scale=-1.0),
+           ["P%d" % k, "sc%d" % h], ["c1%d" % h])
+
+    def other_sign(h, k):
+        op("a", lambda: S.activation(T.sg2[:, 128 * h:128 * h + 128], bank(k, 0, 128), SIGN, bias=sc(1 - h), scale=-1.0),
+           ["P%d" % k, "sc%d" % (1 - h)], ["sg%d" % h])
+
+    def other_side(h):
+        op("a", lambda: S.activation(T.ct[:, 512 * h:512 * h + 512:4], T.sg2[:, 128 * h:128 * h + 128], SIGN, bias=0.5 if h else -0.5),
+           ["sg%d" % h], ["c0%d" % h])
+
+    def ties(h):
+        op("v", lambda: V.tensor_tensor_scan(T.ct[:, 512 * h + 3:512 * h + 512:4], T.tri[:], T.ct[:, 512 * h + 2:512 * h + 512:4],
+                                             0.0, A.max, A.mult), ["tri", "c2%d" % h], ["c3%d" % h])
+
+    ckeys = ["c%d%d" % (t, h) for t in range(4) for h in range(2)]
+
+    def layer(i):
+        u, uk = "u%d" % i, "U%d" % i
+        if i == 0:
+            constants()
+        for h in range(2):
+            for k in range(4):
+                mm(4 * h + k, 128, "w%d" % i, 128 * k, "f", 128 * h, ["W%d" % i, "qf%d" % h])
+        for k, q in enumerate("aaav"):
+            cast(q, 0, k)
+        cast("v", 1, 0)
+        quant_half("h", T.ht, 0, ["h00", "h01", "h02", "h03"])
+        mm(0, 128, "h", 0, u, 0, ["qh0", uk])
+        mm(2, 128, u, 16, "h", 0, ["qh0", uk])
+        cast("a", 1, 1)
+        cast("v", 1, 2)
+        cast("a", 1, 3)
+        quant_half("h", T.ht, 1, ["h10", "h11", "h12", "h13"])
+        mm(1, 128, "h", 128, u, 0, ["qh1", uk])
+        mm(3, 128, u, 16, "h", 128, ["qh1", uk])
+        mm(7, 128, u, 16, "h", 128, ["qh1", uk])
+        score(0)
+        flag(0)
+        equal(0)
+        sign(0, 2)
+
+    def counts(k):
+        def both():
+            PE.matmul_mx(bank(k, 0, 128), T.qk[:, 0:128], T.sk[:, 0:128], T.qg[:, 2:130], T.sg[:, 2:130], True, False)
+            return PE.matmul_mx(bank(k, 0, 128), T.qk[:, 128:256], T.sk[:, 128:256], T.qg[:, 0:128], T.sg[:, 0:128], False, True)
+        op("t", both, ["qk", "qg"], ["P%d" % k])
+
+    def steps_add(k):
+        op("v", lambda: V.tensor_tensor(T.dcum[:], bank(k, 0, 32), T.dcum[:], A.add), ["P%d" % k, "dcum"], ["dcum"])
+
+    def steps_sum():
+        op("v", lambda: V.tensor_tensor_scan(T.acum[:], T.dcum[:], T.zer[:], 0.0, A.add, A.add), ["dcum", "zer"], ["acum"])
+
+    def rank_list(plus, gap):
+        scan(T.sf32[:], T.m16[:], bank(1), ["m16", "P1"], ["sf32"])
+        gap()
+        ts(T.rl[:], T.sf32[:, 15:C:16], c16, plus, A.add, A.add, ["sf32", "c16"], ["rl"])
+        cp(T.orow[:].indirect(T.rl[:]), T.iot[:, 0:C], ["iot", "rl"], ["orow"])
+
+    def unpack(b):
+        mm(4 + b, C, "e", 128 * b, "h", 0, ["qe", "qh0", "qh1"])
+
+    def add(b):
+        op("v", lambda: V.tensor_tensor(T.st[:, b:4 * C:4], bank(4 + b), T.ft[:, b:4 * C:4], A.add), ["P%d" % (4 + b)] + fkeys, ["s%d" % b])
+
+    def swap(q, h):
+        move(q, T.oswp[:, h:C:2], T.orow[:, 1 - h:C:2], ["orow"], ["osw%d" % h])
+
+    def partners(q):
+        move(q, T.mrow[:], T.oswp[:].indirect(T.rl[:]), ["osw0", "osw1", "rl"], ["mrow"])
+
+    def turn(i):
+        offact = OPT["offact"]
+        flag(1)
+        score(1)
+        quant("g", T.gt[:], ["g0", "g1"])
+        counts(0)
+        equal(1)
+        ties(0)
+        if offact:
+            other_sign(0, 2)
+            other_sign(1, 7)
+            sign(1, 7)
+            other_side(0)
+            other_side(1)
+        else:
+            sign(1, 7)
+            other(0)
+            other(1)
+        for b in range(4):
+            unpack(b)
+        ties(1)
+        steps_add(0)
+        cuts = ((0, 2), (2, 8))
+
+        def turned(x):
+            a, b = cuts[x]
+            op("v", lambda: V.tensor_tensor(T.li[:, 16 * a:16 * b], T.dcum[:].indirect(T.doff[:, a:b]), T.lst[:, 16 * a + 16:16 * b + 16], A.add),
+               ["dcum", "doff0", "doff7"] + base, ["li_%d" % x])
+
+        def wrapped(x):
+            a, b = cuts[x]
+            ts(T.lj[:, 16 * a:16 * b], T.li[:, 16 * a:16 * b], 255, None, A.bitwise_and, None, ["li_%d" % x], ["lj%d" % x])
+
+        def offsets(x):
+            a, b = cuts[x]
+            cp(T.off[:, 16 * a:16 * b], T.lj[:, 16 * a:16 * b], ["lj%d" % x], ["off" if x else "off0"])
+
+        def ranks():
+            mm(1, C, "k", 256 if offact else 0, "c", 0, ["qk", "qc0", "qc1"])
+
+        def codes(h):
+            quant_half("c", T.ct, h, ["c%d%d" % (t, h) for t in range(4)])
+        if OPT["qc"] == 0:
+            codes(0)
+        turned(0)
+        if OPT["qc"] == 1:
+            codes(0)
+        else:
+            steps_sum()
+        wrapped(0)
+        if OPT["qc"] < 2:
+            codes(1)
+            ranks()
+        offsets(0)
+        if OPT["qc"] == 2:
+            codes(0)
+            codes(1)
+            ranks()
+        turned(1)
+        if OPT["qc"] == 1:
+            steps_sum()
+        wrapped(1)
+        cp(T.ei[:], T.acum[:].indirect(T.doff[:, 8:9]), ["acum", "aoff"], ["ei"])
+        offsets(1)
+        if OPT["qc"] == 3:
+            codes(0)
+            codes(1)
+            ranks()
+
+        def step(s, a=0, b=16, key=None):
+            src, to = ("rho" if s == 0 else "tb" if s % 2 == 0 else "ta"), ("ta" if s % 2 == 0 else "tb")
+            act(T[to][:, 16 * a:16 * b], T[src][:].indirect(T.off[:, 16 * s + a:16 * s + b]),
+                ([src] if src != "tb" else ["tb", "tb1"]) + ["off0" if s < 2 else "off"], key or ([to] if to != "tb" else ["tb", "tb1"]))
+        gm = OPT["gm"]
+        for s in range(min(gm, 7)):
+            step(s)
+        if OPT["qc"] >= 2:
+            add(0)
+        rank_list(128.0 if offact else 64.0, lambda: ts(T.ej[:, 0:1], T.ei[:, 0:1], 255, None, A.bitwise_and, None, ["ei"], ["ej"]))
+        ts(T.acol[:, 0:1], T.ej[:, 0:1], -1.0, c16, A.mult, A.add, ["ej", "c16"], ["acol"])
+        swap("v", 0)
+        swap("v", 1)
+        rest = [1, 2, 3] if OPT["qc"] >= 2 else [0, 1, 2, 3]
+        if gm < 8:
+            partners("a")
+            for s in range(gm, 7):
+                step(s)
+            for _ in range(OPT["slot"]):
+                add(rest.pop())
+        else:
+            partners("v")
+        step(7, 0, 8, ["tb"])
+        step(7, 8, 16, ["tb1"])
+        cp(T.come[:, 0:C].indirect(T.el[:, 16 * i:16 * i + 16]), T.mrow[:], ["mrow", "el%d" % i], ["come"])
+        act(T.come[:, C:2 * C], T.come[:, 0:C], ["come"], ["come2"])
+        while len(rest) > OPT["gaps"]:
+            add(rest.pop())
+        for h in range(2):
+            scan(T.sa[:, 128 * h:128 * h + 128], T.m16[:, 0:128], T.tb[:, 128 * h:128 * h + 128], ["m16", "tb1" if h else "tb"], ["sa%d" % h])
+        for h in range(2):
+            ts(T.ol[:, 8 * h:8 * h + 8], T.sa[:, 128 * h + 15:128 * h + 128:16], T.acol[:, 0:1], 256.0, A.add, A.add, ["sa%d" % h, "acol"], ["ol%d" % h])
+        if rest:
+            act(T.crow[:, 0:128], T.come[:].indirect(T.ol[:, 0:8]), ["come", "come2", "ol0"], ["cr0"])
+            add(rest.pop())
+        else:
+            cp(T.crow[:, 0:128], T.come[:].indirect(T.ol[:, 0:8]), ["come", "come2", "ol0"], ["cr0"])
+        act(T.crow[:, 128:C], T.come[:].indirect(T.ol[:, 8:16]), ["come", "come2", "ol1"], ["cr1"])
+
+    def path_list(i):
+        def first():
+            cp(T.ei[:], T.ol[:, 0:16], ["ol0", "ol1"], ["ei"])
+
+        def second():
+            ts(T.ej[:], T.ei[:], 255, None, A.bitwise_and, None, ["ei"], ["ej"])
+
+        def third():
+            cp(T.el[:, 16 * i:16 * i + 16], T.ej[:], ["ej"], ["el%d" % i])
+        return first, second, third
+
+    def last(i):
+        score(1)
+        sign(1, 7)
+        equal(1)
+        other(1)
+        other(0)
+        for b in range(4):
+            unpack(b)
+        ties(0)
+        ties(1)
+        flag(1)
+        quant("c", T.ct[:], ckeys)
+        mm(1, C, "k", 0, "c", 0, ["qk", "qc"])
+        quant("g", T.gt[:], ["g0", "g1"])
+        counts(0)
+        add(0)
+        rank_list(64.0, (lambda: add(3)) if OPT["fin"] else (lambda: steps_add(0)))
+        if OPT["fin"]:
+            steps_add(0)
+        swap("v", 0)
+        swap("a", 1)
+        partners("a")
+        steps_sum()
+        add(1)
+        cp(T.acol[:], T.acum[:].indirect(T.doff[:, 8:9]), ["acum", "aoff"], ["acol"])
+        add(2)
+        ts(T.ol[:, 0:16], T.ej[:], T.acol[:, 0:1], None, A.add, None, ["ej", "acol"], ["ol0", "ol1"])
+        act(T.optab[:], T.iot[:].indirect(T.ol[:, 0:16]), ["iot", "iot2", "ol0", "ol1"], ["optab"])
+        cp(T.come[:, 0:C].indirect(T.el[:, 16 * i:16 * i + 16]), T.mrow[:], ["mrow", "el%d" % i], ["come"])
+        if not OPT["fin"]:
+            add(3)
+        gather(False, T.come, ["come", "come"], "x",
+               (lambda: scan(T.sa[:], T.m16[:], T.come[:, 0:C], ["m16", "come"], ["sa0", "sa1"]),
+                lambda: ts(T.ol[:, 16:32], T.sa[:, 15:C:16], c16, None, A.add, None, ["sa0", "sa1", "c16"], ["ol2"])))
+        mm(2, 128, "v", 0, "x", 0, ["qv", "qx0"])
+        mm(3, 128, "v", 0, "x", 128, ["qv", "qx1"])
+        act(T.yb[:, 0:128], bank(2, 0, 128), ["P2"], ["y0"])
+        cp(T.yb[:, 128:C], bank(3, 0, 128), ["P3"], ["y1"])
+        act(T.oprow[:], T.optab[:].indirect(T.ol[:, 16:32]), ["optab", "ol2"], ["oprow"])
+
+        def scales(q, k):
+            op(q, lambda: Q[q].dma_start(T.osc[4 * k:4 * k + 4, :], T.sx[32 * k:32 * k + 4, :]), ["qx0", "qx1"], (), "out" + q, 16)
+        op("s", lambda: g.sync.dma_start(T.y[:, 0:128], T.yb[:, 0:128]), ["y0"], (), "outs", 16)
+        op("s", lambda: g.sync.dma_start(T.oc[:], T.qx[:].bitcast(dt.uint8)), ["qx0", "qx1"], (), "outs", 16)
+        scales("s", 0)
+        scales("s", 1)
+        op("s", lambda: g.sync.dma_start(T.y[:, 128:C], T.yb[:, 128:C]), ["y1"], (), "outs", 16)
+        op("a", lambda: S.dma_start(T.op[:], T.oprow[0:128:16, :]), ["oprow"], (), "outa", 16)
+        scales("a", 2)
+        scales("a", 3)
+
+    for i in range(3):
+        gap = path_list(i) if i else (nothing, nothing, nothing)
+        gather(i == 0, T.crow, ["cr0", "cr1"], "f", gap)
+        gap[2]()
+        layer(i)
+        if i < 2:
+            turn(i)
+        else:
+            last(i)
+
+    for s in SEMAPHORES:
+        if known["g"].get(s, 0) < count.get(s, 0):
+            g.wait_ge(T.sem[s], count[s])

@@ -8,7 +8,10 @@ C = 256
 TURN = [1, 2, 4]
 UP = 144
 X4 = "float8_e4m3fn_x4"
-OPT = {"offact": 0, "gm": 5, "cut": 42, "gaps": 0, "qc": 1, "slot": 3, "fin": 0}
+OPT = {"offact": 0, "gm": "a", "cut": 42, "qc": 1, "fin": 0, "dbl": "a", "e": "aa", "b": "aa", "swap": "a", "back": 1, "lastback": 1,
+       "order": None}
+OPT["order"] = [
+    0,2,13,52,1,3,95,4,10,14,5,11,113,6,12,15,7,21,8,22,9,20,16,96,24,110,23,28,26,25,38,40,37,39,36,31,35,34,30,29,27,49,32,46,53,71,33,108,41,42,72,112,44,45,88,48,47,87,51,50,55,54,57,43,85,56,60,69,59,58,17,61,111,86,114,70,62,93,100,18,92,102,91,63,74,73,94,76,64,75,19,79,81,65,78,77,66,82,103,67,109,80,121,123,97,68,120,84,122,83,117,134,118,107,132,119,133,116,125,128,126,127,124,135,98,129,138,101,136,99,130,154,144,143,137,140,131,139,149,153,106,145,152,141,147,146,198,142,197,156,157,150,164,158,172,166,160,169,173,163,165,174,168,175,89,167,170,151,176,90,188,171,148,177,191,161,159,178,207,162,179,180,187,181,196,183,189,104,184,182,190,186,185,205,208,200,203,206,193,192,204,105,210,217,209,195,155,218,194,214,199,215,201,211,216,115,212,202,221,213,223,219,220,226,222,228,224,225,229,227,237,321,236,230,233,248,232,231,238,234,235,240,241,239,247,242,246,322,243,249,244,250,251,253,245,254,268,257,258,252,266,259,255,263,313,260,261,256,314,269,262,267,271,264,272,278,274,280,277,270,265,289,282,286,275,279,290,273,283,315,276,291,287,284,281,288,285,292,301,302,293,303,309,294,304,295,297,296,305,306,298,312,307,316,299,311,310,300,317,308,319,318,320,323,331,324,325,332,328,326,333,329,327,330,334,335,336,337,338,339,342,340,341,346,344,343,345,405,347,349,352,351,354,350,348,360,353,355,362,361,357,356,358,359,363,367,368,364,365,369,377,371,376,370,380,382,366,373,378,375,374,372,381,383,379,384,401,402,385,412,413,409,390,410,406,392,386,393,387,391,407,394,395,397,399,396,400,398,403,389,408,411,388,404,414,415,416,417,421,418,419,420,423,422,424,426,425,428,427,430,431,432,429,433,434,436,435,437,438]
 
 
 def _pair(name, n):
@@ -24,7 +27,8 @@ for _d in (_of("bfloat16", 4 * C, "xb", "ft", "ht", "ct", "iot"), _of("bfloat16"
            _of("bfloat16", 4 * 130, "gt"), _of("bfloat16", 2048, "et"), _of("bfloat16", 1536, "wt"),
            _of("int32", 144, "lst"), _of("int32", 128, "li", "lj"), _of("uint16", 128, "off"),
            _of("bfloat16", C, "rho", "ta", "tb", "ra", "rb", "m16", "m4", "sa", "sb", "sg2", "orow", "oswp", "mrow", "crow", "optab"),
-           _of("bfloat16", 2 * C, "come"),
+           _of("bfloat16", 2 * C, "come", "tl"), _of("bfloat16", C, "r5", "sr", "erow", "brow", "sc2"),
+           _of("uint16", 16, "ml", "bl"), _of("int32", 16, "di", "dj"),
            _of("float32", C, "sf32", "oprow", "yb"), _of("bfloat16", 128, "tri"),
            _of("uint16", 16, "rl", "moff"), _of("uint16", 48, "el"), _of("uint16", 64, "l4"), _of("uint16", 32, "ol"),
            _of("uint16", 10, "uoff", "doff"), _of("int32", 16, "ei", "ej", "ident"), _of("int32", 32, "ip", "iq"),
@@ -57,7 +61,12 @@ def rank_program(g, core, T, topo):
                 for s, n in ev[2].items():
                     known[q][s] = max(known[q].get(s, 0), n)
 
+    calls = []
+
     def op(q, make, r=(), w=(), sem=None, n=1, upto=None, inc=True):
+        calls.append((q, make, r, w, sem, n, upto, inc))
+
+    def emit(q, make, r, w, sem, n, upto, inc):
         evs = []
         for k in r:
             if k in wrote:
@@ -136,7 +145,7 @@ def rank_program(g, core, T, topo):
     op("s", lambda: g.sync.dma_start(T.sw[:], T.ws[:]), (), ["sw"], "lws", 16)
     op("s", lambda: g.sync.dma_start(T.qw[:].bitcast(dt.uint8), T.wc[:]), (), ["qw"], "lwc", 16)
     for s in range(8):
-        op("a", lambda: S.dma_start(T.lst[16 * s:128, 16 * s:16 * s + 16], T.p[0:128 - 16 * s, :]), (), ["lp%d" % s], "lp", 16, 128)
+        op("a", lambda s=s: S.dma_start(T.lst[16 * s:128, 16 * s:16 * s + 16], T.p[0:128 - 16 * s, :]), (), ["lp%d" % s], "lp", 16, 128)
     op("s", lambda: g.sync.dma_start(T.ub[:], T.u[:]), (), ["ub"], "lu", 16)
     op("s", lambda: g.sync.dma_start(T.xb[:], T.x[:]), (), ["xb"], "lx", 16)
     op("s", lambda: g.sync.dma_start(T.vb[:], T.v[:]), (), ["vb"], "lv", 16)
@@ -203,18 +212,18 @@ def rank_program(g, core, T, topo):
         return T.off[:, 16 * s:16 * s + 16]
 
     act(T.rho[:], T.iot[:, 0:C].indirect(lists(0)), ["iot", "off"], ["rho"])
-    cp(T.ra[:], T.iot[:, 0:C].indirect(lists(5)), ["iot", "off"], ["ra"])
+    cp(T.r5[:], T.iot[:, 0:C].indirect(lists(5)), ["iot", "off"], ["r5"])
     ts(c16, icol, 15.0, 256.0, A.is_lt, A.mult, ["icol"], ["c16"])
     act(T.ta[:], T.rho[:].indirect(lists(1)), ["rho", "off"], ["ta"])
-    cp(T.rb[:], T.ra[:].indirect(lists(6)), ["ra", "off"], ["rb"])
+    cp(T.rb[:], T.r5[:].indirect(lists(6)), ["r5", "off"], ["rb"])
     ts(tmp, icol, 7.0, 16.0, A.min, A.mult, ["icol"], ["tmp"])
     act(T.tb[:], T.ta[:].indirect(lists(2)), ["ta", "off"], ["tb"])
     cp(T.ra[:], T.rb[:].indirect(lists(7)), ["rb", "off"], ["ra"])
     fill(T.uoff[:, 1:10], 0, ["uoff1"])
     ts(T.uoff[:, 0:1], tmp, 1.0, None, A.add, None, ["tmp"], ["uoff0"])
-    scan(T.sa[:], T.m16[:], T.ra[:], ["m16", "ra"], ["sa"])
+    scan(T.sa[:], T.m16[:], T.ra[:], ["m16", "ra"], ["sa0", "sa1"])
     quant("u", T.ub[:], ["ub"])
-    ts(T.rl[:], T.sa[:, 15:C:16], c16, None, A.add, None, ["sa", "c16"], ["rl"])
+    ts(T.rl[:], T.sa[:, 15:C:16], c16, None, A.add, None, ["sa0", "sa1", "c16"], ["rl"])
     act(T.ta[:], T.tb[:].indirect(lists(3)), ["tb", "off"], ["ta"])
     act(T.tb[:], T.ta[:].indirect(lists(4)), ["ta", "off"], ["tb"])
     cp(T.qup[:].bitcast(dt.uint32), T.qu[:].bitcast(dt.uint32).indirect(T.uoff[:, 0:9]), ["qu", "uoff0", "uoff1"], ["qup"])
@@ -230,24 +239,25 @@ def rank_program(g, core, T, topo):
     act(T.m4[:], T.msm[:, 16:32].indirect(T.moff[:]), ["msm", "moff"], ["m4"])
     act(T.crow[:], T.tb[:].indirect(T.rl[:]), ["tb", "rl"], ["cr0", "cr1"])
     ts(tmq, qcol, 3.0, 1024.0, A.is_lt, A.mult, ["icol"], ["tmq"])
-    fill(T.et[:, 0:1024], 0.0, ["e0", "e1"])
     ts(c4, tmq, tcol, None, A.add, None, ["tmq", "icol"], ["c4"])
 
     def constants():
-        fill(T.et[:, 1024:2048], 0.0, ["e2", "e3"])
+        for b in range(8):
+            fill(T.et[:, 256 * b:256 * b + 256], 0.0, ["z%d" % b])
         for t, c in enumerate((1.0, 0.5, -0.5, 1.0)):
             fill(T.wt[:, t:512:4], c, ["k%d" % t])
-        fill(T.wt[:, 512:1024], -1.0, ["k4"])
-        for t, c in enumerate((0.5, 0.5, -0.5, 1.0)):
-            fill(T.wt[:, 1024 + t:1536:4], c, ["k%d" % (5 + t)])
-        scan(T.sa[:], T.m16[:], T.crow[:], ["m16", "cr0", "cr1"], ["sa"])
+        fill(T.wt[:, 512:768], -1.0, ["k4"])
+        fill(T.wt[:, 768:1024], -1.0, ["k5"])
+        scan(T.sa[:], T.m16[:], T.crow[:], ["m16", "cr0", "cr1"], ["sa0", "sa1"])
         for b in range(4):
-            ts(T.et[:, 512 * b + b:512 * b + 512:4], T.iot[:, 0:128], pcol, None, A.is_equal, None, ["iot", "pcol"], ["e%d" % b])
-        ts(T.el[:, 0:16], T.sa[:, 15:C:16], c16, None, A.add, None, ["sa", "c16"], ["el0"])
-        quant("k", T.wt[:], ["k%d" % t for t in range(9)])
+            ts(T.et[:, 512 * b + b:512 * b + 512:4], T.iot[:, 0:128], pcol, None, A.is_equal, None, ["iot", "pcol"],
+               ["z%d" % (2 * b), "z%d" % (2 * b + 1)])
+            quant_half("e", T.et, b, ["z%d" % (2 * b), "z%d" % (2 * b + 1)])
+        ts(T.el[:, 0:16], T.sa[:, 15:C:16], c16, None, A.add, None, ["sa0", "sa1", "c16"], ["el0"])
+        quant_half("k", T.wt, 0, ["k0", "k1", "k2", "k3"])
+        quant_half("k", T.wt, 1, ["k4", "k5"])
         ts(T.tri[:], T.iot[:, 0:128], pcol, None, A.is_gt, None, ["iot", "pcol"], ["tri"])
         ts(T.iq[:, 8:18], T.ip[:, 0:10], 4, None, A.arith_shift_right, None, ["ip0"], ["iq8"])
-        quant("e", T.et[:], ["e0", "e1", "e2", "e3"])
         ts(T.iq[:, 20:27], T.iq[:, 9:16], 1.0, 2.0, A.add, A.mult, ["iq8"], ["iq20"])
         ts(T.doff[:, 8:9], T.iq[:, 8:9], 2.0, None, A.mult, None, ["iq8"], ["aoff"])
         fill(T.doff[:, 7:8], 0, ["doff7"])
@@ -265,7 +275,7 @@ def rank_program(g, core, T, topo):
             ts(T.l4[:, 32 * h:32 * h + 32], T.sb[:, 128 * h + 3:128 * h + 128:4], 4.0, c4, A.mult, A.add, ["sb%d" % h, "c4"], ["l4%d" % h])
 
         def part(q, a, b, key):
-            win, r = (T.xb, ["xb"]) if first else (T.st, ["s0", "s1", "s2", "s3"])
+            win, r = (T.xb, ["xb"]) if first else (T.st, ["s%d%d" % (x, y) for x in range(4) for y in range(2)])
             move(q, T.ft[:, 16 * a:16 * b], win[:].indirect(T.l4[:, a:b]), r + ["l4%d" % (a // 32)], [key], None if first else 0.5)
         cut = OPT["cut"]
         scan4(0)
@@ -347,7 +357,7 @@ def rank_program(g, core, T, topo):
         def both():
             PE.matmul_mx(bank(k, 0, 128), T.qk[:, 0:128], T.sk[:, 0:128], T.qg[:, 2:130], T.sg[:, 2:130], True, False)
             return PE.matmul_mx(bank(k, 0, 128), T.qk[:, 128:256], T.sk[:, 128:256], T.qg[:, 0:128], T.sg[:, 0:128], False, True)
-        op("t", both, ["qk", "qg"], ["P%d" % k])
+        op("t", both, ["qk0", "qk1", "qg"], ["P%d" % k])
 
     def steps_add(k):
         op("v", lambda: V.tensor_tensor(T.dcum[:], bank(k, 0, 32), T.dcum[:], A.add), ["P%d" % k, "dcum"], ["dcum"])
@@ -362,10 +372,13 @@ def rank_program(g, core, T, topo):
         cp(T.orow[:].indirect(T.rl[:]), T.iot[:, 0:C], ["iot", "rl"], ["orow"])
 
     def unpack(b):
-        mm(4 + b, C, "e", 128 * b, "h", 0, ["qe", "qh0", "qh1"])
+        mm(4 + b, C, "e", 128 * b, "h", 0, ["qe%d" % b, "qh0", "qh1"])
 
     def add(b):
-        op("v", lambda: V.tensor_tensor(T.st[:, b:4 * C:4], bank(4 + b), T.ft[:, b:4 * C:4], A.add), ["P%d" % (4 + b)] + fkeys, ["s%d" % b])
+        for h in range(2):
+            op("v", lambda h=h: V.tensor_tensor(T.st[:, 512 * h + b:512 * h + 512:4], bank(4 + b, 128 * h, 128 * h + 128),
+                                                T.ft[:, 512 * h + b:512 * h + 512:4], A.add),
+               ["P%d" % (4 + b)] + fkeys[2 * h:2 * h + 2], ["s%d%d" % (b, h)])
 
     def swap(q, h):
         move(q, T.oswp[:, h:C:2], T.orow[:, 1 - h:C:2], ["orow"], ["osw%d" % h])
@@ -395,7 +408,7 @@ def rank_program(g, core, T, topo):
             unpack(b)
         ties(1)
         steps_add(0)
-        cuts = ((0, 2), (2, 8))
+        cuts = ((0, 2), (4, 8), (2, 4))
 
         def turned(x):
             a, b = cuts[x]
@@ -408,10 +421,10 @@ def rank_program(g, core, T, topo):
 
         def offsets(x):
             a, b = cuts[x]
-            cp(T.off[:, 16 * a:16 * b], T.lj[:, 16 * a:16 * b], ["lj%d" % x], ["off" if x else "off0"])
+            cp(T.off[:, 16 * a:16 * b], T.lj[:, 16 * a:16 * b], ["lj%d" % x], [("off0", "off", "off2")[x]])
 
         def ranks():
-            mm(1, C, "k", 256 if offact else 0, "c", 0, ["qk", "qc0", "qc1"])
+            mm(1, C, "k", 0, "c", 0, ["qk0", "qc0", "qc1"])
 
         def codes(h):
             quant_half("c", T.ct, h, ["c%d%d" % (t, h) for t in range(4)])
@@ -442,44 +455,61 @@ def rank_program(g, core, T, topo):
             codes(1)
             ranks()
 
-        def step(s, a=0, b=16, key=None):
-            src, to = ("rho" if s == 0 else "tb" if s % 2 == 0 else "ta"), ("ta" if s % 2 == 0 else "tb")
-            act(T[to][:, 16 * a:16 * b], T[src][:].indirect(T.off[:, 16 * s + a:16 * s + b]),
-                ([src] if src != "tb" else ["tb", "tb1"]) + ["off0" if s < 2 else "off"], key or ([to] if to != "tb" else ["tb", "tb1"]))
-        gm = OPT["gm"]
-        for s in range(min(gm, 7)):
-            step(s)
-        if OPT["qc"] >= 2:
-            add(0)
-        rank_list(128.0 if offact else 64.0, lambda: ts(T.ej[:, 0:1], T.ei[:, 0:1], 255, None, A.bitwise_and, None, ["ei"], ["ej"]))
+        turned(2)
+        wrapped(2)
+        offsets(2)
+
+        def step(src, to, s):
+            act(T[to][:, 0:C], T[src][:, 0:C].indirect(lists(s)), [src, "off0" if s < 2 else "off2" if s < 4 else "off"], [to])
+        cp(T.di[:], T.dcum[:].indirect(T.doff[:, 4:5]), ["dcum", "doff0"], ["di"])
+        ts(T.dj[:, 0:1], T.di[:, 0:1], 255, None, A.bitwise_and, None, ["di"], ["dj"])
+        ts(T.acol[:, 8:9], T.dj[:, 0:1], c16, None, A.add, None, ["dj", "c16"], ["dcol"])
+        step("rho", "ta", 0)
+        step("r5", "rb", 5)
+        step("ta", "tb", 1)
+        step("rb", "ra", 6)
+        step("tb", "ta", 2)
+        step("ra", "rb", 7)
+        step("ta", "tl", 3)
+        move(OPT["dbl"], T.tl[:, C:2 * C], T.tl[:, 0:C], ["tl"], ["tl2"])
+        scan(T.sr[:], T.m16[:], T.rb[:], ["m16", "rb"], ["sr"])
+        ts(T.ml[:], T.sr[:, 15:C:16], T.acol[:, 8:9], None, A.add, None, ["sr", "dcol"], ["ml"])
+        for h in range(2):
+            move(OPT["e"][h], T.erow[:, 128 * h:128 * h + 128], T.tl[:].indirect(T.ml[:, 8 * h:8 * h + 8]), ["tl", "tl2", "ml"], ["er%d" % h])
+        rank_list(64.0, lambda: ts(T.ej[:, 0:1], T.ei[:, 0:1], 255, None, A.bitwise_and, None, ["ei"], ["ej"]))
         ts(T.acol[:, 0:1], T.ej[:, 0:1], -1.0, c16, A.mult, A.add, ["ej", "c16"], ["acol"])
         swap("v", 0)
-        swap("v", 1)
-        rest = [1, 2, 3] if OPT["qc"] >= 2 else [0, 1, 2, 3]
-        if gm < 8:
-            partners("a")
-            for s in range(gm, 7):
-                step(s)
-            for _ in range(OPT["slot"]):
-                add(rest.pop())
-        else:
-            partners("v")
-        step(7, 0, 8, ["tb"])
-        step(7, 8, 16, ["tb1"])
-        cp(T.come[:, 0:C].indirect(T.el[:, 16 * i:16 * i + 16]), T.mrow[:], ["mrow", "el%d" % i], ["come"])
-        act(T.come[:, C:2 * C], T.come[:, 0:C], ["come"], ["come2"])
-        while len(rest) > OPT["gaps"]:
-            add(rest.pop())
+        swap(OPT["swap"], 1)
+        partners(OPT["gm"])
+        for b in range(4):
+            add(b)
         for h in range(2):
-            scan(T.sa[:, 128 * h:128 * h + 128], T.m16[:, 0:128], T.tb[:, 128 * h:128 * h + 128], ["m16", "tb1" if h else "tb"], ["sa%d" % h])
-        for h in range(2):
+            scan(T.sa[:, 128 * h:128 * h + 128], T.m16[:, 0:128], T.erow[:, 128 * h:128 * h + 128], ["m16", "er%d" % h], ["sa%d" % h])
             ts(T.ol[:, 8 * h:8 * h + 8], T.sa[:, 128 * h + 15:128 * h + 128:16], T.acol[:, 0:1], 256.0, A.add, A.add, ["sa%d" % h, "acol"], ["ol%d" % h])
-        if rest:
-            act(T.crow[:, 0:128], T.come[:].indirect(T.ol[:, 0:8]), ["come", "come2", "ol0"], ["cr0"])
-            add(rest.pop())
+        if OPT["back"]:
+            back(i)
+            move(OPT["dbl"], T.come[:, C:2 * C], T.come[:, 0:C], ["come"], ["come2"])
+            for h in range(2):
+                move(OPT["b"][h], T.brow[:, 128 * h:128 * h + 128], T.come[:].indirect(T.ol[:, 8 * h:8 * h + 8]), ["come", "come2", "ol%d" % h], ["br%d" % h])
+            through(T.brow, ["br0", "br1"])
+            for f in path_list(i + 1):
+                f()
         else:
-            cp(T.crow[:, 0:128], T.come[:].indirect(T.ol[:, 0:8]), ["come", "come2", "ol0"], ["cr0"])
-        act(T.crow[:, 128:C], T.come[:].indirect(T.ol[:, 8:16]), ["come", "come2", "ol1"], ["cr1"])
+            for f in path_list(i + 1):
+                f()
+            cp(T.come[:, 0:C].indirect(T.el[:, 16 * i:16 * i + 16]), T.mrow[:], ["mrow", "el%d" % i], ["come"])
+            for h in range(2):
+                e = 16 * (i + 1) + 8 * h
+                move("va"[h], T.crow[:, 128 * h:128 * h + 128], T.come[:, 0:C].indirect(T.el[:, e:e + 8]), ["come", "el%d" % (i + 1)], ["cr%d" % h])
+
+    def back(i):
+        cp(T.come[:, 0:C].indirect(T.el[:, 16 * i:16 * i + 16]), T.iot[:, 0:C], ["iot", "el%d" % i], ["come"])
+
+    def through(row, keys):
+        for h in range(2):
+            scan(T.sc2[:, 128 * h:128 * h + 128], T.m16[:, 0:128], row[:, 128 * h:128 * h + 128], ["m16", keys[h]], ["s2%d" % h])
+            ts(T.bl[:, 8 * h:8 * h + 8], T.sc2[:, 128 * h + 15:128 * h + 128:16], c16, None, A.add, None, ["s2%d" % h, "c16"], ["bl%d" % h])
+            move("va"[h], T.crow[:, 128 * h:128 * h + 128], T.mrow[:].indirect(T.bl[:, 8 * h:8 * h + 8]), ["mrow", "bl%d" % h], ["cr%d" % h])
 
     def path_list(i):
         def first():
@@ -503,8 +533,9 @@ def rank_program(g, core, T, topo):
         ties(0)
         ties(1)
         flag(1)
-        quant("c", T.ct[:], ckeys)
-        mm(1, C, "k", 0, "c", 0, ["qk", "qc"])
+        for h in range(2):
+            quant_half("c", T.ct, h, ["c%d%d" % (t, h) for t in range(4)])
+        mm(1, C, "k", 0, "c", 0, ["qk0", "qc0", "qc1"])
         quant("g", T.gt[:], ["g0", "g1"])
         counts(0)
         add(0)
@@ -520,11 +551,16 @@ def rank_program(g, core, T, topo):
         add(2)
         ts(T.ol[:, 0:16], T.ej[:], T.acol[:, 0:1], None, A.add, None, ["ej", "acol"], ["ol0", "ol1"])
         act(T.optab[:], T.iot[:].indirect(T.ol[:, 0:16]), ["iot", "iot2", "ol0", "ol1"], ["optab"])
-        cp(T.come[:, 0:C].indirect(T.el[:, 16 * i:16 * i + 16]), T.mrow[:], ["mrow", "el%d" % i], ["come"])
-        if not OPT["fin"]:
-            add(3)
-        gather(False, T.come, ["come", "come"], "x",
-               (lambda: scan(T.sa[:], T.m16[:], T.come[:, 0:C], ["m16", "come"], ["sa0", "sa1"]),
+        if OPT["lastback"]:
+            back(i)
+            through(T.come, ["come", "come"])
+            row, keys = T.crow, ["cr0", "cr1"]
+        else:
+            cp(T.come[:, 0:C].indirect(T.el[:, 16 * i:16 * i + 16]), T.mrow[:], ["mrow", "el%d" % i], ["come"])
+            row, keys = T.come, ["come", "come"]
+        add(3)
+        gather(False, row, keys, "x",
+               (lambda: scan(T.sa[:], T.m16[:], row[:, 0:C], ["m16"] + keys, ["sa0", "sa1"]),
                 lambda: ts(T.ol[:, 16:32], T.sa[:, 15:C:16], c16, None, A.add, None, ["sa0", "sa1", "c16"], ["ol2"])))
         mm(2, 128, "v", 0, "x", 0, ["qv", "qx0"])
         mm(3, 128, "v", 0, "x", 128, ["qv", "qx1"])
@@ -544,15 +580,16 @@ def rank_program(g, core, T, topo):
         scales("a", 3)
 
     for i in range(3):
-        gap = path_list(i) if i else (nothing, nothing, nothing)
-        gather(i == 0, T.crow, ["cr0", "cr1"], "f", gap)
-        gap[2]()
+        gather(i == 0, T.crow, ["cr0", "cr1"], "f")
         layer(i)
         if i < 2:
             turn(i)
         else:
             last(i)
 
+    OPT["calls"] = calls
+    for k in (OPT["order"] or range(len(calls))):
+        emit(*calls[k])
     for s in SEMAPHORES:
         if known["g"].get(s, 0) < count.get(s, 0):
             g.wait_ge(T.sem[s], count[s])

@@ -6,12 +6,11 @@ COPY = ActivationFunctionType.Copy
 SIGN = ActivationFunctionType.Sign
 C = 256
 TURN = [1, 2, 4]
-UP = 144
+UP = 192
 X4 = "float8_e4m3fn_x4"
-OPT = {"offact": 0, "gm": "a", "cut": 42, "qc": 1, "fin": 0, "dbl": "a", "e": "aa", "b": "aa", "swap": "a", "back": 1, "lastback": 1,
-       "order": None}
-OPT["order"] = [
-    0,2,13,52,1,3,95,4,10,14,5,11,113,6,12,15,7,21,8,22,9,20,16,96,24,110,23,28,26,25,38,40,37,39,36,31,35,34,30,29,27,49,32,46,53,71,33,108,41,42,72,112,44,45,88,48,47,87,51,50,55,54,57,43,85,56,60,69,59,58,17,61,111,86,114,70,62,93,100,18,92,102,91,63,74,73,94,76,64,75,19,79,81,65,78,77,66,82,103,67,109,80,121,123,97,68,120,84,122,83,117,134,118,107,132,119,133,116,125,128,126,127,124,135,98,129,138,101,136,99,130,154,144,143,137,140,131,139,149,153,106,145,152,141,147,146,198,142,197,156,157,150,164,158,172,166,160,169,173,163,165,174,168,175,89,167,170,151,176,90,188,171,148,177,191,161,159,178,207,162,179,180,187,181,196,183,189,104,184,182,190,186,185,205,208,200,203,206,193,192,204,105,210,217,209,195,155,218,194,214,199,215,201,211,216,115,212,202,221,213,223,219,220,226,222,228,224,225,229,227,237,321,236,230,233,248,232,231,238,234,235,240,241,239,247,242,246,322,243,249,244,250,251,253,245,254,268,257,258,252,266,259,255,263,313,260,261,256,314,269,262,267,271,264,272,278,274,280,277,270,265,289,282,286,275,279,290,273,283,315,276,291,287,284,281,288,285,292,301,302,293,303,309,294,304,295,297,296,305,306,298,312,307,316,299,311,310,300,317,308,319,318,320,323,331,324,325,332,328,326,333,329,327,330,334,335,336,337,338,339,342,340,341,346,344,343,345,405,347,349,352,351,354,350,348,360,353,355,362,361,357,356,358,359,363,367,368,364,365,369,377,371,376,370,380,382,366,373,378,375,374,372,381,383,379,384,401,402,385,412,413,409,390,410,406,392,386,393,387,391,407,394,395,397,399,396,400,398,403,389,408,411,388,404,414,415,416,417,421,418,419,420,423,422,424,426,425,428,427,430,431,432,429,433,434,436,435,437,438]
+OPT = {"wake": 150, "bias": 120, "gather": 1.2, "scatter": 2.6, "load": 2000, "hop": 2600, "far": 5000, "passes": 1,
+       "other": "a", "cuts": (16, 32, 42), "casts": "vavaavav", "big": "vava",
+       "join": "aa", "m": "va", "crow": "va", "left": "aaa", "right": "aaaa", "dbl": "v", "swap": "vv", "rhalf": 0}
 
 
 def _pair(name, n):
@@ -23,24 +22,112 @@ def _of(dtype, n, *names):
 
 
 SCRATCH = {"ps": ("psum", [128, 4096], "float32")}
-for _d in (_of("bfloat16", 4 * C, "xb", "ft", "ht", "ct", "iot"), _of("bfloat16", 512, "ub", "vb"), _of("float32", 4 * C, "st"),
-           _of("bfloat16", 4 * 130, "gt"), _of("bfloat16", 2048, "et"), _of("bfloat16", 1536, "wt"),
-           _of("int32", 144, "lst"), _of("int32", 128, "li", "lj"), _of("uint16", 128, "off"),
-           _of("bfloat16", C, "rho", "ta", "tb", "ra", "rb", "m16", "m4", "sa", "sb", "sg2", "orow", "oswp", "mrow", "crow", "optab"),
-           _of("bfloat16", 2 * C, "come", "tl"), _of("bfloat16", C, "r5", "sr", "erow", "brow", "sc2"),
-           _of("uint16", 16, "ml", "bl"), _of("int32", 16, "di", "dj"),
-           _of("float32", C, "sf32", "oprow", "yb"), _of("bfloat16", 128, "tri"),
-           _of("uint16", 16, "rl", "moff"), _of("uint16", 48, "el"), _of("uint16", 64, "l4"), _of("uint16", 32, "ol"),
-           _of("uint16", 10, "uoff", "doff"), _of("int32", 16, "ei", "ej", "ident"), _of("int32", 32, "ip", "iq"),
-           _of("float32", 16, "col", "acol"), _of("float32", 32, "cc", "dm", "a1", "a2", "dcum", "acum", "zer"),
-           _of("bfloat16", 32, "msm"), _of("float32", 8, "scol")):
+for _d in (_of("bfloat16", 4 * C, "xb", "ft", "ht", "ct"), _of("bfloat16", 512, "ub", "vb", "kp", "kn", "tl"), _of("float32", 4 * C, "st"),
+           _of("bfloat16", 4 * 136, "gt"), _of("bfloat16", 528, "ea", "eb"), _of("bfloat16", 3 * C, "s3", "r3"),
+           _of("int32", 144, "lst", "li", "lj"), _of("uint16", 144, "off"), _of("uint16", 16, "o6", "o2", "jl", "el", "rl", "cl", "ul", "il", "moff", "goff", "uoff"),
+           _of("bfloat16", C, "iot", "ta", "tb", "ra", "rb", "rc", "m16", "sa", "sb", "sr", "se2", "sg2", "orow", "oswp", "mrow", "me", "crow",
+               "erow", "einv", "optab"),
+           _of("bfloat16", 128, "m4", "tri"), _of("float32", C, "sf32", "oprow", "yb"), _of("uint16", 64, "l4"),
+           _of("int32", 16, "eli", "ei", "ej", "ek", "em", "ip", "iq"), _of("uint16", 2, "aoff"),
+           _of("float32", 16, "col", "acol", "dcum", "acum", "zer", "scol", "dcol"), _of("float32", 32, "cc", "dm", "a1", "a2"),
+           _of("bfloat16", 32, "msm")):
     SCRATCH.update(_d)
 for _n, _k in (("w", 512), ("w0", 512), ("w1", 512), ("w2", 512), ("u", 128), ("up", UP), ("u0", UP), ("u1", UP), ("u2", UP),
-               ("v", 128), ("f", C), ("h", C), ("c", C), ("g", 130), ("e", 512), ("k", 384), ("x", C)):
+               ("v", 128), ("f", C), ("h", C), ("c", C), ("g", 136), ("e", 512), ("k", C), ("x", C)):
     SCRATCH.update(_pair(_n, _k))
 
-SEMAPHORES = ["cv", "ca", "ct", "cg", "lp", "lws", "lwc", "lu", "lx", "lv", "sent",
+SEMAPHORES = ["cv", "ca", "ct", "cg", "lp", "lws", "lwc", "lu", "lx", "lv", "sent", "tripled0", "tripled1",
               "aw0", "aw1", "aw2", "au0", "au1", "au2", "outs", "outa"]
+SIZE = {"float32": 4, "int32": 4, X4: 4, "bfloat16": 2, "uint16": 2, "uint8": 1}
+CYCLE = 0.83
+
+
+def view(name, a=0, b=None, step=1, p0=0, p1=128):
+    return (name, a, SCRATCH[name][1][1] if b is None else b, step, p0, p1)
+
+
+def width(x):
+    return len(range(x[1], x[2], x[3]))
+
+
+def marks(x):
+    if x[0] == "ps":
+        return ("ps", 1 << (x[1] // 512), 1)
+    return (x[0], sum(1 << c for c in range(x[1], x[2], x[3])), (1 << x[5]) - (1 << x[4]))
+
+
+def meet(a, b):
+    return a[0] == b[0] and a[1] & b[1] and a[2] & b[2]
+
+
+def plan(calls):
+    n, wake = len(calls), OPT["wake"]
+    before = [{} for _ in calls]
+    seen = {}
+    for k, c in enumerate(calls):
+        before[k].update((j, 0) for j in c["after"])
+        for x, writes in [(x, False) for x in c["r"]] + [(x, True) for x in c["w"]]:
+            for j, y, wrote in seen.get(x[0], []):
+                if j != k and (writes or wrote) and meet(x, y):
+                    before[k][j] = calls[j]["late"] + wake
+            seen.setdefault(x[0], []).append((k, x, writes))
+    after = [{} for _ in calls]
+    for k in range(n):
+        for j, lag in before[k].items():
+            after[j][k] = lag
+
+    def lay(rank, edges, first, fixed):
+        busy = {q: [] for q in "vatgs"}
+        banks = {}
+        start, end, on = [0.0] * n, [0.0] * n, [None] * n
+        left = [len(edges[0][k]) for k in range(n)]
+        ready = [k for k in range(n) if not left[k]]
+        while ready:
+            k = max(ready, key=lambda j: (rank[j], -j))
+            ready.remove(k)
+            c = calls[k]
+            t0 = max([end[j] + lag for j, lag in edges[0][k].items()] + [first[k]])
+            held = [x[1] for x in c["r"] + c["w"] if x[0] == "ps"]
+            best = None
+            for q, cost in c["cost"].items():
+                if fixed and fixed[k] != q:
+                    continue
+                taken = sorted(busy[q] + [(a - wake, b + wake) for m in held for a, b, o in banks.get(m, []) if o != q])
+                t = t0
+                for a, b in taken:
+                    if t + cost <= a:
+                        break
+                    t = max(t, b)
+                score = t + cost + (OPT["bias"] if q == "v" else 0)
+                if best is None or score < best[0]:
+                    best = (score, q, t, cost)
+            _, q, t, cost = best
+            start[k], end[k], on[k] = t, t + cost, q
+            busy[q].append((t, t + cost))
+            for m in held:
+                banks.setdefault(m, []).append((t, t + cost, q))
+            for j in edges[1][k]:
+                left[j] -= 1
+                if not left[j]:
+                    ready.append(j)
+        return start, end, on
+
+    rank = [0.0] * n
+    for k in reversed(range(n)):
+        rank[k] = min(calls[k]["cost"].values()) + max([rank[j] + lag for j, lag in after[k].items()] + [calls[k]["late"]])
+    best = None
+    late = [c["late"] for c in calls]
+    for _ in range(OPT["passes"]):
+        start, end, on = lay(rank, (before, after), [0.0] * n, None)
+        total = max(e + t for e, t in zip(end, late))
+        if best is None or total < best[0]:
+            best = (total, start, on)
+        rank = lay(end, (after, before), late, on)[1]
+    PLAN["length"] = best[0]
+    return [(k, best[2][k]) for k in sorted(range(n), key=lambda k: (best[1][k], k))]
+
+
+PLAN = {}
 
 
 def rank_program(g, core, T, topo):
@@ -49,140 +136,172 @@ def rank_program(g, core, T, topo):
         return
     Q = {"v": g.vector, "a": g.scalar, "t": g.tensor, "g": g, "s": g.sync}
     V, S, PE = g.vector, g.scalar, g.tensor
-    known = {q: {} for q in Q}
-    count = {}
-    wrote, read = {}, {}
-    serial = [0]
-
-    def need(q, evs):
-        for ev in sorted(evs, key=lambda e: -e[3]):
-            if known[q].get(ev[0], 0) < ev[1]:
-                Q[q].wait_ge(T.sem[ev[0]], ev[1])
-                for s, n in ev[2].items():
-                    known[q][s] = max(known[q].get(s, 0), n)
-
     calls = []
 
-    def op(q, make, r=(), w=(), sem=None, n=1, upto=None, inc=True):
-        calls.append((q, make, r, w, sem, n, upto, inc))
+    def ap(x):
+        if not isinstance(x, tuple):
+            return x
+        if x[0] == "by":
+            return ap(x[1]).indirect(ap(x[2]))
+        return T[x[0]][x[4]:x[5], x[1]:x[2]:x[3]]
 
-    def emit(q, make, r, w, sem, n, upto, inc):
-        evs = []
-        for k in r:
-            if k in wrote:
-                evs.append(wrote[k])
-            if k[0] == "P":
-                evs += [e for e in read.get(k, []) if e[4] != q]
-        for k in w:
-            if k in wrote:
-                evs.append(wrote[k])
-            evs += read.get(k, [])
-        need(q, evs)
-        ins = make()
-        sem = sem or "c" + q
-        count[sem] = count.get(sem, 0) + n
-        if inc:
-            ins.then_inc(T.sem[sem], n)
-        clock = dict(known[q])
-        clock[sem] = upto or count[sem]
-        serial[0] += 1
-        ev = (sem, clock[sem], clock, serial[0], q)
-        for k in r:
-            read.setdefault(k, []).append(ev)
-        for k in w:
-            wrote[k] = ev
-            read[k] = []
+    def by(win, off):
+        return ("by", win, off)
 
-    def arrives(key, sem, n):
-        count[sem] = n
-        wrote[key] = (sem, n, {sem: n}, 0, "x")
+    def parts(xs):
+        out = []
+        for x in xs:
+            if isinstance(x, tuple):
+                out += [x[1], x[2]] if x[0] == "by" else [x]
+        return out
 
-    def bank(k, a=0, b=C):
-        return T.ps[:, 512 * k + a:512 * k + b]
+    def op(cost, make, r=(), w=(), sem=None, n=1, upto=None, inc=True, late=0, after=()):
+        calls.append({"cost": cost, "make": make, "r": [marks(x) for x in parts(r)], "w": [marks(x) for x in parts(w)],
+                      "sem": sem, "n": n, "upto": upto, "inc": inc, "late": late, "after": list(after)})
+        return len(calls) - 1
 
-    def ts(out, in0, s1, s2, op0, op1, r, w):
-        if op1 is None:
-            op("v", lambda: V.tensor_scalar(out, in0, s1, None, op0), r, w)
-        else:
-            op("v", lambda: V.tensor_scalar(out, in0, s1, s2, op0, op1), r, w)
-
-    def cp(out, in_, r, w):
-        op("v", lambda: V.tensor_copy(out, in_), r, w)
-
-    def act(out, in_, r, w, scale=None):
-        if scale is None:
-            op("a", lambda: S.activation(out, in_, COPY), r, w)
-        else:
-            op("a", lambda: S.activation(out, in_, COPY, scale=scale), r, w)
-
-    def move(q, out, in_, r, w, scale=None):
+    def length(q, out, *ins):
+        if out[0] == "by":
+            return 50 + 16 * width(out[2]) * OPT["scatter"]
+        if ins and ins[0][0] == "by":
+            return (50 if q == "v" else 65) + width(out) * OPT["gather"]
         if q == "a":
-            act(out, in_, r, w, scale)
-        elif scale is None:
-            cp(out, in_, r, w)
+            return 60 + width(out) * CYCLE
+        narrow = all(SIZE[SCRATCH[x[0]][2]] == 2 for x in (out,) + ins)
+        return max(64, width(out) * (0.5 if narrow else 1)) * CYCLE
+
+    def bank(k, a=0, b=C, step=1):
+        return view("ps", 512 * k + a, 512 * k + b, step)
+
+    def ts(out, in0, s1, s2, op0, op1=None):
+        more = () if op1 is None else (op1,)
+        op({"v": length("v", out, in0)}, lambda q: V.tensor_scalar(ap(out), ap(in0), ap(s1), ap(s2), op0, *more), [in0, s1, s2], [out])
+
+    def tt(out, in0, in1, how):
+        twice = 1 if "ps" in (in0[0], in1[0]) else 2
+        op({"v": max(64, width(out) * twice) * CYCLE}, lambda q: V.tensor_tensor(ap(out), ap(in0), ap(in1), how), [in0, in1], [out])
+
+    def move(qs, out, in_, scale=None):
+        def make(q):
+            if q == "a":
+                return S.activation(ap(out), ap(in_), COPY) if scale is None else S.activation(ap(out), ap(in_), COPY, scale=scale)
+            return V.tensor_copy(ap(out), ap(in_)) if scale is None else V.tensor_scalar(ap(out), ap(in_), scale, None, A.mult)
+        r, w = ([in_, out[2]], [out[1]]) if out[0] == "by" else ([in_], [out])
+        op({q: length(q, out, in_) for q in qs}, make, r, w)
+
+    def halves(qs, out, win, off):
+        if len(qs) == 1:
+            move(qs, view(out, 0, C), by(win, view(off, 0, 16)))
         else:
-            ts(out, in_, scale, None, A.mult, None, r, w)
+            for h in range(2):
+                move(qs[h], view(out, 128 * h, 128 * h + 128), by(win, view(off, 8 * h, 8 * h + 8)))
 
-    def fill(ap, c, w):
-        op("v", lambda: V.memset(ap, c), (), w)
+    def fill(out, c):
+        op({"v": length("v", out)}, lambda q: V.memset(ap(out), c), (), [out])
 
-    def quant(name, tile, r):
-        op("v", lambda: V.quantize_mx(T["q" + name][:], T["s" + name][:], tile), r, ["q" + name])
+    def sign(out, in_, bias, scale):
+        op({"a": length("a", out)}, lambda q: S.activation(ap(out), ap(in_), SIGN, bias=ap(bias), scale=scale), [in_, bias], [out])
 
-    def quant_half(name, tile, h, r):
-        a, b = 128 * h, 128 * h + 128
-        op("v", lambda: V.quantize_mx(T["q" + name][:, a:b], T["s" + name][:, a:b], tile[:, 4 * a:4 * b]), r, ["q%s%d" % (name, h)])
+    def quant(name, a, n, tile):
+        q, s = view("q" + name, a, a + n), view("s" + name, a, a + n)
+        op({"v": 12 + 0.88 * n}, lambda _: V.quantize_mx(ap(q), ap(s), ap(tile)), [tile], [q, s])
 
-    def mm(k, n, a, a0, b, b0, r):
-        op("t", lambda: PE.matmul_mx(bank(k, 0, n), T["q" + a][:, a0:a0 + 128], T["s" + a][:, a0:a0 + 128],
-                                     T["q" + b][:, b0:b0 + n], T["s" + b][:, b0:b0 + n], True, True), r, ["P%d" % k])
+    def mm(k, n, *sides):
+        vs = [(view("q" + a, a0, a0 + 128), view("s" + a, a0, a0 + 128), view("q" + b, b0, b0 + n), view("s" + b, b0, b0 + n)) for a, a0, b, b0 in sides]
 
-    def scan(out, mask, row, r, w):
-        op("v", lambda: V.tensor_tensor_scan(out, mask, row, 0.0, A.add, A.min), r, w)
+        def make(q):
+            return [PE.matmul_mx(ap(bank(k, 0, n)), ap(x[0]), ap(x[1]), ap(x[2]), ap(x[3]), j == 0, j == len(vs) - 1) for j, x in enumerate(vs)][-1]
+        op({"t": len(vs) * (n + 16) * 0.6}, make, [y for x in vs for y in x], [bank(k, 0, n)])
 
-    pcol, icol, qcol, tcol, c16, c4, tmp, tmq = [T.col[:, k:k + 1] for k in range(8)]
+    def scan(out, d0, d1, op0=A.add, op1=A.min):
+        op({"v": length("v", out, d0, d1)}, lambda q: V.tensor_tensor_scan(ap(out), ap(d0), ap(d1), 0.0, op0, op1), [d0, d1], [out])
 
-    op("s", lambda: g.sync.dma_start(T.sw[:], T.ws[:]), (), ["sw"], "lws", 16)
-    op("s", lambda: g.sync.dma_start(T.qw[:].bitcast(dt.uint8), T.wc[:]), (), ["qw"], "lwc", 16)
+    def iota(out, pattern, base, mult):
+        more = {} if SCRATCH[out[0]][2] == "int32" else {"allow_small_or_imprecise_dtypes": True}
+        op({"g": 130 + 2 * CYCLE * width(out)}, lambda q: g.iota(ap(out), pattern, base, mult, **more), (), [out])
+
+    def dma(q, out, in_, r, w, sem, upto=None, late=0, after=()):
+        return op({q: 60}, lambda _: Q[q].dma_start(out, in_), r, w, sem, 16, upto, late=OPT["load"] + late, after=after)
+
+    def col(name, k):
+        return view(name, k, k + 1)
+
+    def to_list(out, row, tmp, plus, a=0, b=C):
+        scan(view(tmp, a, b), view("m16", 0, b - a), row)
+        ts(view(out, a // 16, b // 16), view(tmp, a + 15, b, 16), plus, None, A.add)
+
+    pcol, icol, qcol, tcol, c16, c4, c80, tmp, tmq, tmr = [col("col", k) for k in range(10)]
+
     for s in range(8):
-        op("a", lambda s=s: S.dma_start(T.lst[16 * s:128, 16 * s:16 * s + 16], T.p[0:128 - 16 * s, :]), (), ["lp%d" % s], "lp", 16, 128)
-    op("s", lambda: g.sync.dma_start(T.ub[:], T.u[:]), (), ["ub"], "lu", 16)
-    op("s", lambda: g.sync.dma_start(T.xb[:], T.x[:]), (), ["xb"], "lx", 16)
-    op("s", lambda: g.sync.dma_start(T.vb[:], T.v[:]), (), ["vb"], "lv", 16)
+        dma("sa"[s % 2], T.lst[16 * s:128, 16 * s + 16:16 * s + 32], T.p[0:128 - 16 * s, :], (), [view("lst", 16 * s + 16, 16 * s + 32, 1, 16 * s)], "lp", 128)
+    lws = dma("s", T.sw[:], T.ws[:], (), [view("sw")], "lws", late=200, after=range(8))
+    lwc = dma("a", T.qw[:].bitcast(dt.uint8), T.wc[:], (), [view("qw")], "lwc", late=900, after=range(8))
+    lu = dma("s", T.ub[:], T.u[:], (), [view("ub")], "lu", late=1200, after=range(8))
+    dma("s", T.xb[:], T.x[:], (), [view("xb")], "lx", late=800, after=[lws])
+    dma("s", T.vb[:], T.v[:], (), [view("vb")], "lv", late=400, after=[lu])
 
-    op("g", lambda: g.iota(T.ip[:, 0:10], [[-16, 10]], 0, 1), (), ["ip0"])
-    op("g", lambda: g.iota(T.cc[:, 0:16], [[1, 16]], 0, 0, allow_small_or_imprecise_dtypes=True), (), ["cc0"])
-    op("g", lambda: g.iota(T.cc[:, 16:32], [[0, 4], [1, 4]], 0, 0, allow_small_or_imprecise_dtypes=True), (), ["cc1"])
-    op("g", lambda: g.iota(T.iot[:, 0:C], [[1, C]], 0, 0, allow_small_or_imprecise_dtypes=True), (), ["iot"])
+    iota(view("ip", 0, 10), [[-16, 10]], 16, 1)
+    iota(view("cc", 0, 16), [[1, 16]], 0, 0)
+    iota(view("cc", 16, 32), [[0, 4], [1, 4]], 0, 0)
+    iota(view("iot"), [[1, C]], 0, 0)
+    p32 = col("ip", 1)
+    ts(col("iq", 0), p32, 15, None, A.bitwise_and)
+    ts(col("iq", 1), p32, 2, 3, A.arith_shift_right, A.bitwise_and)
+    ts(col("iq", 2), p32, 3, None, A.bitwise_and)
+    ts(col("iq", 3), p32, 4, None, A.arith_shift_right)
+    move("v", pcol, p32)
+    move("v", view("col", 1, 4), view("iq", 0, 3))
+    ts(tmp, icol, -16.0, None, A.add)
+    ts(view("goff", 1, 10), view("ip", 1, 10), tmp, 16.0, A.max, A.add)
+    move("v", col("goff", 0), icol)
+    ts(view("lst", 0, 16), view("cc", 0, 16), 16.0, icol, A.mult, A.add)
+    for s in range(1, 8):
+        fill(view("lst", 16 * s + 16, 16 * s + 32, 1, 0, 16 * s), 0)
+    ts(view("dm", 0, 16), view("cc", 0, 16), icol, None, A.subtract)
+    ts(view("dm", 16, 32), view("cc", 16, 32), qcol, None, A.subtract)
+    ts(view("moff"), view("cc", 0, 16), 0.0, icol, A.mult, A.add)
+    ts(view("a1"), view("dm"), 0.0, 1024.0, A.is_equal, A.mult)
+    ts(view("a2"), view("dm"), 1.0, -256.0, A.is_equal, A.mult)
+    tt(view("msm"), view("a1"), view("a2"), A.add)
+    move("a", view("m16"), by(view("msm", 0, 16), view("moff")))
+    move("a", view("m4"), by(view("msm", 16, 32), view("moff", 0, 8)))
+    ts(c16, icol, 15.0, 256.0, A.is_lt, A.mult)
+    ts(c80, c16, 64.0, None, A.add)
+    short = (c80, c80)
+    if OPT["other"] == "a":
+        short = (c80, col("col", 10))
+        ts(short[1], c16, 128.0, None, A.add)
+    ts(tmq, qcol, 3.0, 1024.0, A.is_lt, A.mult)
+    ts(c4, tmq, tcol, None, A.add)
+    ts(tmr, icol, 8.0, 16.0, A.is_ge, A.mult)
+    ts(view("dm", 0, 4), view("cc", 0, 4), 32.0, 1.0, A.mult, A.add)
+    ts(view("uoff", 0, 4), view("dm", 0, 4), tmr, None, A.add)
+    fill(view("uoff", 4, 12), 0)
+    move("v", col("aoff", 0), col("iq", 3))
 
-    fill(T.gt[:], 0.0, ["g0", "g1"])
-    fill(T.dcum[:], 0.0, ["dcum"])
-    fill(T.zer[:], 0.0, ["zer"])
-    ts(T.iq[:, 0:1], T.ip[:, 0:1], 15, None, A.bitwise_and, None, ["ip0"], ["iq0"])
-    ts(T.iq[:, 1:2], T.ip[:, 0:1], 2, 3, A.arith_shift_right, A.bitwise_and, ["ip0"], ["iq1"])
-    ts(T.iq[:, 2:3], T.ip[:, 0:1], 3, None, A.bitwise_and, None, ["ip0"], ["iq2"])
-    cp(pcol, T.ip[:, 0:1], ["ip0"], ["pcol"])
-    cp(T.col[:, 1:4], T.iq[:, 0:3], ["iq0", "iq1", "iq2"], ["icol"])
-    ts(T.dm[:, 0:16], T.cc[:, 0:16], icol, None, A.subtract, None, ["cc0", "icol"], ["dm0"])
-    ts(T.dm[:, 16:32], T.cc[:, 16:32], qcol, None, A.subtract, None, ["cc1", "icol"], ["dm1"])
-    ts(T.moff[:], T.cc[:, 0:16], 0.0, icol, A.mult, A.add, ["cc0", "icol"], ["moff"])
-    ts(T.ident[:], T.cc[:, 0:16], 16.0, icol, A.mult, A.add, ["cc0", "icol"], ["ident"])
-    ts(T.a1[:], T.dm[:], 0.0, 1024.0, A.is_equal, A.mult, ["dm0", "dm1"], ["a1"])
-    ts(T.a2[:], T.dm[:], 1.0, -256.0, A.is_equal, A.mult, ["dm0", "dm1"], ["a2"])
-    cp(T.lst[0:16, 16:32], T.ident[0:16, :], ["ident"], ["li1"])
-    op("v", lambda: V.tensor_tensor(T.msm[:], T.a1[:], T.a2[:], A.add), ["a1", "a2"], ["msm"])
-    act(T.m16[:], T.msm[:, 0:16].indirect(T.moff[:]), ["msm", "moff"], ["m16"])
-    for s in range(2, 9):
-        cp(T.lst[0:16 * s, 16 * s:16 * s + 16], T.ident[0:16 * s, :], ["ident"], ["li%d" % s])
-    base = ["lp%d" % s for s in range(8)] + ["li%d" % s for s in range(1, 9)]
-    cp(T.off[:], T.lst[:, 0:128], base, ["off"])
+    for name, at in (("ea", 2), ("eb", 3)):
+        fill(view(name), 0.0)
+        ts(view(name, at, at + 512, 4), view("iot", 0, 128), pcol, None, A.is_equal)
+    for b in range(4):
+        at = 2 - 2 * (b // 2)
+        quant("e", 128 * b, 128, view(("ea", "eb")[b % 2], at, at + 512))
+    for t, c in enumerate((0.5, 0.5, -0.5, 1.0)):
+        fill(view("kp", t, 512, 4), c)
+        fill(view("kn", t, 512, 4), -c)
+    quant("k", 0, 128, view("kp"))
+    quant("k", 128, 128, view("kn"))
+    ts(view("tri"), view("iot", 0, 128), pcol, None, A.is_gt)
+    fill(view("gt"), 0.0)
+    fill(view("dcum"), 0.0)
+    fill(view("zer"), 0.0)
+    quant("v", 0, 128, view("vb"))
 
     peers = [T.cores[rank ^ h] for h in TURN]
     every = topo.engines(core, peers[0])
     far = topo.engines(core, peers[1])
-    near = [e for e in every if e not in far]
-    ways = [near, far[:len(far) // 2], far[len(far) // 2:]]
+    ways = [every, far[:len(far) // 2], far[len(far) // 2:]]
     aw, au = ["aw0", "aw1", "aw2"], ["au0", "au1", "au2"]
+    remote = []
 
     def bits(es):
         return sum(1 << e for e in es)
@@ -191,405 +310,228 @@ def rank_program(g, core, T, topo):
         a = topo.addr(c)
         return DstId(rid=a[0], pnc=a[1])
 
-    def send(src, lands, which, sems, r):
+    def whole(name):
+        return T[name][:].bitcast(dt.uint8) if name[0] == "q" else T[name][:]
+
+    def send(src, land, sems):
         tr = [RemoteDMATransfer(dst_ids=[dst(peers[i])], dma_engine_mask=bits(ways[i]), remote_sem=T.sem[sems[i]],
-                                src=src, dst=lands[i]) for i in which]
-        op("g", lambda: g.remote_dma_fused(tr, local_sem=T.sem.sent), r, (), "sent", sum(len(ways[i]) for i in which), inc=False)
+                                src=whole(src), dst=whole(land % i)) for i in (1, 2)]
+        remote.append(op({"g": 400}, lambda q: g.remote_dma_fused(tr, local_sem=T.sem.sent), [view(src)], [view(land % i) for i in (1, 2)],
+                         "sent", len(far), inc=False, late=OPT["far"], after=remote[-1:]))
 
-    def write(out, src, i, es, r, sems):
+    def write(src, land, i, es, sems, late):
         a = topo.addr(peers[i])
-        op("g", lambda: g.remote_dma(out, src, T.sem[sems[i]], T.sem.sent, a[1], a[0], bits(es)), r, (), "sent", len(es), inc=False)
+        remote.append(op({"g": 400}, lambda q: g.remote_dma(whole(land % i), whole(src), T.sem[sems[i]], T.sem.sent, a[1], a[0], bits(es)),
+                         [view(src)], [view(land % i)], "sent", len(es), inc=False, late=late, after=remote[-1:]))
 
-    write(T.sw0[:], T.sw[:], 0, every, ["sw"], aw)
-    write(T.qw0[:].bitcast(dt.uint8), T.qw[:].bitcast(dt.uint8), 0, every, ["qw"], aw)
-    arrives("W0", "aw0", 2 * len(every))
-    arrives("W1", "aw1", len(ways[1]) + len(far))
-    arrives("W2", "aw2", len(ways[2]) + len(far))
+    arrivals = {}
     for i in range(3):
-        arrives("U%d" % i, au[i], 2 * len(ways[i] if i else every))
+        for name in ("qw%d", "sw%d"):
+            arrivals[name % i] = (aw[i], len(ways[i]) + len(far if i else every))
+        for name in ("qu%d", "su%d"):
+            arrivals[name % i] = (au[i], 2 * len(ways[i]))
 
-    def lists(s):
-        return T.off[:, 16 * s:16 * s + 16]
+    quant("u", 0, 128, view("ub"))
+    op({"v": 50 + UP * OPT["gather"]},
+       lambda q: V.tensor_copy(T.qup[:].bitcast(dt.uint32), T.qu[:].bitcast(dt.uint32).indirect(T.uoff[:, 0:12])),
+       [view("qu"), view("uoff", 0, 12)], [view("qup")])
+    move("va", view("sup"), by(view("su"), view("uoff", 0, 12)))
+    write("sw", "sw%d", 0, every, aw, OPT["hop"])
+    write("qw", "qw%d", 0, every, aw, OPT["hop"] + 600)
+    write("qup", "qu%d", 0, every, au, OPT["hop"])
+    write("sup", "su%d", 0, every, au, OPT["hop"])
+    write("qw", "qw%d", 1, far, aw, OPT["far"])
+    send("sw", "sw%d", aw)
+    send("qup", "qu%d", au)
+    send("sup", "su%d", au)
+    write("qw", "qw%d", 2, far, aw, OPT["far"])
 
-    act(T.rho[:], T.iot[:, 0:C].indirect(lists(0)), ["iot", "off"], ["rho"])
-    cp(T.r5[:], T.iot[:, 0:C].indirect(lists(5)), ["iot", "off"], ["r5"])
-    ts(c16, icol, 15.0, 256.0, A.is_lt, A.mult, ["icol"], ["c16"])
-    act(T.ta[:], T.rho[:].indirect(lists(1)), ["rho", "off"], ["ta"])
-    cp(T.rb[:], T.r5[:].indirect(lists(6)), ["r5", "off"], ["rb"])
-    ts(tmp, icol, 7.0, 16.0, A.min, A.mult, ["icol"], ["tmp"])
-    act(T.tb[:], T.ta[:].indirect(lists(2)), ["ta", "off"], ["tb"])
-    cp(T.ra[:], T.rb[:].indirect(lists(7)), ["rb", "off"], ["ra"])
-    fill(T.uoff[:, 1:10], 0, ["uoff1"])
-    ts(T.uoff[:, 0:1], tmp, 1.0, None, A.add, None, ["tmp"], ["uoff0"])
-    scan(T.sa[:], T.m16[:], T.ra[:], ["m16", "ra"], ["sa0", "sa1"])
-    quant("u", T.ub[:], ["ub"])
-    ts(T.rl[:], T.sa[:, 15:C:16], c16, None, A.add, None, ["sa0", "sa1", "c16"], ["rl"])
-    act(T.ta[:], T.tb[:].indirect(lists(3)), ["tb", "off"], ["ta"])
-    act(T.tb[:], T.ta[:].indirect(lists(4)), ["ta", "off"], ["tb"])
-    cp(T.qup[:].bitcast(dt.uint32), T.qu[:].bitcast(dt.uint32).indirect(T.uoff[:, 0:9]), ["qu", "uoff0", "uoff1"], ["qup"])
-    cp(T.sup[:], T.su[:].indirect(T.uoff[:, 0:9]), ["qu", "uoff0", "uoff1"], ["sup"])
-    write(T.qu0[:].bitcast(dt.uint8), T.qup[:].bitcast(dt.uint8), 0, every, ["qup"], au)
-    write(T.su0[:], T.sup[:], 0, every, ["sup"], au)
-    write(T.qw1[:].bitcast(dt.uint8), T.qw[:].bitcast(dt.uint8), 1, far, ["qw"], aw)
-    send(T.sw[:], [T["sw%d" % i][:] for i in range(3)], (1, 2), aw, ["sw"])
-    send(T.qup[:].bitcast(dt.uint8), [T["qu%d" % i][:].bitcast(dt.uint8) for i in range(3)], (1, 2), au, ["qup"])
-    send(T.sup[:], [T["su%d" % i][:] for i in range(3)], (1, 2), au, ["sup"])
-    write(T.qw2[:].bitcast(dt.uint8), T.qw[:].bitcast(dt.uint8), 2, far, ["qw"], aw)
-    op("g", lambda: g.iota(T.iot[:, C:4 * C], [[0, 3], [1, C]], 0, 0, allow_small_or_imprecise_dtypes=True), (), ["iot2"])
-    act(T.m4[:], T.msm[:, 16:32].indirect(T.moff[:]), ["msm", "moff"], ["m4"])
-    act(T.crow[:], T.tb[:].indirect(T.rl[:]), ["tb", "rl"], ["cr0", "cr1"])
-    ts(tmq, qcol, 3.0, 1024.0, A.is_lt, A.mult, ["icol"], ["tmq"])
-    ts(c4, tmq, tcol, None, A.add, None, ["tmq", "icol"], ["c4"])
+    def lists(m):
+        return view("off", 16 * m, 16 * m + 16)
 
-    def constants():
-        for b in range(8):
-            fill(T.et[:, 256 * b:256 * b + 256], 0.0, ["z%d" % b])
-        for t, c in enumerate((1.0, 0.5, -0.5, 1.0)):
-            fill(T.wt[:, t:512:4], c, ["k%d" % t])
-        fill(T.wt[:, 512:768], -1.0, ["k4"])
-        fill(T.wt[:, 768:1024], -1.0, ["k5"])
-        scan(T.sa[:], T.m16[:], T.crow[:], ["m16", "cr0", "cr1"], ["sa0", "sa1"])
-        for b in range(4):
-            ts(T.et[:, 512 * b + b:512 * b + 512:4], T.iot[:, 0:128], pcol, None, A.is_equal, None, ["iot", "pcol"],
-               ["z%d" % (2 * b), "z%d" % (2 * b + 1)])
-            quant_half("e", T.et, b, ["z%d" % (2 * b), "z%d" % (2 * b + 1)])
-        ts(T.el[:, 0:16], T.sa[:, 15:C:16], c16, None, A.add, None, ["sa0", "sa1", "c16"], ["el0"])
-        quant_half("k", T.wt, 0, ["k0", "k1", "k2", "k3"])
-        quant_half("k", T.wt, 1, ["k4", "k5"])
-        ts(T.tri[:], T.iot[:, 0:128], pcol, None, A.is_gt, None, ["iot", "pcol"], ["tri"])
-        ts(T.iq[:, 8:18], T.ip[:, 0:10], 4, None, A.arith_shift_right, None, ["ip0"], ["iq8"])
-        ts(T.iq[:, 20:27], T.iq[:, 9:16], 1.0, 2.0, A.add, A.mult, ["iq8"], ["iq20"])
-        ts(T.doff[:, 8:9], T.iq[:, 8:9], 2.0, None, A.mult, None, ["iq8"], ["aoff"])
-        fill(T.doff[:, 7:8], 0, ["doff7"])
-        ts(T.doff[:, 0:7], T.iq[:, 20:27], 1.0, None, A.max, None, ["iq20"], ["doff0"])
-        quant("v", T.vb[:], ["vb"])
+    for a, b in ((8, 9), (4, 8), (0, 4)):
+        move("v", view("off", 16 * a, 16 * b), by(view("lst"), view("goff", a, b)))
+    mid = lambda name: view(name, C, 2 * C)
+    for q, rows, m in (("a", (view("iot"), mid("s3"), view("ta"), view("tb"), view("tl", 0, C)), 8),
+                       ("v", (view("iot"), mid("r3"), view("ra"), view("rb"), view("rc")), 4)):
+        for s in range(4):
+            move(q, rows[s + 1], by(rows[s], lists(m - s)))
+    to_list("jl", view("rc"), "sr", c16)
+    halves("va", "erow", view("tl", 0, C), "jl")
+    for k, name in enumerate(("s3", "r3")):
+        for a in (0, 2 * C):
+            dma("s", ap(view(name, a, a + C)), ap(mid(name)), [mid(name)], [view(name, a, a + C)], "tripled%d" % k, 32)
+    move("va", view("lj", 0, 64), view("off", 0, 64))
+    move("va"[0], view("lj", 80, 128), view("off", 80, 128))
+    fill(view("lj", 64, 80), 0)
 
-    fkeys = ["f0", "f1", "f2", "f3"]
-    nothing = lambda: None
+    def path_list():
+        scan(view("se2"), view("m16"), view("erow"))
+        ts(view("eli"), view("se2", 15, C, 16), c16, None, A.add)
 
-    def gather(first, row, keys, name, gap=(nothing, nothing)):
-        def scan4(h):
-            scan(T.sb[:, 128 * h:128 * h + 128], T.m4[:, 0:128], row[:, 128 * h:128 * h + 128], ["m4", keys[h]], ["sb%d" % h])
+    def gather(first, row, name):
+        for h in range(2):
+            scan(view("sb", 128 * h, 128 * h + 128), view("m4"), view(row, 128 * h, 128 * h + 128))
+            ts(view("l4", 32 * h, 32 * h + 32), view("sb", 128 * h + 3, 128 * h + 128, 4), 4.0, c4, A.mult, A.add)
+        cuts = (0,) + OPT["cuts"] + (64,)
+        for k in range(len(cuts) - 1):
+            a, b = cuts[k], cuts[k + 1]
+            move(OPT["big"][k], view("ft", 16 * a, 16 * b), by(view("xb" if first else "st"), view("l4", a, b)), None if first else 0.5)
+        for h in range(2):
+            quant(name, 128 * h, 128, view("ft", 512 * h, 512 * h + 512))
 
-        def list4(h):
-            ts(T.l4[:, 32 * h:32 * h + 32], T.sb[:, 128 * h + 3:128 * h + 128:4], 4.0, c4, A.mult, A.add, ["sb%d" % h, "c4"], ["l4%d" % h])
-
-        def part(q, a, b, key):
-            win, r = (T.xb, ["xb"]) if first else (T.st, ["s%d%d" % (x, y) for x in range(4) for y in range(2)])
-            move(q, T.ft[:, 16 * a:16 * b], win[:].indirect(T.l4[:, a:b]), r + ["l4%d" % (a // 32)], [key], None if first else 0.5)
-        cut = OPT["cut"]
-        scan4(0)
-        scan4(1)
-        list4(0)
-        list4(1)
-        part("a", 16, 32, "f1")
-        part("v", 0, 16, "f0")
-        part("a", cut, 64, "f3")
-        gap[0]()
-        quant_half(name, T.ft, 0, ["f0", "f1"])
-        part("v", 32, cut, "f2")
-        gap[1]()
-        quant_half(name, T.ft, 1, ["f2", "f3"])
-
-    def cast(q, h, k):
-        move(q, T.ht[:, 512 * h + k:512 * h + 512:4], bank(4 * h + k, 0, 128), ["P%d" % (4 * h + k)], ["h%d%d" % (h, k)], 0.0078125)
-
-    def score(h):
-        cp(T.scol[:, 4 * h:4 * h + 1], bank(h, 16, 17), ["P%d" % h], ["sc%d" % h])
-
-    def flag(h):
-        ts(T.gt[:, 8 + 3 * h:72 + 3 * h:8], bank(h, 0, 8), 0.0, None, A.is_gt, None, ["P%d" % h], ["g%d" % h])
-
-    def sc(h):
-        return T.scol[:, 4 * h:4 * h + 1]
-
-    def equal(h):
-        ts(T.ct[:, 512 * h + 2:512 * h + 512:4], bank(2 + h, 0, 128), sc(h), None, A.is_equal, None, ["P%d" % (2 + h), "sc%d" % h], ["c2%d" % h])
-
-    def other(h):
-        ts(T.ct[:, 512 * h:512 * h + 512:4], bank(2 + h, 0, 128), sc(1 - h), None, A.is_le if h else A.is_lt, None,
-           ["P%d" % (2 + h), "sc%d" % (1 - h)], ["c0%d" % h])
-
-    def sign(h, k):
-        op("a", lambda: S.activation(T.ct[:, 512 * h + 1:512 * h + 512:4], bank(k, 0, 128), SIGN, bias=sc(h), scale=-1.0),
-           ["P%d" % k, "sc%d" % h], ["c1%d" % h])
-
-    def other_sign(h, k):
-        op("a", lambda: S.activation(T.sg2[:, 128 * h:128 * h + 128], bank(k, 0, 128), SIGN, bias=sc(1 - h), scale=-1.0),
-           ["P%d" % k, "sc%d" % (1 - h)], ["sg%d" % h])
-
-    def other_side(h):
-        op("a", lambda: S.activation(T.ct[:, 512 * h:512 * h + 512:4], T.sg2[:, 128 * h:128 * h + 128], SIGN, bias=0.5 if h else -0.5),
-           ["sg%d" % h], ["c0%d" % h])
-
-    def ties(h):
-        op("v", lambda: V.tensor_tensor_scan(T.ct[:, 512 * h + 3:512 * h + 512:4], T.tri[:], T.ct[:, 512 * h + 2:512 * h + 512:4],
-                                             0.0, A.max, A.mult), ["tri", "c2%d" % h], ["c3%d" % h])
-
-    ckeys = ["c%d%d" % (t, h) for t in range(4) for h in range(2)]
+    COLS, ROWS, SIGNS, COUNTS, RANKS, UNPACK = (0, 4), (1, 5), (2, 6), 3, (7, 4), (0, 1, 2, 5)
 
     def layer(i):
-        u, uk = "u%d" % i, "U%d" % i
-        if i == 0:
-            constants()
+        u = "u%d" % i
         for h in range(2):
             for k in range(4):
-                mm(4 * h + k, 128, "w%d" % i, 128 * k, "f", 128 * h, ["W%d" % i, "qf%d" % h])
-        for k, q in enumerate("aaav"):
-            cast(q, 0, k)
-        cast("v", 1, 0)
-        quant_half("h", T.ht, 0, ["h00", "h01", "h02", "h03"])
-        mm(0, 128, "h", 0, u, 0, ["qh0", uk])
-        mm(2, 128, u, 16, "h", 0, ["qh0", uk])
-        cast("a", 1, 1)
-        cast("v", 1, 2)
-        cast("a", 1, 3)
-        quant_half("h", T.ht, 1, ["h10", "h11", "h12", "h13"])
-        mm(1, 128, "h", 128, u, 0, ["qh1", uk])
-        mm(3, 128, u, 16, "h", 128, ["qh1", uk])
-        mm(7, 128, u, 16, "h", 128, ["qh1", uk])
-        score(0)
-        flag(0)
-        equal(0)
-        sign(0, 2)
-
-    def counts(k):
-        def both():
-            PE.matmul_mx(bank(k, 0, 128), T.qk[:, 0:128], T.sk[:, 0:128], T.qg[:, 2:130], T.sg[:, 2:130], True, False)
-            return PE.matmul_mx(bank(k, 0, 128), T.qk[:, 128:256], T.sk[:, 128:256], T.qg[:, 0:128], T.sg[:, 0:128], False, True)
-        op("t", both, ["qk0", "qk1", "qg"], ["P%d" % k])
-
-    def steps_add(k):
-        op("v", lambda: V.tensor_tensor(T.dcum[:], bank(k, 0, 32), T.dcum[:], A.add), ["P%d" % k, "dcum"], ["dcum"])
-
-    def steps_sum():
-        op("v", lambda: V.tensor_tensor_scan(T.acum[:], T.dcum[:], T.zer[:], 0.0, A.add, A.add), ["dcum", "zer"], ["acum"])
-
-    def rank_list(plus, gap):
-        scan(T.sf32[:], T.m16[:], bank(1), ["m16", "P1"], ["sf32"])
-        gap()
-        ts(T.rl[:], T.sf32[:, 15:C:16], c16, plus, A.add, A.add, ["sf32", "c16"], ["rl"])
-        cp(T.orow[:].indirect(T.rl[:]), T.iot[:, 0:C], ["iot", "rl"], ["orow"])
-
-    def unpack(b):
-        mm(4 + b, C, "e", 128 * b, "h", 0, ["qe%d" % b, "qh0", "qh1"])
-
-    def add(b):
+                mm(4 * h + k, 128, ("w%d" % i, 128 * k, "f", 128 * h))
         for h in range(2):
-            op("v", lambda h=h: V.tensor_tensor(T.st[:, 512 * h + b:512 * h + 512:4], bank(4 + b, 128 * h, 128 * h + 128),
-                                                T.ft[:, 512 * h + b:512 * h + 512:4], A.add),
-               ["P%d" % (4 + b)] + fkeys[2 * h:2 * h + 2], ["s%d%d" % (b, h)])
-
-    def swap(q, h):
-        move(q, T.oswp[:, h:C:2], T.orow[:, 1 - h:C:2], ["orow"], ["osw%d" % h])
-
-    def partners(q):
-        move(q, T.mrow[:], T.oswp[:].indirect(T.rl[:]), ["osw0", "osw1", "rl"], ["mrow"])
-
-    def turn(i):
-        offact = OPT["offact"]
-        flag(1)
-        score(1)
-        quant("g", T.gt[:], ["g0", "g1"])
-        counts(0)
-        equal(1)
-        ties(0)
-        if offact:
-            other_sign(0, 2)
-            other_sign(1, 7)
-            sign(1, 7)
-            other_side(0)
-            other_side(1)
-        else:
-            sign(1, 7)
-            other(0)
-            other(1)
-        for b in range(4):
-            unpack(b)
-        ties(1)
-        steps_add(0)
-        cuts = ((0, 2), (4, 8), (2, 4))
-
-        def turned(x):
-            a, b = cuts[x]
-            op("v", lambda: V.tensor_tensor(T.li[:, 16 * a:16 * b], T.dcum[:].indirect(T.doff[:, a:b]), T.lst[:, 16 * a + 16:16 * b + 16], A.add),
-               ["dcum", "doff0", "doff7"] + base, ["li_%d" % x])
-
-        def wrapped(x):
-            a, b = cuts[x]
-            ts(T.lj[:, 16 * a:16 * b], T.li[:, 16 * a:16 * b], 255, None, A.bitwise_and, None, ["li_%d" % x], ["lj%d" % x])
-
-        def offsets(x):
-            a, b = cuts[x]
-            cp(T.off[:, 16 * a:16 * b], T.lj[:, 16 * a:16 * b], ["lj%d" % x], [("off0", "off", "off2")[x]])
-
-        def ranks():
-            mm(1, C, "k", 0, "c", 0, ["qk0", "qc0", "qc1"])
-
-        def codes(h):
-            quant_half("c", T.ct, h, ["c%d%d" % (t, h) for t in range(4)])
-        if OPT["qc"] == 0:
-            codes(0)
-        turned(0)
-        if OPT["qc"] == 1:
-            codes(0)
-        else:
-            steps_sum()
-        wrapped(0)
-        if OPT["qc"] < 2:
-            codes(1)
-            ranks()
-        offsets(0)
-        if OPT["qc"] == 2:
-            codes(0)
-            codes(1)
-            ranks()
-        turned(1)
-        if OPT["qc"] == 1:
-            steps_sum()
-        wrapped(1)
-        cp(T.ei[:], T.acum[:].indirect(T.doff[:, 8:9]), ["acum", "aoff"], ["ei"])
-        offsets(1)
-        if OPT["qc"] == 3:
-            codes(0)
-            codes(1)
-            ranks()
-
-        turned(2)
-        wrapped(2)
-        offsets(2)
-
-        def step(src, to, s):
-            act(T[to][:, 0:C], T[src][:, 0:C].indirect(lists(s)), [src, "off0" if s < 2 else "off2" if s < 4 else "off"], [to])
-        cp(T.di[:], T.dcum[:].indirect(T.doff[:, 4:5]), ["dcum", "doff0"], ["di"])
-        ts(T.dj[:, 0:1], T.di[:, 0:1], 255, None, A.bitwise_and, None, ["di"], ["dj"])
-        ts(T.acol[:, 8:9], T.dj[:, 0:1], c16, None, A.add, None, ["dj", "c16"], ["dcol"])
-        step("rho", "ta", 0)
-        step("r5", "rb", 5)
-        step("ta", "tb", 1)
-        step("rb", "ra", 6)
-        step("tb", "ta", 2)
-        step("ra", "rb", 7)
-        step("ta", "tl", 3)
-        move(OPT["dbl"], T.tl[:, C:2 * C], T.tl[:, 0:C], ["tl"], ["tl2"])
-        scan(T.sr[:], T.m16[:], T.rb[:], ["m16", "rb"], ["sr"])
-        ts(T.ml[:], T.sr[:, 15:C:16], T.acol[:, 8:9], None, A.add, None, ["sr", "dcol"], ["ml"])
+            for k in range(4):
+                move(OPT["casts"][4 * h + k], view("ht", 512 * h + k, 512 * h + 512, 4), bank(4 * h + k, 0, 128), 0.0078125)
+            quant("h", 128 * h, 128, view("ht", 512 * h, 512 * h + 512))
         for h in range(2):
-            move(OPT["e"][h], T.erow[:, 128 * h:128 * h + 128], T.tl[:].indirect(T.ml[:, 8 * h:8 * h + 8]), ["tl", "tl2", "ml"], ["er%d" % h])
-        rank_list(64.0, lambda: ts(T.ej[:, 0:1], T.ei[:, 0:1], 255, None, A.bitwise_and, None, ["ei"], ["ej"]))
-        ts(T.acol[:, 0:1], T.ej[:, 0:1], -1.0, c16, A.mult, A.add, ["ej", "c16"], ["acol"])
-        swap("v", 0)
-        swap(OPT["swap"], 1)
-        partners(OPT["gm"])
-        for b in range(4):
-            add(b)
+            mm(COLS[h], 128, ("h", 128 * h, u, 0))
+            mm(ROWS[h], 128, (u, 64, "h", 128 * h))
+            mm(SIGNS[h], 128, (u, 64, "h", 128 * h))
+            move("v", col("scol", 4 * h), bank(COLS[h], 64, 65))
+            ts(view("gt", 32 + 3 * h, 288, 4), bank(COLS[h], 0, 64), 0.0, 2.0 - h, A.is_gt, A.mult)
+        slot = lambda h, t: view("ct", 512 * h + t, 512 * h + 512, 4)
         for h in range(2):
-            scan(T.sa[:, 128 * h:128 * h + 128], T.m16[:, 0:128], T.erow[:, 128 * h:128 * h + 128], ["m16", "er%d" % h], ["sa%d" % h])
-            ts(T.ol[:, 8 * h:8 * h + 8], T.sa[:, 128 * h + 15:128 * h + 128:16], T.acol[:, 0:1], 256.0, A.add, A.add, ["sa%d" % h, "acol"], ["ol%d" % h])
-        if OPT["back"]:
-            back(i)
-            move(OPT["dbl"], T.come[:, C:2 * C], T.come[:, 0:C], ["come"], ["come2"])
+            ts(slot(h, 2), bank(ROWS[h], 0, 128), col("scol", 4 * h), None, A.is_equal)
+            scan(slot(h, 3), view("tri"), slot(h, 2), A.max, A.mult)
+            sign(slot(h, 1), bank(SIGNS[h], 0, 128), col("scol", 4 * h), -1.0)
+        for h in range(2):
+            if h and OPT["other"] == "a":
+                sign(view("sg2", 0, 128), bank(SIGNS[h], 0, 128), col("scol", 0), -1.0)
+                op({"a": length("a", slot(h, 0))}, lambda q: S.activation(ap(slot(1, 0)), ap(view("sg2", 0, 128)), SIGN, bias=0.5), [view("sg2", 0, 128)], [slot(1, 0)])
+            else:
+                ts(slot(h, 0), bank(ROWS[h], 0, 128), col("scol", 4 - 4 * h), 2.0, A.is_le if h else A.is_lt, A.mult)
+        quant("g", 0, 136, view("gt"))
+        mm(COUNTS, 128, ("k", 0, "g", 8), ("k", 128, "g", 0))
+        for h in range(2):
+            quant("c", 128 * h, 128, view("ct", 512 * h, 512 * h + 512))
+
+    def sort():
+        if OPT["rhalf"]:
             for h in range(2):
-                move(OPT["b"][h], T.brow[:, 128 * h:128 * h + 128], T.come[:].indirect(T.ol[:, 8 * h:8 * h + 8]), ["come", "come2", "ol%d" % h], ["br%d" % h])
-            through(T.brow, ["br0", "br1"])
-            for f in path_list(i + 1):
-                f()
-        else:
-            for f in path_list(i + 1):
-                f()
-            cp(T.come[:, 0:C].indirect(T.el[:, 16 * i:16 * i + 16]), T.mrow[:], ["mrow", "el%d" % i], ["come"])
+                mm(RANKS[h], 128, ("k", 0, "c", 128 * h))
+                to_list("rl", bank(RANKS[h], 0, 128), "sf32", short[h], 128 * h, 128 * h + 128)
             for h in range(2):
-                e = 16 * (i + 1) + 8 * h
-                move("va"[h], T.crow[:, 128 * h:128 * h + 128], T.come[:, 0:C].indirect(T.el[:, e:e + 8]), ["come", "el%d" % (i + 1)], ["cr%d" % h])
-
-    def back(i):
-        cp(T.come[:, 0:C].indirect(T.el[:, 16 * i:16 * i + 16]), T.iot[:, 0:C], ["iot", "el%d" % i], ["come"])
-
-    def through(row, keys):
-        for h in range(2):
-            scan(T.sc2[:, 128 * h:128 * h + 128], T.m16[:, 0:128], row[:, 128 * h:128 * h + 128], ["m16", keys[h]], ["s2%d" % h])
-            ts(T.bl[:, 8 * h:8 * h + 8], T.sc2[:, 128 * h + 15:128 * h + 128:16], c16, None, A.add, None, ["s2%d" % h, "c16"], ["bl%d" % h])
-            move("va"[h], T.crow[:, 128 * h:128 * h + 128], T.mrow[:].indirect(T.bl[:, 8 * h:8 * h + 8]), ["mrow", "bl%d" % h], ["cr%d" % h])
-
-    def path_list(i):
-        def first():
-            cp(T.ei[:], T.ol[:, 0:16], ["ol0", "ol1"], ["ei"])
-
-        def second():
-            ts(T.ej[:], T.ei[:], 255, None, A.bitwise_and, None, ["ei"], ["ej"])
-
-        def third():
-            cp(T.el[:, 16 * i:16 * i + 16], T.ej[:], ["ej"], ["el%d" % i])
-        return first, second, third
-
-    def last(i):
-        score(1)
-        sign(1, 7)
-        equal(1)
-        other(1)
-        other(0)
-        for b in range(4):
-            unpack(b)
-        ties(0)
-        ties(1)
-        flag(1)
-        for h in range(2):
-            quant_half("c", T.ct, h, ["c%d%d" % (t, h) for t in range(4)])
-        mm(1, C, "k", 0, "c", 0, ["qk0", "qc0", "qc1"])
-        quant("g", T.gt[:], ["g0", "g1"])
-        counts(0)
-        add(0)
-        rank_list(64.0, (lambda: add(3)) if OPT["fin"] else (lambda: steps_add(0)))
-        if OPT["fin"]:
-            steps_add(0)
-        swap("v", 0)
-        swap("a", 1)
-        partners("a")
-        steps_sum()
-        add(1)
-        cp(T.acol[:], T.acum[:].indirect(T.doff[:, 8:9]), ["acum", "aoff"], ["acol"])
-        add(2)
-        ts(T.ol[:, 0:16], T.ej[:], T.acol[:, 0:1], None, A.add, None, ["ej", "acol"], ["ol0", "ol1"])
-        act(T.optab[:], T.iot[:].indirect(T.ol[:, 0:16]), ["iot", "iot2", "ol0", "ol1"], ["optab"])
-        if OPT["lastback"]:
-            back(i)
-            through(T.come, ["come", "come"])
-            row, keys = T.crow, ["cr0", "cr1"]
+                move("v", by(view("orow"), view("rl", 8 * h, 8 * h + 8)), view("iot", 128 * h, 128 * h + 128))
         else:
-            cp(T.come[:, 0:C].indirect(T.el[:, 16 * i:16 * i + 16]), T.mrow[:], ["mrow", "el%d" % i], ["come"])
-            row, keys = T.come, ["come", "come"]
-        add(3)
-        gather(False, row, keys, "x",
-               (lambda: scan(T.sa[:], T.m16[:], row[:, 0:C], ["m16"] + keys, ["sa0", "sa1"]),
-                lambda: ts(T.ol[:, 16:32], T.sa[:, 15:C:16], c16, None, A.add, None, ["sa0", "sa1", "c16"], ["ol2"])))
-        mm(2, 128, "v", 0, "x", 0, ["qv", "qx0"])
-        mm(3, 128, "v", 0, "x", 128, ["qv", "qx1"])
-        act(T.yb[:, 0:128], bank(2, 0, 128), ["P2"], ["y0"])
-        cp(T.yb[:, 128:C], bank(3, 0, 128), ["P3"], ["y1"])
-        act(T.oprow[:], T.optab[:].indirect(T.ol[:, 16:32]), ["optab", "ol2"], ["oprow"])
+            mm(RANKS[0], C, ("k", 0, "c", 0))
+            scan(view("sf32"), view("m16"), bank(RANKS[0]))
+            for a, b in ((0, C),) if short[0] == short[1] else ((0, 128), (128, C)):
+                ts(view("rl", a // 16, b // 16), view("sf32", a + 15, b, 16), short[a // 128], None, A.add)
+            move("v", by(view("orow"), view("rl")), view("iot"))
+        for h in range(2):
+            move(OPT["swap"][h], view("oswp", h, C, 2), view("orow", 1 - h, C, 2))
+        halves(OPT["m"], "mrow", view("oswp"), "rl")
 
-        def scales(q, k):
-            op(q, lambda: Q[q].dma_start(T.osc[4 * k:4 * k + 4, :], T.sx[32 * k:32 * k + 4, :]), ["qx0", "qx1"], (), "out" + q, 16)
-        op("s", lambda: g.sync.dma_start(T.y[:, 0:128], T.yb[:, 0:128]), ["y0"], (), "outs", 16)
-        op("s", lambda: g.sync.dma_start(T.oc[:], T.qx[:].bitcast(dt.uint8)), ["qx0", "qx1"], (), "outs", 16)
-        scales("s", 0)
-        scales("s", 1)
-        op("s", lambda: g.sync.dma_start(T.y[:, 128:C], T.yb[:, 128:C]), ["y1"], (), "outs", 16)
-        op("a", lambda: S.dma_start(T.op[:], T.oprow[0:128:16, :]), ["oprow"], (), "outa", 16)
-        scales("a", 2)
-        scales("a", 3)
+    def unpack():
+        for b in range(4):
+            mm(UNPACK[b], C, ("e", 128 * b, "h", 0))
+            for h in range(2):
+                tt(view("st", 512 * h + b, 512 * h + 512, 4), bank(UNPACK[b], 128 * h, 128 * h + 128), view("ft", 512 * h + b, 512 * h + 512, 4), A.add)
+
+    def steps():
+        tt(view("dcum", 0, 9), bank(COUNTS, 0, 72, 8), view("dcum", 0, 9), A.add)
+
+    def turn():
+        ts(view("o6"), view("lj", 112, 128), bank(COUNTS, 56, 57), 256.0, A.add, A.add)
+        ts(view("o2"), view("lj", 48, 64), bank(COUNTS, 24, 25), 256.0, A.add, A.add)
+        for e in range(2):
+            tt(view("li", e, 128, 2), bank(COUNTS, 0, 64), view("lj", e, 128, 2), A.add)
+        ts(view("li", 128, 144), view("eli"), bank(COUNTS, 64, 65), None, A.subtract)
+        steps()
+        ts(view("lj"), view("li"), 255, None, A.bitwise_and)
+        move("v", view("off"), view("lj"))
+        ts(col("dcol", 0), col("lj", 64), c16, None, A.add)
+        left = ((view("s3"), view("o6")), (view("ta"), lists(6)), (view("tb"), lists(5)))
+        for s, to in enumerate((view("ta"), view("tb"), view("tl", 0, C))):
+            move(OPT["left"][s], to, by(*left[s]))
+        right = ((view("r3"), view("o2")), (view("ra"), lists(2)), (view("rb"), lists(1)), (view("ra"), lists(0)))
+        for s, to in enumerate((view("ra"), view("rb"), view("ra"), view("rc"))):
+            move(OPT["right"][s], to, by(*right[s]))
+        move(OPT["dbl"], view("tl", C, 2 * C), view("tl", 0, C))
+        to_list("jl", view("rc"), "sr", col("dcol", 0))
+        halves(OPT["join"], "erow", view("tl"), "jl")
+        for h in range(2):
+            to_list("el", view("erow", 128 * h, 128 * h + 128), "se2", c16, 128 * h, 128 * h + 128)
+        sort()
+        unpack()
+        move("v", by(view("me"), lists(8)), view("mrow"))
+        halves(OPT["crow"], "crow", view("me"), "el")
+        move("v", view("eli"), view("el"))
+
+    def last():
+        ts(view("ei"), view("eli"), col("dcum", 8), None, A.add)
+        ts(view("ej"), view("ei"), 255, None, A.bitwise_and)
+        move("v", view("ul"), view("ej"))
+        move("v", by(view("einv"), view("ul")), view("iot"))
+        to_list("il", view("einv"), "sa", c16)
+        steps()
+        scan(view("acum", 0, 9), view("dcum", 0, 9), view("zer", 0, 9), A.add, A.add)
+        move("v", view("acol"), by(view("acum", 0, 9), col("aoff", 0)))
+        ts(view("ek"), view("ej"), col("acol", 0), None, A.add)
+        ts(view("em"), view("ek"), 255, None, A.bitwise_and)
+        move("v", view("jl"), view("em"))
+        move("a", view("optab"), by(view("iot"), view("jl")))
+        sort()
+        unpack()
+        halves(OPT["crow"], "crow", view("mrow"), "il")
+        gather(False, "crow", "x")
+        to_list("cl", view("crow"), "sa", c16)
+        move("a", view("oprow"), by(view("optab"), view("cl")))
+        for h in range(2):
+            mm(3 + 4 * h, 128, ("v", 0, "x", 128 * h))
+            move("av"[h], view("yb", 128 * h, 128 * h + 128), bank(3 + 4 * h, 0, 128))
+        dma("s", T.oc[:], T.qx[:].bitcast(dt.uint8), [view("qx")], (), "outs")
+        for k in range(4):
+            dma("sa"[k // 2], T.osc[4 * k:4 * k + 4, :], T.sx[32 * k:32 * k + 4, :], [view("sx")], (), "out" + "sa"[k // 2])
+        for h in range(2):
+            dma("s", T.y[:, 128 * h:128 * h + 128], T.yb[:, 128 * h:128 * h + 128], [view("yb", 128 * h, 128 * h + 128)], (), "outs")
+        dma("a", T.op[:], T.oprow[0:128:16, :], [view("oprow")], (), "outa")
 
     for i in range(3):
-        gather(i == 0, T.crow, ["cr0", "cr1"], "f")
+        gather(i == 0, "crow" if i else "erow", "f")
+        if i == 0:
+            path_list()
         layer(i)
         if i < 2:
-            turn(i)
+            turn()
         else:
-            last(i)
+            last()
 
-    OPT["calls"] = calls
-    for k in (OPT["order"] or range(len(calls))):
-        emit(*calls[k])
+    if "order" not in PLAN:
+        PLAN["order"] = plan(calls)
+    known = {q: {} for q in Q}
+    count = {}
+    touched = {}
+    for name, (sem, n) in arrivals.items():
+        count[sem] = n
+        touched[name] = [(marks(view(name)), True, (sem, n, {sem: n}, 0, "x"))]
+    for serial, (k, q) in enumerate(PLAN["order"]):
+        c = calls[k]
+        mine = [(x, False) for x in c["r"]] + [(x, True) for x in c["w"] if c["inc"]]
+        evs = [ev for x, writes in mine for y, wrote, ev in touched.get(x[0], [])
+               if meet(x, y) and (writes or wrote or (x[0] == "ps" and ev[4] != q))]
+        for ev in sorted(evs, key=lambda e: -e[3]):
+            if known[q].get(ev[0], 0) < ev[1]:
+                Q[q].wait_ge(T.sem[ev[0]], ev[1])
+                for s, n in ev[2].items():
+                    known[q][s] = max(known[q].get(s, 0), n)
+        ins = c["make"](q)
+        sem = c["sem"] or "c" + q
+        count[sem] = count.get(sem, 0) + c["n"]
+        if c["inc"]:
+            ins.then_inc(T.sem[sem], c["n"])
+        clock = dict(known[q])
+        clock[sem] = c["upto"] or count[sem]
+        for x, writes in mine:
+            touched.setdefault(x[0], []).append((x, writes, (sem, clock[sem], clock, serial + 1, q)))
     for s in SEMAPHORES:
         if known["g"].get(s, 0) < count.get(s, 0):
             g.wait_ge(T.sem[s], count[s])

@@ -4,13 +4,20 @@ from concourse.mybir import dt, AluOpType, ActivationFunctionType
 A = AluOpType
 COPY = ActivationFunctionType.Copy
 SIGN = ActivationFunctionType.Sign
+IDENT = ActivationFunctionType.Identity
 C = 256
 TURN = [1, 2, 4]
 UP = 192
 X4 = "float8_e4m3fn_x4"
-OPT = {"wake": 150, "bias": 120, "gather": 1.2, "scatter": 2.6, "load": 2000, "hop": 2600, "far": 5000, "passes": 1,
+OPT = {"wake": 150, "bias": 120, "gather": 1.2, "scatter": 2.6, "load": 2000, "hop": 2600, "far": 5000, "passes": 6,
        "other": "a", "cuts": (16, 32, 42), "casts": "vavaavav", "big": "vava",
-       "join": "aa", "m": "va", "crow": "va", "left": "aaa", "right": "aaaa", "dbl": "v", "swap": "vv", "rhalf": 0}
+       "join": "aa", "m": "va", "crow": "va", "left": "aaa", "right": "aaaa", "dbl": "v", "swap": "vv", "rhalf": 0,
+       "skew": 0, "sends": (("sw", (0, "every")), ("qw", (0, "every")), ("qup", (0, "every")), ("sup", (0, "every")), ("qw", (1, "far")),
+                            ("sw", (1, "low"), (2, "high")), ("qup", (1, "far")), ("sup", (1, "low"), (2, "high")), ("qw", (2, "far")), ("qup", (2, "far"))),
+       "rule": "time", "ahead": 100, "rivals": 8, "grain": 60, "tie": 1, "mix": 1.0, "eg": 1, "holes": 3, "plate": 300,
+       "mend": 60, "reach": 2, "even": 0.05, "fold": 0, "fleft": "aaaa", "ml": "va",
+       "lift": 0, "direct": 1, "triple": "va", "last": "scatter", "pieces": 1, "loads": {"s": "SWuxv", "a": "01234567"}}
+OPT.update(wake=200, hop=3600, last="ranks", triple="va", skew=2, table=3000, near=4, far=3500, casts=("va",) * 8, dbl="va", fold=0, rule="mend", passes=1, mend=40, rhalf=1)
 
 
 def _pair(name, n):
@@ -21,12 +28,12 @@ def _of(dtype, n, *names):
     return {k: ("sbuf", [128, n], dtype) for k in names}
 
 
-SCRATCH = {"ps": ("psum", [128, 4096], "float32")}
+SCRATCH = {"ps": ("psum", [128, 4096], "float32"), "flat": ("dram", [1, 129 * C], "bfloat16"), "skew": ("sbuf", [128, C + 16], "bfloat16")}
 for _d in (_of("bfloat16", 4 * C, "xb", "ft", "ht", "ct"), _of("bfloat16", 512, "ub", "vb", "kp", "kn", "tl"), _of("float32", 4 * C, "st"),
            _of("bfloat16", 4 * 136, "gt"), _of("bfloat16", 528, "ea", "eb"), _of("bfloat16", 3 * C, "s3", "r3"),
            _of("int32", 144, "lst", "li", "lj"), _of("uint16", 144, "off"), _of("uint16", 16, "o6", "o2", "jl", "el", "rl", "cl", "ul", "il", "moff", "goff", "uoff"),
            _of("bfloat16", C, "iot", "ta", "tb", "ra", "rb", "rc", "m16", "sa", "sb", "sr", "se2", "sg2", "orow", "oswp", "mrow", "me", "crow",
-               "erow", "einv", "optab"),
+               "erow", "einv", "optab", "rho", "brow"), _of("uint16", 16, "o0", "bl"), _of("bfloat16", 2 * C, "ml"),
            _of("bfloat16", 128, "m4", "tri"), _of("float32", C, "sf32", "oprow", "yb"), _of("uint16", 64, "l4"),
            _of("int32", 16, "eli", "ei", "ej", "ek", "em", "ip", "iq"), _of("uint16", 2, "aoff"),
            _of("float32", 16, "col", "acol", "dcum", "acum", "zer", "scol", "dcol"), _of("float32", 32, "cc", "dm", "a1", "a2"),
@@ -36,7 +43,7 @@ for _n, _k in (("w", 512), ("w0", 512), ("w1", 512), ("w2", 512), ("u", 128), ("
                ("v", 128), ("f", C), ("h", C), ("c", C), ("g", 136), ("e", 512), ("k", C), ("x", C)):
     SCRATCH.update(_pair(_n, _k))
 
-SEMAPHORES = ["cv", "ca", "ct", "cg", "lp", "lws", "lwc", "lu", "lx", "lv", "sent", "tripled0", "tripled1",
+SEMAPHORES = ["cv", "ca", "ct", "cg", "lp", "lsw", "lqw", "lub", "lxb", "lvb", "sent", "laid", "skewed",
               "aw0", "aw1", "aw2", "au0", "au1", "au2", "outs", "outa"]
 SIZE = {"float32": 4, "int32": 4, X4: 4, "bfloat16": 2, "uint16": 2, "uint8": 1}
 CYCLE = 0.83
@@ -116,7 +123,122 @@ def plan(calls):
     for k in reversed(range(n)):
         rank[k] = min(calls[k]["cost"].values()) + max([rank[j] + lag for j, lag in after[k].items()] + [calls[k]["late"]])
     best = None
+    PLAN["chain"] = max(rank)
+    rank = [r + c["lift"] for r, c in zip(rank, calls)]
     late = [c["late"] for c in calls]
+
+    def forward(rank):
+        free = {q: 0.0 for q in "vatgs"}
+        banks = {}
+        start, end, on = [0.0] * n, [0.0] * n, [None] * n
+        left = [len(before[k]) for k in range(n)]
+        ready = {k: 0.0 for k in range(n) if not left[k]}
+        while ready:
+            can = []
+            for k, t0 in ready.items():
+                t0 = max([t0] + [banks[x[1]][0] + wake * (banks[x[1]][1] != q) for x in calls[k]["r"] + calls[k]["w"]
+                                 if x[0] == "ps" and x[1] in banks for q in calls[k]["cost"]])
+                q = min(calls[k]["cost"], key=lambda q: max(t0, free[q]) + calls[k]["cost"][q] + OPT["bias"] * (q == "v"))
+                can.append((max(t0, free[q]) + calls[k]["cost"][q], max(t0, free[q]), q, k))
+            first = min(can)
+            q = first[2]
+            rivals = sorted([c for c in can if c[2] == q and c[1] < first[0] + OPT["ahead"]], key=lambda c: -rank[c[3]])[:OPT["rivals"]]
+
+            def worst(c):
+                t, most = c[0], c[1] + rank[c[3]]
+                for d in rivals:
+                    if d is not c:
+                        t = max(t, d[1])
+                        most = max(most, t + rank[d[3]])
+                        t += d[0] - d[1]
+                return (round(most / OPT["grain"]), c[1] if OPT["tie"] else -rank[c[3]])
+            end_k, t, q, k = min(rivals, key=worst)
+            del ready[k]
+            start[k], end[k], on[k], free[q] = t, end_k, q, end_k
+            for x in calls[k]["r"] + calls[k]["w"]:
+                if x[0] == "ps":
+                    banks[x[1]] = (end_k, q)
+            for j, lag in after[k].items():
+                left[j] -= 1
+                if not left[j]:
+                    ready[j] = max(end[i] + g for i, g in before[j].items())
+        return start, end, on
+
+    if "search" in OPT:
+        return OPT["search"](lay, forward, rank, before, after, late, calls)
+    banks_of = [[x[1] for x in c["r"] + c["w"] if x[0] == "ps"] for c in calls]
+
+    def timed(seq, on):
+        last, held, end, why, total, k0 = {}, {}, [0.0] * n, [None] * n, 0.0, None
+        for k in seq:
+            q, t = on[k], 0.0
+            if q in last:
+                t, why[k] = end[last[q]], (last[q], True)
+            for j, lag in before[k].items():
+                if end[j] + lag > t:
+                    t, why[k] = end[j] + lag, (j, False)
+            for b in banks_of[k]:
+                if b in held and on[held[b]] != q and end[held[b]] + wake > t:
+                    t, why[k] = end[held[b]] + wake, (held[b], True)
+                held[b] = k
+            end[k], last[q] = t + calls[k]["cost"][q], k
+            if end[k] + late[k] > total:
+                total, k0 = end[k] + late[k], k
+        pairs = []
+        while why[k0]:
+            if why[k0][1]:
+                pairs.append((why[k0][0], k0))
+            k0 = why[k0][0]
+        return total + OPT["even"] * sum(end) / n, pairs
+
+    def moved(seq, k, j, edges):
+        a, b = seq.index(k), seq.index(j)
+        span = seq[a:b + 1] if a < b else seq[b:a + 1][::-1]
+        need, take, rest = {k}, [], []
+        for x in span:
+            (take if x in need else rest).append(x)
+            if x in need:
+                need.update(edges[x])
+        if j in need:
+            return None
+        return seq[:a] + rest + take + seq[b + 1:] if a < b else seq[:b] + take[::-1] + rest[::-1] + seq[a + 1:]
+
+    def mended(seq, on):
+        total, pairs = timed(seq, on)
+        for _ in range(OPT["mend"]):
+            tries = []
+            for u, v in pairs:
+                mates = [x for x in seq if on[x] == on[u]]
+                a = mates.index(u)
+                tries += [(moved(seq, v, x, before), on) for x in mates[max(0, a - OPT["reach"]):a + 1]]
+                tries += [(moved(seq, u, x, before), on) for x in mates[max(0, a - OPT["reach"]):a]]
+                tries += [(moved(seq, u, x, after), on) for x in mates[a + 1:a + 2 + OPT["reach"]]]
+                tries += [(seq, on[:x] + ["av"[on[x] == "a"]] + on[x + 1:]) for x in (u, v) if len(calls[x]["cost"]) > 1]
+            found = min([timed(s, o) + (s, o) for s, o in tries if s], key=lambda f: f[0], default=None)
+            if found is None or found[0] >= total:
+                break
+            total, pairs, seq, on = found
+        return total, seq, on
+
+    if OPT["rule"] == "mend":
+        for _ in range(OPT["passes"]):
+            start, end, on = forward(rank)
+            found = mended(sorted(range(n), key=lambda k: (start[k], k)), on)
+            if best is None or found[0] < best[0]:
+                best = found
+            rank = [b + c["lift"] for b, c in zip(lay(end, (after, before), late, on)[1], calls)]
+        PLAN["length"] = best[0]
+        return [(k, best[2][k]) for k in best[1]]
+    if OPT["rule"] == "time":
+        for _ in range(OPT["passes"]):
+            start, end, on = forward(rank)
+            total = max(e + t for e, t in zip(end, late))
+            if best is None or total < best[0]:
+                best = (total, start, on)
+            back = lay(end, (after, before), late, on)[1]
+            rank = [OPT["mix"] * (b + c["lift"]) + (1 - OPT["mix"]) * r for b, r, c in zip(back, rank, calls)]
+        PLAN["length"] = best[0]
+        return [(k, best[2][k]) for k in sorted(range(n), key=lambda k: (best[1][k], k))]
     for _ in range(OPT["passes"]):
         start, end, on = lay(rank, (before, after), [0.0] * n, None)
         total = max(e + t for e, t in zip(end, late))
@@ -137,6 +259,7 @@ def rank_program(g, core, T, topo):
     Q = {"v": g.vector, "a": g.scalar, "t": g.tensor, "g": g, "s": g.sync}
     V, S, PE = g.vector, g.scalar, g.tensor
     calls = []
+    lift = [0]
 
     def ap(x):
         if not isinstance(x, tuple):
@@ -157,7 +280,7 @@ def rank_program(g, core, T, topo):
 
     def op(cost, make, r=(), w=(), sem=None, n=1, upto=None, inc=True, late=0, after=()):
         calls.append({"cost": cost, "make": make, "r": [marks(x) for x in parts(r)], "w": [marks(x) for x in parts(w)],
-                      "sem": sem, "n": n, "upto": upto, "inc": inc, "late": late, "after": list(after)})
+                      "sem": sem, "n": n, "upto": upto, "inc": inc, "late": late, "after": list(after), "lift": lift[0]})
         return len(calls) - 1
 
     def length(q, out, *ins):
@@ -232,13 +355,21 @@ def rank_program(g, core, T, topo):
 
     pcol, icol, qcol, tcol, c16, c4, c80, tmp, tmq, tmr = [col("col", k) for k in range(10)]
 
-    for s in range(8):
-        dma("sa"[s % 2], T.lst[16 * s:128, 16 * s + 16:16 * s + 32], T.p[0:128 - 16 * s, :], (), [view("lst", 16 * s + 16, 16 * s + 32, 1, 16 * s)], "lp", 128)
-    lws = dma("s", T.sw[:], T.ws[:], (), [view("sw")], "lws", late=200, after=range(8))
-    lwc = dma("a", T.qw[:].bitcast(dt.uint8), T.wc[:], (), [view("qw")], "lwc", late=900, after=range(8))
-    lu = dma("s", T.ub[:], T.u[:], (), [view("ub")], "lu", late=1200, after=range(8))
-    dma("s", T.xb[:], T.x[:], (), [view("xb")], "lx", late=800, after=[lws])
-    dma("s", T.vb[:], T.v[:], (), [view("vb")], "lv", late=400, after=[lu])
+    def rotor(s):
+        return lambda q, after: dma(q, T.lst[16 * s:128, 16 * s + 16:16 * s + 32], T.p[0:128 - 16 * s, :], (),
+                                    [view("lst", 16 * s + 16, 16 * s + 32, 1, 16 * s)], "lp", 128, late=OPT["plate"], after=after)
+
+    def load(name, out, in_, late):
+        return lambda q, after: dma(q, out, in_, (), [view(name)], "l" + name, late=late, after=after)
+    loads = {"S": load("sw", T.sw[:], T.ws[:], 200), "W": load("qw", T.qw[:].bitcast(dt.uint8), T.wc[:], 900), "u": load("ub", T.ub[:], T.u[:], 1200),
+             "x": load("xb", T.xb[:], T.x[:], 1600), "v": load("vb", T.vb[:], T.v[:], 1600)}
+    loads.update((str(s), rotor(s)) for s in range(8))
+    for q, names in OPT["loads"].items():
+        prev = []
+        for name in names:
+            lift[0] = 1e6
+            prev = [loads[name](q, prev)]
+    lift[0] = 0
 
     iota(view("ip", 0, 10), [[-16, 10]], 16, 1)
     iota(view("cc", 0, 16), [[1, 16]], 0, 0)
@@ -256,7 +387,10 @@ def rank_program(g, core, T, topo):
     move("v", col("goff", 0), icol)
     ts(view("lst", 0, 16), view("cc", 0, 16), 16.0, icol, A.mult, A.add)
     for s in range(1, 8):
-        fill(view("lst", 16 * s + 16, 16 * s + 32, 1, 0, 16 * s), 0)
+        if s > OPT["holes"]:
+            iota(view("lst", 16 * s + 16, 16 * s + 32, 1, 0, 16 * s), [[0, 16]], 0, 0)
+        else:
+            fill(view("lst", 16 * s + 16, 16 * s + 32, 1, 0, 16 * s), 0)
     ts(view("dm", 0, 16), view("cc", 0, 16), icol, None, A.subtract)
     ts(view("dm", 16, 32), view("cc", 16, 32), qcol, None, A.subtract)
     ts(view("moff"), view("cc", 0, 16), 0.0, icol, A.mult, A.add)
@@ -267,6 +401,8 @@ def rank_program(g, core, T, topo):
     move("a", view("m4"), by(view("msm", 16, 32), view("moff", 0, 8)))
     ts(c16, icol, 15.0, 256.0, A.is_lt, A.mult)
     ts(c80, c16, 64.0, None, A.add)
+    mirror, tms = col("col", 11), col("col", 12)
+    ts(mirror, c16, -1.0, 255.0, A.mult, A.add)
     short = (c80, c80)
     if OPT["other"] == "a":
         short = (c80, col("col", 10))
@@ -279,19 +415,25 @@ def rank_program(g, core, T, topo):
     fill(view("uoff", 4, 12), 0)
     move("v", col("aoff", 0), col("iq", 3))
 
-    for name, at in (("ea", 2), ("eb", 3)):
-        fill(view(name), 0.0)
-        ts(view(name, at, at + 512, 4), view("iot", 0, 128), pcol, None, A.is_equal)
-    for b in range(4):
-        at = 2 - 2 * (b // 2)
-        quant("e", 128 * b, 128, view(("ea", "eb")[b % 2], at, at + 512))
+    fill(view("gt"), 0.0)
+
+    def unit_tiles(after):
+        for name, at in (("ea", 2), ("eb", 3)):
+            if OPT["eg"]:
+                op({"g": 170 + 2 * CYCLE * 528}, lambda q, name=name, at=at: g.affine_select(T[name][:], T.gt[:, 0:528], [[1, 528]], A.not_equal, 1.0, -at, -4),
+                   [view("gt")], [view(name)], after=after)
+            else:
+                fill(view(name), 0.0)
+                ts(view(name, at, at + 512, 4), view("iot", 0, 128), pcol, None, A.is_equal)
+        for b in range(4):
+            at = 2 - 2 * (b // 2)
+            quant("e", 128 * b, 128, view(("ea", "eb")[b % 2], at, at + 512))
     for t, c in enumerate((0.5, 0.5, -0.5, 1.0)):
         fill(view("kp", t, 512, 4), c)
         fill(view("kn", t, 512, 4), -c)
     quant("k", 0, 128, view("kp"))
     quant("k", 128, 128, view("kn"))
     ts(view("tri"), view("iot", 0, 128), pcol, None, A.is_gt)
-    fill(view("gt"), 0.0)
     fill(view("dcum"), 0.0)
     fill(view("zer"), 0.0)
     quant("v", 0, 128, view("vb"))
@@ -299,52 +441,38 @@ def rank_program(g, core, T, topo):
     peers = [T.cores[rank ^ h] for h in TURN]
     every = topo.engines(core, peers[0])
     far = topo.engines(core, peers[1])
-    ways = [every, far[:len(far) // 2], far[len(far) // 2:]]
-    aw, au = ["aw0", "aw1", "aw2"], ["au0", "au1", "au2"]
+    near = [e for e in every if e not in far]
+    sets = {"every": every, "far": far, "near": near, "low": far[:len(far) // 2], "high": far[len(far) // 2:]}
     remote = []
-
-    def bits(es):
-        return sum(1 << e for e in es)
-
-    def dst(c):
-        a = topo.addr(c)
-        return DstId(rid=a[0], pnc=a[1])
+    landed = {}
 
     def whole(name):
         return T[name][:].bitcast(dt.uint8) if name[0] == "q" else T[name][:]
 
-    def send(src, land, sems):
-        tr = [RemoteDMATransfer(dst_ids=[dst(peers[i])], dma_engine_mask=bits(ways[i]), remote_sem=T.sem[sems[i]],
-                                src=whole(src), dst=whole(land % i)) for i in (1, 2)]
-        remote.append(op({"g": 400}, lambda q: g.remote_dma_fused(tr, local_sem=T.sem.sent), [view(src)], [view(land % i) for i in (1, 2)],
-                         "sent", len(far), inc=False, late=OPT["far"], after=remote[-1:]))
-
-    def write(src, land, i, es, sems, late):
+    def remote_call(src, *to):
+        tr = []
+        for i, es in to:
+            a = topo.addr(peers[i])
+            sem = "a%s%d" % (src[1], i)
+            landed[sem] = landed.get(sem, 0) + len(sets[es])
+            tr.append(RemoteDMATransfer(dst_ids=[DstId(rid=a[0], pnc=a[1])], dma_engine_mask=sum(1 << e for e in sets[es]),
+                                        remote_sem=T.sem[sem], src=whole(src), dst=whole(src[:2] + str(i))))
+        i, es = to[0]
         a = topo.addr(peers[i])
-        remote.append(op({"g": 400}, lambda q: g.remote_dma(whole(land % i), whole(src), T.sem[sems[i]], T.sem.sent, a[1], a[0], bits(es)),
-                         [view(src)], [view(land % i)], "sent", len(es), inc=False, late=late, after=remote[-1:]))
 
-    arrivals = {}
-    for i in range(3):
-        for name in ("qw%d", "sw%d"):
-            arrivals[name % i] = (aw[i], len(ways[i]) + len(far if i else every))
-        for name in ("qu%d", "su%d"):
-            arrivals[name % i] = (au[i], 2 * len(ways[i]))
+        def make(q):
+            if len(tr) > 1:
+                return g.remote_dma_fused(tr, local_sem=T.sem.sent)
+            return g.remote_dma(whole(src[:2] + str(i)), whole(src), T.sem["a%s%d" % (src[1], i)], T.sem.sent, a[1], a[0], sum(1 << e for e in sets[es]))
+        r = [view(src)] + ([view("skew")] if OPT["skew"] == 2 and i else [])
+        remote.append(op({"g": 400}, make, r, [view(src[:2] + str(j)) for j, _ in to], "sent", sum(len(sets[e]) for _, e in to), inc=False,
+                         late=OPT["far"] if i else OPT["hop"] + 600 * (src == "qw"), after=remote[-1:]))
 
     quant("u", 0, 128, view("ub"))
     op({"v": 50 + UP * OPT["gather"]},
        lambda q: V.tensor_copy(T.qup[:].bitcast(dt.uint32), T.qu[:].bitcast(dt.uint32).indirect(T.uoff[:, 0:12])),
        [view("qu"), view("uoff", 0, 12)], [view("qup")])
     move("va", view("sup"), by(view("su"), view("uoff", 0, 12)))
-    write("sw", "sw%d", 0, every, aw, OPT["hop"])
-    write("qw", "qw%d", 0, every, aw, OPT["hop"] + 600)
-    write("qup", "qu%d", 0, every, au, OPT["hop"])
-    write("sup", "su%d", 0, every, au, OPT["hop"])
-    write("qw", "qw%d", 1, far, aw, OPT["far"])
-    send("sw", "sw%d", aw)
-    send("qup", "qu%d", au)
-    send("sup", "su%d", au)
-    write("qw", "qw%d", 2, far, aw, OPT["far"])
 
     def lists(m):
         return view("off", 16 * m, 16 * m + 16)
@@ -358,26 +486,40 @@ def rank_program(g, core, T, topo):
             move(q, rows[s + 1], by(rows[s], lists(m - s)))
     to_list("jl", view("rc"), "sr", c16)
     halves("va", "erow", view("tl", 0, C), "jl")
-    for k, name in enumerate(("s3", "r3")):
+    for name in ("s3", "r3")[OPT["fold"]:]:
         for a in (0, 2 * C):
-            dma("s", ap(view(name, a, a + C)), ap(mid(name)), [mid(name)], [view(name, a, a + C)], "tripled%d" % k, 32)
-    move("va", view("lj", 0, 64), view("off", 0, 64))
-    move("va"[0], view("lj", 80, 128), view("off", 80, 128))
+            move(OPT["triple"], view(name, a, a + C), mid(name))
+    move("v", view("lj", 0, 128 + 16 * OPT["fold"]), view("off", 0, 128 + 16 * OPT["fold"]))
     fill(view("lj", 64, 80), 0)
+    if OPT["skew"]:
+        late_table = OPT["table"]
+        move("a", view("rho"), by(view("iot"), lists(1)))
+        dma("s", T.flat[0:1, 0:128 * C], T.rho[:], [view("rho")], [("flat", 0, 1, 1, 0, 1)], "laid", 32)
+        dma("s", T.flat[0:1, 128 * C:129 * C], T.rho[0:1, :], [view("rho")], [("flat", 1, 2, 1, 0, 1)], "laid", 32)
+        dma("s", T.skew[:, 0:C + 1], T.flat[0:1, 0:128 * (C + 1)], [("flat", 0, 2, 1, 0, 1)], [view("skew")], "skewed", late=late_table)
+        ts(tms, col("iq", 3), -1.0, icol, A.mult, A.add)
+        ts(col("lj", 0), tms, 16.0, None, A.mult)
+    for k, step in enumerate(OPT["sends"]):
+        if k == OPT["near"]:
+            unit_tiles(remote[-1:])
+        remote_call(*step)
 
     def path_list():
         scan(view("se2"), view("m16"), view("erow"))
-        ts(view("eli"), view("se2", 15, C, 16), c16, None, A.add)
+        ts(view("lj", 128, 144), view("se2", 15, C, 16), -1.0, mirror, A.mult, A.add)
 
     def gather(first, row, name):
         for h in range(2):
+            lift[0] = OPT["lift"] * (1 - h)
             scan(view("sb", 128 * h, 128 * h + 128), view("m4"), view(row, 128 * h, 128 * h + 128))
             ts(view("l4", 32 * h, 32 * h + 32), view("sb", 128 * h + 3, 128 * h + 128, 4), 4.0, c4, A.mult, A.add)
         cuts = (0,) + OPT["cuts"] + (64,)
         for k in range(len(cuts) - 1):
             a, b = cuts[k], cuts[k + 1]
+            lift[0] = OPT["lift"] * (a < 32)
             move(OPT["big"][k], view("ft", 16 * a, 16 * b), by(view("xb" if first else "st"), view("l4", a, b)), None if first else 0.5)
         for h in range(2):
+            lift[0] = OPT["lift"] * (1 - h)
             quant(name, 128 * h, 128, view("ft", 512 * h, 512 * h + 512))
 
     COLS, ROWS, SIGNS, COUNTS, RANKS, UNPACK = (0, 4), (1, 5), (2, 6), 3, (7, 4), (0, 1, 2, 5)
@@ -385,9 +527,9 @@ def rank_program(g, core, T, topo):
     def layer(i):
         u = "u%d" % i
         for h in range(2):
+            lift[0] = OPT["lift"] * (1 - h)
             for k in range(4):
                 mm(4 * h + k, 128, ("w%d" % i, 128 * k, "f", 128 * h))
-        for h in range(2):
             for k in range(4):
                 move(OPT["casts"][4 * h + k], view("ht", 512 * h + k, 512 * h + 512, 4), bank(4 * h + k, 0, 128), 0.0078125)
             quant("h", 128 * h, 128, view("ht", 512 * h, 512 * h + 512))
@@ -398,8 +540,9 @@ def rank_program(g, core, T, topo):
             move("v", col("scol", 4 * h), bank(COLS[h], 64, 65))
             ts(view("gt", 32 + 3 * h, 288, 4), bank(COLS[h], 0, 64), 0.0, 2.0 - h, A.is_gt, A.mult)
         slot = lambda h, t: view("ct", 512 * h + t, 512 * h + 512, 4)
+        score = lambda h: bank(COLS[h], 64, 65) if OPT["direct"] else col("scol", 4 * h)
         for h in range(2):
-            ts(slot(h, 2), bank(ROWS[h], 0, 128), col("scol", 4 * h), None, A.is_equal)
+            ts(slot(h, 2), bank(ROWS[h], 0, 128), score(h), None, A.is_equal)
             scan(slot(h, 3), view("tri"), slot(h, 2), A.max, A.mult)
             sign(slot(h, 1), bank(SIGNS[h], 0, 128), col("scol", 4 * h), -1.0)
         for h in range(2):
@@ -407,13 +550,13 @@ def rank_program(g, core, T, topo):
                 sign(view("sg2", 0, 128), bank(SIGNS[h], 0, 128), col("scol", 0), -1.0)
                 op({"a": length("a", slot(h, 0))}, lambda q: S.activation(ap(slot(1, 0)), ap(view("sg2", 0, 128)), SIGN, bias=0.5), [view("sg2", 0, 128)], [slot(1, 0)])
             else:
-                ts(slot(h, 0), bank(ROWS[h], 0, 128), col("scol", 4 - 4 * h), 2.0, A.is_le if h else A.is_lt, A.mult)
+                ts(slot(h, 0), bank(ROWS[h], 0, 128), score(1 - h), 2.0, A.is_le if h else A.is_lt, A.mult)
         quant("g", 0, 136, view("gt"))
         mm(COUNTS, 128, ("k", 0, "g", 8), ("k", 128, "g", 0))
         for h in range(2):
             quant("c", 128 * h, 128, view("ct", 512 * h, 512 * h + 512))
 
-    def sort():
+    def sort(partners=True):
         if OPT["rhalf"]:
             for h in range(2):
                 mm(RANKS[h], 128, ("k", 0, "c", 128 * h))
@@ -428,7 +571,8 @@ def rank_program(g, core, T, topo):
             move("v", by(view("orow"), view("rl")), view("iot"))
         for h in range(2):
             move(OPT["swap"][h], view("oswp", h, C, 2), view("orow", 1 - h, C, 2))
-        halves(OPT["m"], "mrow", view("oswp"), "rl")
+        if partners:
+            halves(OPT["m"], "mrow", view("oswp"), "rl")
 
     def unpack():
         for b in range(4):
@@ -443,8 +587,7 @@ def rank_program(g, core, T, topo):
         ts(view("o6"), view("lj", 112, 128), bank(COUNTS, 56, 57), 256.0, A.add, A.add)
         ts(view("o2"), view("lj", 48, 64), bank(COUNTS, 24, 25), 256.0, A.add, A.add)
         for e in range(2):
-            tt(view("li", e, 128, 2), bank(COUNTS, 0, 64), view("lj", e, 128, 2), A.add)
-        ts(view("li", 128, 144), view("eli"), bank(COUNTS, 64, 65), None, A.subtract)
+            tt(view("li", e, 144, 2), bank(COUNTS, 0, 72), view("lj", e, 144, 2), A.add)
         steps()
         ts(view("lj"), view("li"), 255, None, A.bitwise_and)
         move("v", view("off"), view("lj"))
@@ -452,26 +595,104 @@ def rank_program(g, core, T, topo):
         left = ((view("s3"), view("o6")), (view("ta"), lists(6)), (view("tb"), lists(5)))
         for s, to in enumerate((view("ta"), view("tb"), view("tl", 0, C))):
             move(OPT["left"][s], to, by(*left[s]))
-        right = ((view("r3"), view("o2")), (view("ra"), lists(2)), (view("rb"), lists(1)), (view("ra"), lists(0)))
-        for s, to in enumerate((view("ra"), view("rb"), view("ra"), view("rc"))):
-            move(OPT["right"][s], to, by(*right[s]))
+        if OPT["skew"]:
+            ts(view("ei"), by(view("skew", 0, C), col("off", 0)), col("dcum", 1), None, A.add)
+            ts(view("ej"), view("ei"), 255, None, A.bitwise_and)
+            move("v", view("o0"), view("ej"))
+            right = ((view("r3"), view("o2")), (view("ra"), lists(2)), (view("rb"), view("o0")))
+            for s, to in enumerate((view("ra"), view("rb"), view("rc"))):
+                move(OPT["right"][s], to, by(*right[s]))
+        else:
+            right = ((view("r3"), view("o2")), (view("ra"), lists(2)), (view("rb"), lists(1)), (view("ra"), lists(0)))
+            for s, to in enumerate((view("ra"), view("rb"), view("ra"), view("rc"))):
+                move(OPT["right"][s], to, by(*right[s]))
         move(OPT["dbl"], view("tl", C, 2 * C), view("tl", 0, C))
         to_list("jl", view("rc"), "sr", col("dcol", 0))
         halves(OPT["join"], "erow", view("tl"), "jl")
         for h in range(2):
-            to_list("el", view("erow", 128 * h, 128 * h + 128), "se2", c16, 128 * h, 128 * h + 128)
+            scan(view("se2", 128 * h, 128 * h + 128), view("m16", 0, 128), view("erow", 128 * h, 128 * h + 128))
+            ts(view("el", 8 * h, 8 * h + 8), view("se2", 128 * h + 15, 128 * h + 128, 16), -1.0, mirror, A.mult, A.add)
         sort()
         unpack()
         move("v", by(view("me"), lists(8)), view("mrow"))
         halves(OPT["crow"], "crow", view("me"), "el")
-        move("v", view("eli"), view("el"))
+        move("v", view("lj", 128, 144), view("el"))
+
+    def inverse(tripled):
+        to_list("ul", view("erow"), "se2", c16)
+        n = 16 // OPT["pieces"]
+        for a in range(0, 16, n):
+            move("v", by(mid("s3"), view("ul", a, a + n)), view("iot", 16 * a, 16 * (a + n)))
+        if tripled:
+            for a in (0, 2 * C):
+                move(OPT["triple"], view("s3", a, a + C), mid("s3"))
+        else:
+            to_list("il", mid("s3"), "sa", c16)
+
+    def folded(i):
+        ts(view("o6"), view("lj", 128, 144), bank(COUNTS, 64, 65), 256.0, A.add, A.add)
+        ts(view("o2"), view("lj", 48, 64), bank(COUNTS, 24, 25), 256.0, A.add, A.add)
+        for e in range(2):
+            tt(view("li", e, 144, 2), bank(COUNTS, 0, 72), view("lj", e, 144, 2), A.add)
+        steps()
+        ts(view("lj"), view("li"), 255, None, A.bitwise_and)
+        move("v", view("off"), view("lj"))
+        ts(col("dcol", 0), col("lj", 64), c16, None, A.add)
+        left = ((view("s3"), view("o6")), (view("ta"), lists(7)), (view("tb"), lists(6)), (view("ta"), lists(5)))
+        for s, to in enumerate((view("ta"), view("tb"), view("ta"), view("tl", 0, C))):
+            move(OPT["fleft"][s], to, by(*left[s]))
+        if OPT["skew"]:
+            ts(view("ei"), by(view("skew", 0, C), col("off", 0)), col("dcum", 1), None, A.add)
+            ts(view("ej"), view("ei"), 255, None, A.bitwise_and)
+            move("v", view("o0"), view("ej"))
+            right = ((view("r3"), view("o2")), (view("ra"), lists(2)), (view("rb"), view("o0")))
+            for s, to in enumerate((view("ra"), view("rb"), view("rc"))):
+                move(OPT["right"][s], to, by(*right[s]))
+        else:
+            right = ((view("r3"), view("o2")), (view("ra"), lists(2)), (view("rb"), lists(1)), (view("ra"), lists(0)))
+            for s, to in enumerate((view("ra"), view("rb"), view("ra"), view("rc"))):
+                move(OPT["right"][s], to, by(*right[s]))
+        to_list("el", view("tl", 0, C), "sa", c16)
+        to_list("jl", view("rc"), "sr", col("dcol", 0))
+        sort()
+        unpack()
+        for h in range(2):
+            move(OPT["ml"][h], view("ml", C * h, C * h + C), by(view("mrow"), view("el")))
+        halves(OPT["crow"], "crow", view("ml"), "jl")
+        move(OPT["dbl"], view("tl", C, 2 * C), view("tl", 0, C))
+        halves("a", "brow", view("tl"), "jl")
+        to_list("bl", view("brow"), "sr", c16)
+        move("a", view("me"), view("erow")) if 0 else None
+        move("a", view(("me", "erow")[i]), by(view(("erow", "me")[i]), view("bl")))
+        if i == 0:
+            to_list("ul", view("me"), "se2", c16)
+            n = 16 // OPT["pieces"]
+            for a in range(0, 16, n):
+                move("v", by(mid("s3"), view("ul", a, a + n)), view("iot", 16 * a, 16 * (a + n)))
+            for a in (0, 2 * C):
+                move(OPT["triple"], view("s3", a, a + C), mid("s3"))
+        else:
+            inverse(False)
 
     def last():
-        ts(view("ei"), view("eli"), col("dcum", 8), None, A.add)
+        if OPT["fold"]:
+            move("v", view("ej"), view("ul"))
+        else:
+            unfolded()
+        finish()
+
+    def unfolded():
+        ts(col("dcol", 1), col("dcum", 8), 255.0, None, A.add)
+        ts(view("ei"), view("lj", 128, 144), -1.0, col("dcol", 1), A.mult, A.add)
         ts(view("ej"), view("ei"), 255, None, A.bitwise_and)
         move("v", view("ul"), view("ej"))
-        move("v", by(view("einv"), view("ul")), view("iot"))
-        to_list("il", view("einv"), "sa", c16)
+        if OPT["last"] != "scatter":
+            n = 16 // OPT["pieces"]
+            for a in range(0, 16, n):
+                move("v", by(view("einv"), view("ul", a, a + n)), view("iot", 16 * a, 16 * (a + n)))
+            to_list("il", view("einv"), "sa", c16)
+
+    def finish():
         steps()
         scan(view("acum", 0, 9), view("dcum", 0, 9), view("zer", 0, 9), A.add, A.add)
         move("v", view("acol"), by(view("acum", 0, 9), col("aoff", 0)))
@@ -479,9 +700,24 @@ def rank_program(g, core, T, topo):
         ts(view("em"), view("ek"), 255, None, A.bitwise_and)
         move("v", view("jl"), view("em"))
         move("a", view("optab"), by(view("iot"), view("jl")))
-        sort()
-        unpack()
-        halves(OPT["crow"], "crow", view("mrow"), "il")
+        if OPT["last"] == "ranks":
+            sort(False)
+            mm(RANKS[1], C, ("k", 0, "c", 0))
+            for h in range(2):
+                op({"a": length("a", view("ta", 0, 128))},
+                   lambda q, h=h: S.activation(T.ta[:, 128 * h:128 * h + 128], ap(bank(RANKS[1], 128 * h, 128 * h + 128)), IDENT, bias=64.0 if short[h] == c80 else 128.0),
+                   [bank(RANKS[1])], [view("ta", 128 * h, 128 * h + 128)])
+            move("a", view("tb"), by(view("ta"), view("il")))
+            to_list("el", view("tb"), "sr", c16)
+            unpack()
+            halves(OPT["crow"], "crow", view("oswp"), "el")
+        else:
+            sort()
+            unpack()
+            if OPT["last"] == "scatter":
+                move("v", by(view("crow"), view("ul")), view("mrow"))
+            else:
+                halves(OPT["crow"], "crow", view("mrow"), "il")
         gather(False, "crow", "x")
         to_list("cl", view("crow"), "sa", c16)
         move("a", view("oprow"), by(view("optab"), view("cl")))
@@ -498,10 +734,10 @@ def rank_program(g, core, T, topo):
     for i in range(3):
         gather(i == 0, "crow" if i else "erow", "f")
         if i == 0:
-            path_list()
+            inverse(True) if OPT["fold"] else path_list()
         layer(i)
         if i < 2:
-            turn()
+            folded(i) if OPT["fold"] else turn()
         else:
             last()
 
@@ -510,9 +746,10 @@ def rank_program(g, core, T, topo):
     known = {q: {} for q in Q}
     count = {}
     touched = {}
-    for name, (sem, n) in arrivals.items():
+    for sem, n in landed.items():
         count[sem] = n
-        touched[name] = [(marks(view(name)), True, (sem, n, {sem: n}, 0, "x"))]
+        for name in ("q" + sem[1:], "s" + sem[1:]):
+            touched[name] = [(marks(view(name)), True, (sem, n, {sem: n}, 0, "x"))]
     for serial, (k, q) in enumerate(PLAN["order"]):
         c = calls[k]
         mine = [(x, False) for x in c["r"]] + [(x, True) for x in c["w"] if c["inc"]]

@@ -17,7 +17,14 @@ OPT = {"wake": 150, "bias": 120, "gather": 1.2, "scatter": 2.6, "load": 2000, "h
        "rule": "time", "ahead": 100, "rivals": 8, "grain": 60, "tie": 1, "mix": 1.0, "eg": 1, "holes": 3, "plate": 300,
        "mend": 60, "reach": 2, "even": 0.05, "fold": 0, "fleft": "aaaa", "ml": "va",
        "lift": 0, "direct": 1, "triple": "va", "last": "scatter", "pieces": 1, "loads": {"s": "SWuxv", "a": "01234567"}}
-OPT.update(wake=200, hop=3600, last="ranks", triple="va", skew=2, table=3000, near=4, far=3500, casts=("va",) * 8, dbl="va", fold=0, rule="mend", passes=1, mend=40, rhalf=1)
+OPT.update(wake=200, hop=3600, last="ranks", triple="va", skew=2, table=3000, inorder=1, near=4, far=3500, casts=("va",) * 8, dbl="va", fold=0, rule="mend", passes=1, mend=40, rhalf=1)
+FAR = ((3500, ("qw", 0, 512, 1, "far", "aw1")), (3500, ("sw", 0, 512, 1, "low", "aw1"), ("sw", 0, 512, 2, "high", "aw2")),
+       (3500, ("qup", 0, UP, 1, "far", "au1")), (3500, ("sup", 0, UP, 1, "low", "au1"), ("sup", 0, UP, 2, "high", "au2")),
+       (3500, ("qw", 0, 512, 2, "far", "aw2")), (3500, ("qup", 0, UP, 2, "far", "au2")))
+NEAR_U = ((2400, ("qup", 0, UP, 0, "every", "au0")), (2400, ("sup", 0, UP, 0, "every", "au0")))
+OPT.update(inorder=0, issue=100, vlate=1, near=5, loads={"s": "S135ABx", "a": "02467u"}, skew=3, plate=-400, table=0, holes=7, early=3000, least=0.05, passes=3,
+           sends=((1800, ("sw", 0, 512, 0, "every", "aw0")), (1900, ("qw", 0, 256, 0, "every", "aw0")), (2400, ("qw", 256, 512, 0, "every", "ax0")))
+           + NEAR_U + FAR)
 
 
 def _pair(name, n):
@@ -36,7 +43,7 @@ for _d in (_of("bfloat16", 4 * C, "xb", "ft", "ht", "ct"), _of("bfloat16", 512, 
                "erow", "einv", "optab", "rho", "brow"), _of("uint16", 16, "o0", "bl"), _of("bfloat16", 2 * C, "ml"),
            _of("bfloat16", 128, "m4", "tri"), _of("float32", C, "sf32", "oprow", "yb"), _of("uint16", 64, "l4"),
            _of("int32", 16, "eli", "ei", "ej", "ek", "em", "ip", "iq"), _of("uint16", 2, "aoff"),
-           _of("float32", 16, "col", "acol", "dcum", "acum", "zer", "scol", "dcol"), _of("float32", 32, "cc", "dm", "a1", "a2"),
+           _of("float32", 16, "col", "acol", "dcum", "acum", "keep", "scol", "dcol"), _of("bfloat16", 2 * C, "wrap"), _of("float32", 32, "cc", "dm", "a1", "a2"),
            _of("bfloat16", 32, "msm")):
     SCRATCH.update(_d)
 for _n, _k in (("w", 512), ("w0", 512), ("w1", 512), ("w2", 512), ("u", 128), ("up", UP), ("u0", UP), ("u1", UP), ("u2", UP),
@@ -44,7 +51,7 @@ for _n, _k in (("w", 512), ("w0", 512), ("w1", 512), ("w2", 512), ("u", 128), ("
     SCRATCH.update(_pair(_n, _k))
 
 SEMAPHORES = ["cv", "ca", "ct", "cg", "lp", "lsw", "lqw", "lub", "lxb", "lvb", "sent", "laid", "skewed",
-              "aw0", "aw1", "aw2", "au0", "au1", "au2", "outs", "outa"]
+              "aw0", "aw1", "aw2", "au0", "au1", "au2", "outs", "ax0", "lqx"]
 SIZE = {"float32": 4, "int32": 4, X4: 4, "bfloat16": 2, "uint16": 2, "uint8": 1}
 CYCLE = 0.83
 
@@ -76,7 +83,10 @@ def plan(calls):
         for x, writes in [(x, False) for x in c["r"]] + [(x, True) for x in c["w"]]:
             for j, y, wrote in seen.get(x[0], []):
                 if j != k and (writes or wrote) and meet(x, y):
-                    before[k][j] = calls[j]["late"] + wake
+                    if OPT["inorder"] and writes and list(c["cost"]) == list(calls[j]["cost"]) in (["v"], ["a"]):
+                        before[k].setdefault(j, 0)
+                    else:
+                        before[k][j] = calls[j]["late"] + wake
             seen.setdefault(x[0], []).append((k, x, writes))
     after = [{} for _ in calls]
     for k in range(n):
@@ -205,19 +215,21 @@ def plan(calls):
 
     def mended(seq, on):
         total, pairs = timed(seq, on)
-        for _ in range(OPT["mend"]):
-            tries = []
-            for u, v in pairs:
-                mates = [x for x in seq if on[x] == on[u]]
-                a = mates.index(u)
-                tries += [(moved(seq, v, x, before), on) for x in mates[max(0, a - OPT["reach"]):a + 1]]
-                tries += [(moved(seq, u, x, before), on) for x in mates[max(0, a - OPT["reach"]):a]]
-                tries += [(moved(seq, u, x, after), on) for x in mates[a + 1:a + 2 + OPT["reach"]]]
-                tries += [(seq, on[:x] + ["av"[on[x] == "a"]] + on[x + 1:]) for x in (u, v) if len(calls[x]["cost"]) > 1]
+        at = idle = 0
+        while idle < len(pairs):
+            u, v = pairs[at % len(pairs)]
+            mates = [x for x in seq if on[x] == on[u]]
+            a = mates.index(u)
+            tries = [(moved(seq, v, x, before), on) for x in mates[max(0, a - OPT["reach"]):a + 1]]
+            tries += [(moved(seq, u, x, before), on) for x in mates[max(0, a - OPT["reach"]):a]]
+            tries += [(moved(seq, u, x, after), on) for x in mates[a + 1:a + 2 + OPT["reach"]]]
+            tries += [(seq, on[:x] + [q] + on[x + 1:]) for x in (u, v) for q in calls[x]["cost"] if q != on[x]]
             found = min([timed(s, o) + (s, o) for s, o in tries if s], key=lambda f: f[0], default=None)
-            if found is None or found[0] >= total:
-                break
-            total, pairs, seq, on = found
+            if found and found[0] < total - OPT["least"]:
+                total, pairs, seq, on = found
+                idle = 0
+            else:
+                at, idle = at + 1, idle + 1
         return total, seq, on
 
     if OPT["rule"] == "mend":
@@ -339,12 +351,12 @@ def rank_program(g, core, T, topo):
     def scan(out, d0, d1, op0=A.add, op1=A.min):
         op({"v": length("v", out, d0, d1)}, lambda q: V.tensor_tensor_scan(ap(out), ap(d0), ap(d1), 0.0, op0, op1), [d0, d1], [out])
 
-    def iota(out, pattern, base, mult):
+    def iota(out, pattern, base, mult, after=()):
         more = {} if SCRATCH[out[0]][2] == "int32" else {"allow_small_or_imprecise_dtypes": True}
-        op({"g": 130 + 2 * CYCLE * width(out)}, lambda q: g.iota(ap(out), pattern, base, mult, **more), (), [out])
+        op({"g": 130 + 2 * CYCLE * width(out)}, lambda q: g.iota(ap(out), pattern, base, mult, **more), (), [out], after=after)
 
     def dma(q, out, in_, r, w, sem, upto=None, late=0, after=()):
-        return op({q: 60}, lambda _: Q[q].dma_start(out, in_), r, w, sem, 16, upto, late=OPT["load"] + late, after=after)
+        return op({x: OPT["issue"] for x in q}, lambda x: Q[x].dma_start(out, in_), r, w, sem, 16, upto, late=OPT["load"] + late, after=after)
 
     def col(name, k):
         return view(name, k, k + 1)
@@ -364,6 +376,9 @@ def rank_program(g, core, T, topo):
     loads = {"S": load("sw", T.sw[:], T.ws[:], 200), "W": load("qw", T.qw[:].bitcast(dt.uint8), T.wc[:], 900), "u": load("ub", T.ub[:], T.u[:], 1200),
              "x": load("xb", T.xb[:], T.x[:], 1600), "v": load("vb", T.vb[:], T.v[:], 1600)}
     loads.update((str(s), rotor(s)) for s in range(8))
+    for k, name in enumerate("AB"):
+        loads[name] = lambda q, after, k=k: dma(q, T.qw[:, 256 * k:256 * k + 256].bitcast(dt.uint8), T.wc[:, 1024 * k:1024 * k + 1024], (),
+                                                [view("qw", 256 * k, 256 * k + 256)], ("lqw", "lqx")[k], late=500 + 400 * k, after=after)
     for q, names in OPT["loads"].items():
         prev = []
         for name in names:
@@ -371,6 +386,7 @@ def rank_program(g, core, T, topo):
             prev = [loads[name](q, prev)]
     lift[0] = 0
 
+    lift[0] = OPT["early"]
     iota(view("ip", 0, 10), [[-16, 10]], 16, 1)
     iota(view("cc", 0, 16), [[1, 16]], 0, 0)
     iota(view("cc", 16, 32), [[0, 4], [1, 4]], 0, 0)
@@ -399,6 +415,7 @@ def rank_program(g, core, T, topo):
     tt(view("msm"), view("a1"), view("a2"), A.add)
     move("a", view("m16"), by(view("msm", 0, 16), view("moff")))
     move("a", view("m4"), by(view("msm", 16, 32), view("moff", 0, 8)))
+    lift[0] = 0
     ts(c16, icol, 15.0, 256.0, A.is_lt, A.mult)
     ts(c80, c16, 64.0, None, A.add)
     mirror, tms = col("col", 11), col("col", 12)
@@ -413,7 +430,8 @@ def rank_program(g, core, T, topo):
     ts(view("dm", 0, 4), view("cc", 0, 4), 32.0, 1.0, A.mult, A.add)
     ts(view("uoff", 0, 4), view("dm", 0, 4), tmr, None, A.add)
     fill(view("uoff", 4, 12), 0)
-    move("v", col("aoff", 0), col("iq", 3))
+    ts(col("col", 13), col("iq", 3), 1.0, None, A.add)
+    ts(view("keep", 0, 9), view("cc", 0, 9), col("col", 13), None, A.not_equal)
 
     fill(view("gt"), 0.0)
 
@@ -435,8 +453,6 @@ def rank_program(g, core, T, topo):
     quant("k", 128, 128, view("kn"))
     ts(view("tri"), view("iot", 0, 128), pcol, None, A.is_gt)
     fill(view("dcum"), 0.0)
-    fill(view("zer"), 0.0)
-    quant("v", 0, 128, view("vb"))
 
     peers = [T.cores[rank ^ h] for h in TURN]
     every = topo.engines(core, peers[0])
@@ -446,27 +462,31 @@ def rank_program(g, core, T, topo):
     remote = []
     landed = {}
 
-    def whole(name):
-        return T[name][:].bitcast(dt.uint8) if name[0] == "q" else T[name][:]
+    def sent(x):
+        return ap(x).bitcast(dt.uint8) if x[0][0] == "q" else ap(x)
 
-    def remote_call(src, *to):
-        tr = []
-        for i, es in to:
-            a = topo.addr(peers[i])
-            sem = "a%s%d" % (src[1], i)
-            landed[sem] = landed.get(sem, 0) + len(sets[es])
-            tr.append(RemoteDMATransfer(dst_ids=[DstId(rid=a[0], pnc=a[1])], dma_engine_mask=sum(1 << e for e in sets[es]),
-                                        remote_sem=T.sem[sem], src=whole(src), dst=whole(src[:2] + str(i))))
-        i, es = to[0]
-        a = topo.addr(peers[i])
+    def remote_call(late, *moves):
+        tr, r, w = [], [], []
+        for src, a, b, i, es, sem in moves:
+            to = topo.addr(peers[i])
+            r.append(view(src, a, b))
+            w.append(view(src[:2] + str(i), a, b))
+            es = sets[es] if isinstance(es, str) else [every[e] for e in range(*es)]
+            landed.setdefault(sem, [0, []])[0] += len(es)
+            landed[sem][1].append(w[-1])
+            tr.append((sent(w[-1]), sent(r[-1]), T.sem[sem], to, sum(1 << e for e in es), len(es)))
 
         def make(q):
             if len(tr) > 1:
-                return g.remote_dma_fused(tr, local_sem=T.sem.sent)
-            return g.remote_dma(whole(src[:2] + str(i)), whole(src), T.sem["a%s%d" % (src[1], i)], T.sem.sent, a[1], a[0], sum(1 << e for e in sets[es]))
-        r = [view(src)] + ([view("skew")] if OPT["skew"] == 2 and i else [])
-        remote.append(op({"g": 400}, make, r, [view(src[:2] + str(j)) for j, _ in to], "sent", sum(len(sets[e]) for _, e in to), inc=False,
-                         late=OPT["far"] if i else OPT["hop"] + 600 * (src == "qw"), after=remote[-1:]))
+                return g.remote_dma_fused([RemoteDMATransfer(dst_ids=[DstId(rid=to[0], pnc=to[1])], dma_engine_mask=m, remote_sem=s, src=x, dst=y)
+                                           for y, x, s, to, m, _ in tr], local_sem=T.sem.sent)
+            y, x, s, to, m, _ = tr[0]
+            return g.remote_dma(y, x, s, T.sem.sent, to[1], to[0], m)
+        if OPT["skew"] == 2 and moves[0][3]:
+            r.append(view("skew"))
+        if OPT["skew"] == 3 and moves[0][3]:
+            r.append(("flat", 0, 2, 1, 0, 1))
+        remote.append(op({"g": 400}, make, r, w, "sent", sum(t[5] for t in tr), inc=False, late=late, after=remote[-1:]))
 
     quant("u", 0, 128, view("ub"))
     op({"v": 50 + UP * OPT["gather"]},
@@ -503,6 +523,10 @@ def rank_program(g, core, T, topo):
         if k == OPT["near"]:
             unit_tiles(remote[-1:])
         remote_call(*step)
+    iota(view("wrap"), [[0, 2], [1, C]], 0, 0, remote[-1:])
+    if OPT["vlate"]:
+        dma("s", T.vb[:], T.v[:], [view("skew")], [view("vb")], "lvb", late=9000)
+    quant("v", 0, 128, view("vb"))
 
     def path_list():
         scan(view("se2"), view("m16"), view("erow"))
@@ -693,20 +717,19 @@ def rank_program(g, core, T, topo):
             to_list("il", view("einv"), "sa", c16)
 
     def finish():
-        steps()
-        scan(view("acum", 0, 9), view("dcum", 0, 9), view("zer", 0, 9), A.add, A.add)
-        move("v", view("acol"), by(view("acum", 0, 9), col("aoff", 0)))
-        ts(view("ek"), view("ej"), col("acol", 0), None, A.add)
+        scan(view("acum", 0, 9), view("keep", 0, 9), view("dcum", 0, 9), A.mult, A.add)
+        ts(view("ek"), view("ej"), col("acum", 8), None, A.subtract)
         ts(view("em"), view("ek"), 255, None, A.bitwise_and)
-        move("v", view("jl"), view("em"))
-        move("a", view("optab"), by(view("iot"), view("jl")))
+        scan(view("acol", 0, 9), view("keep", 0, 9), bank(COUNTS, 0, 72, 8), A.mult, A.add)
+        ts(view("jl"), view("em"), col("acol", 8), None, A.subtract)
+        move("a", view("optab"), by(view("wrap"), view("jl")))
         if OPT["last"] == "ranks":
             sort(False)
-            mm(RANKS[1], C, ("k", 0, "c", 0))
+            mm(SIGNS[1], C, ("k", 0, "c", 0))
             for h in range(2):
                 op({"a": length("a", view("ta", 0, 128))},
-                   lambda q, h=h: S.activation(T.ta[:, 128 * h:128 * h + 128], ap(bank(RANKS[1], 128 * h, 128 * h + 128)), IDENT, bias=64.0 if short[h] == c80 else 128.0),
-                   [bank(RANKS[1])], [view("ta", 128 * h, 128 * h + 128)])
+                   lambda q, h=h: S.activation(T.ta[:, 128 * h:128 * h + 128], ap(bank(SIGNS[1], 128 * h, 128 * h + 128)), IDENT, bias=64.0 if short[h] == c80 else 128.0),
+                   [bank(SIGNS[1])], [view("ta", 128 * h, 128 * h + 128)])
             move("a", view("tb"), by(view("ta"), view("il")))
             to_list("el", view("tb"), "sr", c16)
             unpack()
@@ -723,13 +746,13 @@ def rank_program(g, core, T, topo):
         move("a", view("oprow"), by(view("optab"), view("cl")))
         for h in range(2):
             mm(3 + 4 * h, 128, ("v", 0, "x", 128 * h))
-            move("av"[h], view("yb", 128 * h, 128 * h + 128), bank(3 + 4 * h, 0, 128))
-        dma("s", T.oc[:], T.qx[:].bitcast(dt.uint8), [view("qx")], (), "outs")
+            move("va", view("yb", 128 * h, 128 * h + 128), bank(3 + 4 * h, 0, 128))
+        dma("sa", T.oc[:], T.qx[:].bitcast(dt.uint8), [view("qx")], (), "outs", late=500)
         for k in range(4):
-            dma("sa"[k // 2], T.osc[4 * k:4 * k + 4, :], T.sx[32 * k:32 * k + 4, :], [view("sx")], (), "out" + "sa"[k // 2])
+            dma("sa", T.osc[4 * k:4 * k + 4, :], T.sx[32 * k:32 * k + 4, :], [view("sx")], (), "outs")
         for h in range(2):
-            dma("s", T.y[:, 128 * h:128 * h + 128], T.yb[:, 128 * h:128 * h + 128], [view("yb", 128 * h, 128 * h + 128)], (), "outs")
-        dma("a", T.op[:], T.oprow[0:128:16, :], [view("oprow")], (), "outa")
+            dma("sa", T.y[:, 128 * h:128 * h + 128], T.yb[:, 128 * h:128 * h + 128], [view("yb", 128 * h, 128 * h + 128)], (), "outs", late=300)
+        dma("sa", T.op[:], T.oprow[0:128:16, :], [view("oprow")], (), "outs")
 
     for i in range(3):
         gather(i == 0, "crow" if i else "erow", "f")
@@ -746,15 +769,16 @@ def rank_program(g, core, T, topo):
     known = {q: {} for q in Q}
     count = {}
     touched = {}
-    for sem, n in landed.items():
+    for sem, (n, views) in landed.items():
         count[sem] = n
-        for name in ("q" + sem[1:], "s" + sem[1:]):
-            touched[name] = [(marks(view(name)), True, (sem, n, {sem: n}, 0, "x"))]
+        for x in views:
+            touched.setdefault(x[0], []).append((marks(x), True, (sem, n, {sem: n}, 0, "x")))
     for serial, (k, q) in enumerate(PLAN["order"]):
         c = calls[k]
         mine = [(x, False) for x in c["r"]] + [(x, True) for x in c["w"] if c["inc"]]
         evs = [ev for x, writes in mine for y, wrote, ev in touched.get(x[0], [])
-               if meet(x, y) and (writes or wrote or (x[0] == "ps" and ev[4] != q))]
+               if meet(x, y) and (writes or wrote or (x[0] == "ps" and ev[4] != q))
+               and not (OPT["inorder"] and writes and ev[0] == "c" + q and not c["sem"] and q in "va")]
         for ev in sorted(evs, key=lambda e: -e[3]):
             if known[q].get(ev[0], 0) < ev[1]:
                 Q[q].wait_ge(T.sem[ev[0]], ev[1])

from concourse.bass import DstId, RemoteDMATransfer
from concourse.mybir import dt, AluOpType, ActivationFunctionType

A = AluOpType
COPY = ActivationFunctionType.Copy
SIGN = ActivationFunctionType.Sign
IDENT = ActivationFunctionType.Identity
C = 256
TURN = [1, 2, 4]
UP = 192
X4 = "float8_e4m3fn_x4"
OPT = {"wake": 150, "bias": 120, "gather": 1.2, "scatter": 2.6, "load": 2000, "hop": 2600, "far": 5000, "passes": 6,
       "other": "a", "cuts": (16, 32, 42), "casts": "vavaavav", "big": "vava",
       "join": "aa", "m": "va", "crow": "va", "left": "aaa", "right": "aaaa", "dbl": "v", "swap": "vv", "rhalf": 0,
       "skew": 0, "sends": (("sw", (0, "every")), ("qw", (0, "every")), ("qup", (0, "every")), ("sup", (0, "every")), ("qw", (1, "far")),
                            ("sw", (1, "low"), (2, "high")), ("qup", (1, "far")), ("sup", (1, "low"), (2, "high")), ("qw", (2, "far")), ("qup", (2, "far"))),
       "rule": "time", "ahead": 100, "rivals": 8, "grain": 60, "tie": 1, "mix": 1.0, "eg": 1, "holes": 3, "plate": 300,
       "mend": 60, "reach": 2, "even": 0.05, "fold": 0, "fleft": "aaaa", "ml": "va",
       "lift": 0, "direct": 1, "triple": "va", "last": "scatter", "pieces": 1, "loads": {"s": "SWuxv", "a": "01234567"}}
OPT.update(wake=200, hop=3600, last="ranks", triple="va", skew=2, table=3000, inorder=1, near=4, far=3500, casts=("va",) * 8, dbl="va", fold=0, rule="mend", passes=1, mend=40, rhalf=1)
FAR = ((3500, ("qw", 0, 512, 1, "far", "aw1")), (3500, ("sw", 0, 512, 1, "low", "aw1"), ("sw", 0, 512, 2, "high", "aw2")),
       (3500, ("qup", 0, UP, 1, "far", "au1")), (3500, ("sup", 0, UP, 1, "low", "au1"), ("sup", 0, UP, 2, "high", "au2")),
       (3500, ("qw", 0, 512, 2, "far", "aw2")), (3500, ("qup", 0, UP, 2, "far", "au2")))
NEAR_U = ((2400, ("qup", 0, UP, 0, "every", "au0")), (2400, ("sup", 0, UP, 0, "every", "au0")))
OPT.update(inorder=0, issue=100, vlate=1, near=5, loads={"s": "S135ABx", "a": "02467u"}, skew=3, plate=-400, table=0, holes=7, early=3000, least=0.05, passes=3,
           sends=((1800, ("sw", 0, 512, 0, "every", "aw0")), (1900, ("qw", 0, 256, 0, "every", "aw0")), (2400, ("qw", 256, 512, 0, "every", "ax0")))
           + NEAR_U + FAR)


def _pair(name, n):
    return {"q" + name: ("sbuf", [128, n], X4), "s" + name: ("sbuf", [128, n], "uint8")}


def _of(dtype, n, *names):
    return {k: ("sbuf", [128, n], dtype) for k in names}


SCRATCH = {"ps": ("psum", [128, 4096], "float32"), "flat": ("dram", [1, 129 * C], "bfloat16"), "skew": ("sbuf", [128, C + 16], "bfloat16")}
for _d in (_of("bfloat16", 4 * C, "xb", "ft", "ht", "ct"), _of("bfloat16", 512, "ub", "vb", "kp", "kn", "tl"), _of("float32", 4 * C, "st"),
           _of("bfloat16", 4 * 136, "gt"), _of("bfloat16", 528, "ea", "eb"), _of("bfloat16", 3 * C, "s3", "r3"),
           _of("int32", 144, "lst", "li", "lj"), _of("uint16", 144, "off"), _of("uint16", 16, "o6", "o2", "jl", "el", "rl", "cl", "ul", "il", "moff", "goff", "uoff"),
           _of("bfloat16", C, "iot", "ta", "tb", "ra", "rb", "rc", "m16", "sa", "sb", "sr", "se2", "sg2", "orow", "oswp", "mrow", "me", "crow",
               "erow", "einv", "optab", "rho", "brow"), _of("uint16", 16, "o0", "bl"), _of("bfloat16", 2 * C, "ml"),
           _of("bfloat16", 128, "m4", "tri"), _of("float32", C, "sf32", "oprow", "yb"), _of("uint16", 64, "l4"),
           _of("int32", 16, "eli", "ei", "ej", "ek", "em", "ip", "iq"), _of("uint16", 2, "aoff"),
           _of("float32", 16, "col", "acol", "dcum", "acum", "keep", "scol", "dcol"), _of("bfloat16", 2 * C, "wrap"), _of("float32", 32, "cc", "dm", "a1", "a2"),
           _of("bfloat16", 32, "msm")):
    SCRATCH.update(_d)
for _n, _k in (("w", 512), ("w0", 512), ("w1", 512), ("w2", 512), ("u", 128), ("up", UP), ("u0", UP), ("u1", UP), ("u2", UP),
               ("v", 128), ("f", C), ("h", C), ("c", C), ("g", 136), ("e", 512), ("k", C), ("x", C)):
    SCRATCH.update(_pair(_n, _k))

SEMAPHORES = ["cv", "ca", "ct", "cg", "lp", "lsw", "lqw", "lub", "lxb", "lvb", "sent", "laid", "skewed",
              "aw0", "aw1", "aw2", "au0", "au1", "au2", "outs", "ax0", "lqx"]
SIZE = {"float32": 4, "int32": 4, X4: 4, "bfloat16": 2, "uint16": 2, "uint8": 1}
CYCLE = 0.83


def view(name, a=0, b=None, step=1, p0=0, p1=128):
    return (name, a, SCRATCH[name][1][1] if b is None else b, step, p0, p1)


def width(x):
    return len(range(x[1], x[2], x[3]))


def marks(x):
    if x[0] == "ps":
        return ("ps", 1 << (x[1] // 512), 1)
    return (x[0], sum(1 << c for c in range(x[1], x[2], x[3])), (1 << x[5]) - (1 << x[4]))


def meet(a, b):
    return a[0] == b[0] and a[1] & b[1] and a[2] & b[2]


def plan(calls):
    n, wake = len(calls), OPT["wake"]
    before = [{} for _ in calls]
    seen = {}
    for k, c in enumerate(calls):
        before[k].update((j, 0) for j in c["after"])
        for x, writes in [(x, False) for x in c["r"]] + [(x, True) for x in c["w"]]:
            for j, y, wrote in seen.get(x[0], []):
                if j != k and (writes or wrote) and meet(x, y):
                    if OPT["inorder"] and writes and list(c["cost"]) == list(calls[j]["cost"]) in (["v"], ["a"]):
                        before[k].setdefault(j, 0)
                    else:
                        before[k][j] = calls[j]["late"] + wake
            seen.setdefault(x[0], []).append((k, x, writes))
    after = [{} for _ in calls]
    for k in range(n):
        for j, lag in before[k].items():
            after[j][k] = lag

    def lay(rank, edges, first, fixed):
        busy = {q: [] for q in "vatgs"}
        banks = {}
        start, end, on = [0.0] * n, [0.0] * n, [None] * n
        left = [len(edges[0][k]) for k in range(n)]
        ready = [k for k in range(n) if not left[k]]
        while ready:
            k = max(ready, key=lambda j: (rank[j], -j))
            ready.remove(k)
            c = calls[k]
            t0 = max([end[j] + lag for j, lag in edges[0][k].items()] + [first[k]])
            held = [x[1] for x in c["r"] + c["w"] if x[0] == "ps"]
            best = None
            for q, cost in c["cost"].items():
                if fixed and fixed[k] != q:
                    continue
                taken = sorted(busy[q] + [(a - wake, b + wake) for m in held for a, b, o in banks.get(m, []) if o != q])
                t = t0
                for a, b in taken:
                    if t + cost <= a:
                        break
                    t = max(t, b)
                score = t + cost + (OPT["bias"] if q == "v" else 0)
                if best is None or score < best[0]:
                    best = (score, q, t, cost)
            _, q, t, cost = best
            start[k], end[k], on[k] = t, t + cost, q
            busy[q].append((t, t + cost))
            for m in held:
                banks.setdefault(m, []).append((t, t + cost, q))
            for j in edges[1][k]:
                left[j] -= 1
                if not left[j]:
                    ready.append(j)
        return start, end, on

    rank = [0.0] * n
    for k in reversed(range(n)):
        rank[k] = min(calls[k]["cost"].values()) + max([rank[j] + lag for j, lag in after[k].items()] + [calls[k]["late"]])
    best = None
    PLAN["chain"] = max(rank)
    rank = [r + c["lift"] for r, c in zip(rank, calls)]
    late = [c["late"] for c in calls]

    def forward(rank):
        free = {q: 0.0 for q in "vatgs"}
        banks = {}
        start, end, on = [0.0] * n, [0.0] * n, [None] * n
        left = [len(before[k]) for k in range(n)]
        ready = {k: 0.0 for k in range(n) if not left[k]}
        while ready:
            can = []
            for k, t0 in ready.items():
                t0 = max([t0] + [banks[x[1]][0] + wake * (banks[x[1]][1] != q) for x in calls[k]["r"] + calls[k]["w"]
                                 if x[0] == "ps" and x[1] in banks for q in calls[k]["cost"]])
                q = min(calls[k]["cost"], key=lambda q: max(t0, free[q]) + calls[k]["cost"][q] + OPT["bias"] * (q == "v"))
                can.append((max(t0, free[q]) + calls[k]["cost"][q], max(t0, free[q]), q, k))
            first = min(can)
            q = first[2]
            rivals = sorted([c for c in can if c[2] == q and c[1] < first[0] + OPT["ahead"]], key=lambda c: -rank[c[3]])[:OPT["rivals"]]

            def worst(c):
                t, most = c[0], c[1] + rank[c[3]]
                for d in rivals:
                    if d is not c:
                        t = max(t, d[1])
                        most = max(most, t + rank[d[3]])
                        t += d[0] - d[1]
                return (round(most / OPT["grain"]), c[1] if OPT["tie"] else -rank[c[3]])
            end_k, t, q, k = min(rivals, key=worst)
            del ready[k]
            start[k], end[k], on[k], free[q] = t, end_k, q, end_k
            for x in calls[k]["r"] + calls[k]["w"]:
                if x[0] == "ps":
                    banks[x[1]] = (end_k, q)
            for j, lag in after[k].items():
                left[j] -= 1
                if not left[j]:
                    ready[j] = max(end[i] + g for i, g in before[j].items())
        return start, end, on

    if "search" in OPT:
        return OPT["search"](lay, forward, rank, before, after, late, calls)
    banks_of = [[x[1] for x in c["r"] + c["w"] if x[0] == "ps"] for c in calls]

    def timed(seq, on):
        last, held, end, why, total, k0 = {}, {}, [0.0] * n, [None] * n, 0.0, None
        for k in seq:
            q, t = on[k], 0.0
            if q in last:
                t, why[k] = end[last[q]], (last[q], True)
            for j, lag in before[k].items():
                if end[j] + lag > t:
                    t, why[k] = end[j] + lag, (j, False)
            for b in banks_of[k]:
                if b in held and on[held[b]] != q and end[held[b]] + wake > t:
                    t, why[k] = end[held[b]] + wake, (held[b], True)
                held[b] = k
            end[k], last[q] = t + calls[k]["cost"][q], k
            if end[k] + late[k] > total:
                total, k0 = end[k] + late[k], k
        pairs = []
        while why[k0]:
            if why[k0][1]:
                pairs.append((why[k0][0], k0))
            k0 = why[k0][0]
        return total + OPT["even"] * sum(end) / n, pairs

    def moved(seq, k, j, edges):
        a, b = seq.index(k), seq.index(j)
        span = seq[a:b + 1] if a < b else seq[b:a + 1][::-1]
        need, take, rest = {k}, [], []
        for x in span:
            (take if x in need else rest).append(x)
            if x in need:
                need.update(edges[x])
        if j in need:
            return None
        return seq[:a] + rest + take + seq[b + 1:] if a < b else seq[:b] + take[::-1] + rest[::-1] + seq[a + 1:]

    def mended(seq, on):
        total, pairs = timed(seq, on)
        at = idle = 0
        while idle < len(pairs):
            u, v = pairs[at % len(pairs)]
            mates = [x for x in seq if on[x] == on[u]]
            a = mates.index(u)
            tries = [(moved(seq, v, x, before), on) for x in mates[max(0, a - OPT["reach"]):a + 1]]
            tries += [(moved(seq, u, x, before), on) for x in mates[max(0, a - OPT["reach"]):a]]
            tries += [(moved(seq, u, x, after), on) for x in mates[a + 1:a + 2 + OPT["reach"]]]
            tries += [(seq, on[:x] + [q] + on[x + 1:]) for x in (u, v) for q in calls[x]["cost"] if q != on[x]]
            found = min([timed(s, o) + (s, o) for s, o in tries if s], key=lambda f: f[0], default=None)
            if found and found[0] < total - OPT["least"]:
                total, pairs, seq, on = found
                idle = 0
            else:
                at, idle = at + 1, idle + 1
        return total, seq, on

    if OPT["rule"] == "mend":
        for _ in range(OPT["passes"]):
            start, end, on = forward(rank)
            found = mended(sorted(range(n), key=lambda k: (start[k], k)), on)
            if best is None or found[0] < best[0]:
                best = found
            rank = [b + c["lift"] for b, c in zip(lay(end, (after, before), late, on)[1], calls)]
        PLAN["length"] = best[0]
        return [(k, best[2][k]) for k in best[1]]
    if OPT["rule"] == "time":
        for _ in range(OPT["passes"]):
            start, end, on = forward(rank)
            total = max(e + t for e, t in zip(end, late))
            if best is None or total < best[0]:
                best = (total, start, on)
            back = lay(end, (after, before), late, on)[1]
            rank = [OPT["mix"] * (b + c["lift"]) + (1 - OPT["mix"]) * r for b, r, c in zip(back, rank, calls)]
        PLAN["length"] = best[0]
        return [(k, best[2][k]) for k in sorted(range(n), key=lambda k: (best[1][k], k))]
    for _ in range(OPT["passes"]):
        start, end, on = lay(rank, (before, after), [0.0] * n, None)
        total = max(e + t for e, t in zip(end, late))
        if best is None or total < best[0]:
            best = (total, start, on)
        rank = lay(end, (after, before), late, on)[1]
    PLAN["length"] = best[0]
    return [(k, best[2][k]) for k in sorted(range(n), key=lambda k: (best[1][k], k))]


PLAN = {}


def rank_program(g, core, T, topo):
    rank = T.rank_of(core)
    if rank is None:
        return
    Q = {"v": g.vector, "a": g.scalar, "t": g.tensor, "g": g, "s": g.sync}
    V, S, PE = g.vector, g.scalar, g.tensor
    calls = []
    lift = [0]

    def ap(x):
        if not isinstance(x, tuple):
            return x
        if x[0] == "by":
            return ap(x[1]).indirect(ap(x[2]))
        return T[x[0]][x[4]:x[5], x[1]:x[2]:x[3]]

    def by(win, off):
        return ("by", win, off)

    def parts(xs):
        out = []
        for x in xs:
            if isinstance(x, tuple):
                out += [x[1], x[2]] if x[0] == "by" else [x]
        return out

    def op(cost, make, r=(), w=(), sem=None, n=1, upto=None, inc=True, late=0, after=()):
        calls.append({"cost": cost, "make": make, "r": [marks(x) for x in parts(r)], "w": [marks(x) for x in parts(w)],
                      "sem": sem, "n": n, "upto": upto, "inc": inc, "late": late, "after": list(after), "lift": lift[0]})
        return len(calls) - 1

    def length(q, out, *ins):
        if out[0] == "by":
            return 50 + 16 * width(out[2]) * OPT["scatter"]
        if ins and ins[0][0] == "by":
            return (50 if q == "v" else 65) + width(out) * OPT["gather"]
        if q == "a":
            return 60 + width(out) * CYCLE
        narrow = all(SIZE[SCRATCH[x[0]][2]] == 2 for x in (out,) + ins)
        return max(64, width(out) * (0.5 if narrow else 1)) * CYCLE

    def bank(k, a=0, b=C, step=1):
        return view("ps", 512 * k + a, 512 * k + b, step)

    def ts(out, in0, s1, s2, op0, op1=None):
        more = () if op1 is None else (op1,)
        op({"v": length("v", out, in0)}, lambda q: V.tensor_scalar(ap(out), ap(in0), ap(s1), ap(s2), op0, *more), [in0, s1, s2], [out])

    def tt(out, in0, in1, how):
        twice = 1 if "ps" in (in0[0], in1[0]) else 2
        op({"v": max(64, width(out) * twice) * CYCLE}, lambda q: V.tensor_tensor(ap(out), ap(in0), ap(in1), how), [in0, in1], [out])

    def move(qs, out, in_, scale=None):
        def make(q):
            if q == "a":
                return S.activation(ap(out), ap(in_), COPY) if scale is None else S.activation(ap(out), ap(in_), COPY, scale=scale)
            return V.tensor_copy(ap(out), ap(in_)) if scale is None else V.tensor_scalar(ap(out), ap(in_), scale, None, A.mult)
        r, w = ([in_, out[2]], [out[1]]) if out[0] == "by" else ([in_], [out])
        op({q: length(q, out, in_) for q in qs}, make, r, w)

    def halves(qs, out, win, off):
        if len(qs) == 1:
            move(qs, view(out, 0, C), by(win, view(off, 0, 16)))
        else:
            for h in range(2):
                move(qs[h], view(out, 128 * h, 128 * h + 128), by(win, view(off, 8 * h, 8 * h + 8)))

    def fill(out, c):
        op({"v": length("v", out)}, lambda q: V.memset(ap(out), c), (), [out])

    def sign(out, in_, bias, scale):
        op({"a": length("a", out)}, lambda q: S.activation(ap(out), ap(in_), SIGN, bias=ap(bias), scale=scale), [in_, bias], [out])

    def quant(name, a, n, tile):
        q, s = view("q" + name, a, a + n), view("s" + name, a, a + n)
        op({"v": 12 + 0.88 * n}, lambda _: V.quantize_mx(ap(q), ap(s), ap(tile)), [tile], [q, s])

    def mm(k, n, *sides):
        vs = [(view("q" + a, a0, a0 + 128), view("s" + a, a0, a0 + 128), view("q" + b, b0, b0 + n), view("s" + b, b0, b0 + n)) for a, a0, b, b0 in sides]

        def make(q):
            return [PE.matmul_mx(ap(bank(k, 0, n)), ap(x[0]), ap(x[1]), ap(x[2]), ap(x[3]), j == 0, j == len(vs) - 1) for j, x in enumerate(vs)][-1]
        op({"t": len(vs) * (n + 16) * 0.6}, make, [y for x in vs for y in x], [bank(k, 0, n)])

    def scan(out, d0, d1, op0=A.add, op1=A.min):
        op({"v": length("v", out, d0, d1)}, lambda q: V.tensor_tensor_scan(ap(out), ap(d0), ap(d1), 0.0, op0, op1), [d0, d1], [out])

    def iota(out, pattern, base, mult, after=()):
        more = {} if SCRATCH[out[0]][2] == "int32" else {"allow_small_or_imprecise_dtypes": True}
        op({"g": 130 + 2 * CYCLE * width(out)}, lambda q: g.iota(ap(out), pattern, base, mult, **more), (), [out], after=after)

    def dma(q, out, in_, r, w, sem, upto=None, late=0, after=()):
        return op({x: OPT["issue"] for x in q}, lambda x: Q[x].dma_start(out, in_), r, w, sem, 16, upto, late=OPT["load"] + late, after=after)

    def col(name, k):
        return view(name, k, k + 1)

    def to_list(out, row, tmp, plus, a=0, b=C):
        scan(view(tmp, a, b), view("m16", 0, b - a), row)
        ts(view(out, a // 16, b // 16), view(tmp, a + 15, b, 16), plus, None, A.add)

    pcol, icol, qcol, tcol, c16, c4, c80, tmp, tmq, tmr = [col("col", k) for k in range(10)]

    def rotor(s):
        return lambda q, after: dma(q, T.lst[16 * s:128, 16 * s + 16:16 * s + 32], T.p[0:128 - 16 * s, :], (),
                                    [view("lst", 16 * s + 16, 16 * s + 32, 1, 16 * s)], "lp", 128, late=OPT["plate"], after=after)

    def load(name, out, in_, late):
        return lambda q, after: dma(q, out, in_, (), [view(name)], "l" + name, late=late, after=after)
    loads = {"S": load("sw", T.sw[:], T.ws[:], 200), "W": load("qw", T.qw[:].bitcast(dt.uint8), T.wc[:], 900), "u": load("ub", T.ub[:], T.u[:], 1200),
             "x": load("xb", T.xb[:], T.x[:], 1600), "v": load("vb", T.vb[:], T.v[:], 1600)}
    loads.update((str(s), rotor(s)) for s in range(8))
    for k, name in enumerate("AB"):
        loads[name] = lambda q, after, k=k: dma(q, T.qw[:, 256 * k:256 * k + 256].bitcast(dt.uint8), T.wc[:, 1024 * k:1024 * k + 1024], (),
                                                [view("qw", 256 * k, 256 * k + 256)], ("lqw", "lqx")[k], late=500 + 400 * k, after=after)
    for q, names in OPT["loads"].items():
        prev = []
        for name in names:
            lift[0] = 1e6
            prev = [loads[name](q, prev)]
    lift[0] = 0

    lift[0] = OPT["early"]
    iota(view("ip", 0, 10), [[-16, 10]], 16, 1)
    iota(view("cc", 0, 16), [[1, 16]], 0, 0)
    iota(view("cc", 16, 32), [[0, 4], [1, 4]], 0, 0)
    iota(view("iot"), [[1, C]], 0, 0)
    p32 = col("ip", 1)
    ts(col("iq", 0), p32, 15, None, A.bitwise_and)
    ts(col("iq", 1), p32, 2, 3, A.arith_shift_right, A.bitwise_and)
    ts(col("iq", 2), p32, 3, None, A.bitwise_and)
    ts(col("iq", 3), p32, 4, None, A.arith_shift_right)
    move("v", pcol, p32)
    move("v", view("col", 1, 4), view("iq", 0, 3))
    ts(tmp, icol, -16.0, None, A.add)
    ts(view("goff", 1, 10), view("ip", 1, 10), tmp, 16.0, A.max, A.add)
    move("v", col("goff", 0), icol)
    ts(view("lst", 0, 16), view("cc", 0, 16), 16.0, icol, A.mult, A.add)
    for s in range(1, 8):
        if s > OPT["holes"]:
            iota(view("lst", 16 * s + 16, 16 * s + 32, 1, 0, 16 * s), [[0, 16]], 0, 0)
        else:
            fill(view("lst", 16 * s + 16, 16 * s + 32, 1, 0, 16 * s), 0)
    ts(view("dm", 0, 16), view("cc", 0, 16), icol, None, A.subtract)
    ts(view("dm", 16, 32), view("cc", 16, 32), qcol, None, A.subtract)
    ts(view("moff"), view("cc", 0, 16), 0.0, icol, A.mult, A.add)
    ts(view("a1"), view("dm"), 0.0, 1024.0, A.is_equal, A.mult)
    ts(view("a2"), view("dm"), 1.0, -256.0, A.is_equal, A.mult)
    tt(view("msm"), view("a1"), view("a2"), A.add)
    move("a", view("m16"), by(view("msm", 0, 16), view("moff")))
    move("a", view("m4"), by(view("msm", 16, 32), view("moff", 0, 8)))
    lift[0] = 0
    ts(c16, icol, 15.0, 256.0, A.is_lt, A.mult)
    ts(c80, c16, 64.0, None, A.add)
    mirror, tms = col("col", 11), col("col", 12)
    ts(mirror, c16, -1.0, 255.0, A.mult, A.add)
    short = (c80, c80)
    if OPT["other"] == "a":
        short = (c80, col("col", 10))
        ts(short[1], c16, 128.0, None, A.add)
    ts(tmq, qcol, 3.0, 1024.0, A.is_lt, A.mult)
    ts(c4, tmq, tcol, None, A.add)
    ts(tmr, icol, 8.0, 16.0, A.is_ge, A.mult)
    ts(view("dm", 0, 4), view("cc", 0, 4), 32.0, 1.0, A.mult, A.add)
    ts(view("uoff", 0, 4), view("dm", 0, 4), tmr, None, A.add)
    fill(view("uoff", 4, 12), 0)
    ts(col("col", 13), col("iq", 3), 1.0, None, A.add)
    ts(view("keep", 0, 9), view("cc", 0, 9), col("col", 13), None, A.not_equal)

    fill(view("gt"), 0.0)

    def unit_tiles(after):
        for name, at in (("ea", 2), ("eb", 3)):
            if OPT["eg"]:
                op({"g": 170 + 2 * CYCLE * 528}, lambda q, name=name, at=at: g.affine_select(T[name][:], T.gt[:, 0:528], [[1, 528]], A.not_equal, 1.0, -at, -4),
                   [view("gt")], [view(name)], after=after)
            else:
                fill(view(name), 0.0)
                ts(view(name, at, at + 512, 4), view("iot", 0, 128), pcol, None, A.is_equal)
        for b in range(4):
            at = 2 - 2 * (b // 2)
            quant("e", 128 * b, 128, view(("ea", "eb")[b % 2], at, at + 512))
    for t, c in enumerate((0.5, 0.5, -0.5, 1.0)):
        fill(view("kp", t, 512, 4), c)
        fill(view("kn", t, 512, 4), -c)
    quant("k", 0, 128, view("kp"))
    quant("k", 128, 128, view("kn"))
    ts(view("tri"), view("iot", 0, 128), pcol, None, A.is_gt)
    fill(view("dcum"), 0.0)

    peers = [T.cores[rank ^ h] for h in TURN]
    every = topo.engines(core, peers[0])
    far = topo.engines(core, peers[1])
    near = [e for e in every if e not in far]
    sets = {"every": every, "far": far, "near": near, "low": far[:len(far) // 2], "high": far[len(far) // 2:]}
    remote = []
    landed = {}

    def sent(x):
        return ap(x).bitcast(dt.uint8) if x[0][0] == "q" else ap(x)

    def remote_call(late, *moves):
        tr, r, w = [], [], []
        for src, a, b, i, es, sem in moves:
            to = topo.addr(peers[i])
            r.append(view(src, a, b))
            w.append(view(src[:2] + str(i), a, b))
            es = sets[es] if isinstance(es, str) else [every[e] for e in range(*es)]
            landed.setdefault(sem, [0, []])[0] += len(es)
            landed[sem][1].append(w[-1])
            tr.append((sent(w[-1]), sent(r[-1]), T.sem[sem], to, sum(1 << e for e in es), len(es)))

        def make(q):
            if len(tr) > 1:
                return g.remote_dma_fused([RemoteDMATransfer(dst_ids=[DstId(rid=to[0], pnc=to[1])], dma_engine_mask=m, remote_sem=s, src=x, dst=y)
                                           for y, x, s, to, m, _ in tr], local_sem=T.sem.sent)
            y, x, s, to, m, _ = tr[0]
            return g.remote_dma(y, x, s, T.sem.sent, to[1], to[0], m)
        if OPT["skew"] == 2 and moves[0][3]:
            r.append(view("skew"))
        if OPT["skew"] == 3 and moves[0][3]:
            r.append(("flat", 0, 2, 1, 0, 1))
        remote.append(op({"g": 400}, make, r, w, "sent", sum(t[5] for t in tr), inc=False, late=late, after=remote[-1:]))

    quant("u", 0, 128, view("ub"))
    op({"v": 50 + UP * OPT["gather"]},
       lambda q: V.tensor_copy(T.qup[:].bitcast(dt.uint32), T.qu[:].bitcast(dt.uint32).indirect(T.uoff[:, 0:12])),
       [view("qu"), view("uoff", 0, 12)], [view("qup")])
    move("va", view("sup"), by(view("su"), view("uoff", 0, 12)))

    def lists(m):
        return view("off", 16 * m, 16 * m + 16)

    for a, b in ((8, 9), (4, 8), (0, 4)):
        move("v", view("off", 16 * a, 16 * b), by(view("lst"), view("goff", a, b)))
    mid = lambda name: view(name, C, 2 * C)
    for q, rows, m in (("a", (view("iot"), mid("s3"), view("ta"), view("tb"), view("tl", 0, C)), 8),
                       ("v", (view("iot"), mid("r3"), view("ra"), view("rb"), view("rc")), 4)):
        for s in range(4):
            move(q, rows[s + 1], by(rows[s], lists(m - s)))
    to_list("jl", view("rc"), "sr", c16)
    halves("va", "erow", view("tl", 0, C), "jl")
    for name in ("s3", "r3")[OPT["fold"]:]:
        for a in (0, 2 * C):
            move(OPT["triple"], view(name, a, a + C), mid(name))
    move("v", view("lj", 0, 128 + 16 * OPT["fold"]), view("off", 0, 128 + 16 * OPT["fold"]))
    fill(view("lj", 64, 80), 0)
    if OPT["skew"]:
        late_table = OPT["table"]
        move("a", view("rho"), by(view("iot"), lists(1)))
        dma("s", T.flat[0:1, 0:128 * C], T.rho[:], [view("rho")], [("flat", 0, 1, 1, 0, 1)], "laid", 32)
        dma("s", T.flat[0:1, 128 * C:129 * C], T.rho[0:1, :], [view("rho")], [("flat", 1, 2, 1, 0, 1)], "laid", 32)
        dma("s", T.skew[:, 0:C + 1], T.flat[0:1, 0:128 * (C + 1)], [("flat", 0, 2, 1, 0, 1)], [view("skew")], "skewed", late=late_table)
        ts(tms, col("iq", 3), -1.0, icol, A.mult, A.add)
        ts(col("lj", 0), tms, 16.0, None, A.mult)
    for k, step in enumerate(OPT["sends"]):
        if k == OPT["near"]:
            unit_tiles(remote[-1:])
        remote_call(*step)
    iota(view("wrap"), [[0, 2], [1, C]], 0, 0, remote[-1:])
    if OPT["vlate"]:
        dma("s", T.vb[:], T.v[:], [view("skew")], [view("vb")], "lvb", late=9000)
    quant("v", 0, 128, view("vb"))

    def path_list():
        scan(view("se2"), view("m16"), view("erow"))
        ts(view("lj", 128, 144), view("se2", 15, C, 16), -1.0, mirror, A.mult, A.add)

    def gather(first, row, name):
        for h in range(2):
            lift[0] = OPT["lift"] * (1 - h)
            scan(view("sb", 128 * h, 128 * h + 128), view("m4"), view(row, 128 * h, 128 * h + 128))
            ts(view("l4", 32 * h, 32 * h + 32), view("sb", 128 * h + 3, 128 * h + 128, 4), 4.0, c4, A.mult, A.add)
        cuts = (0,) + OPT["cuts"] + (64,)
        for k in range(len(cuts) - 1):
            a, b = cuts[k], cuts[k + 1]
            lift[0] = OPT["lift"] * (a < 32)
            move(OPT["big"][k], view("ft", 16 * a, 16 * b), by(view("xb" if first else "st"), view("l4", a, b)), None if first else 0.5)
        for h in range(2):
            lift[0] = OPT["lift"] * (1 - h)
            quant(name, 128 * h, 128, view("ft", 512 * h, 512 * h + 512))

    COLS, ROWS, SIGNS, COUNTS, RANKS, UNPACK = (0, 4), (1, 5), (2, 6), 3, (7, 4), (0, 1, 2, 5)

    def layer(i):
        u = "u%d" % i
        for h in range(2):
            lift[0] = OPT["lift"] * (1 - h)
            for k in range(4):
                mm(4 * h + k, 128, ("w%d" % i, 128 * k, "f", 128 * h))
            for k in range(4):
                move(OPT["casts"][4 * h + k], view("ht", 512 * h + k, 512 * h + 512, 4), bank(4 * h + k, 0, 128), 0.0078125)
            quant("h", 128 * h, 128, view("ht", 512 * h, 512 * h + 512))
        for h in range(2):
            mm(COLS[h], 128, ("h", 128 * h, u, 0))
            mm(ROWS[h], 128, (u, 64, "h", 128 * h))
            mm(SIGNS[h], 128, (u, 64, "h", 128 * h))
            move("v", col("scol", 4 * h), bank(COLS[h], 64, 65))
            ts(view("gt", 32 + 3 * h, 288, 4), bank(COLS[h], 0, 64), 0.0, 2.0 - h, A.is_gt, A.mult)
        slot = lambda h, t: view("ct", 512 * h + t, 512 * h + 512, 4)
        score = lambda h: bank(COLS[h], 64, 65) if OPT["direct"] else col("scol", 4 * h)
        for h in range(2):
            ts(slot(h, 2), bank(ROWS[h], 0, 128), score(h), None, A.is_equal)
            scan(slot(h, 3), view("tri"), slot(h, 2), A.max, A.mult)
            sign(slot(h, 1), bank(SIGNS[h], 0, 128), col("scol", 4 * h), -1.0)
        for h in range(2):
            if h and OPT["other"] == "a":
                sign(view("sg2", 0, 128), bank(SIGNS[h], 0, 128), col("scol", 0), -1.0)
                op({"a": length("a", slot(h, 0))}, lambda q: S.activation(ap(slot(1, 0)), ap(view("sg2", 0, 128)), SIGN, bias=0.5), [view("sg2", 0, 128)], [slot(1, 0)])
            else:
                ts(slot(h, 0), bank(ROWS[h], 0, 128), score(1 - h), 2.0, A.is_le if h else A.is_lt, A.mult)
        quant("g", 0, 136, view("gt"))
        mm(COUNTS, 128, ("k", 0, "g", 8), ("k", 128, "g", 0))
        for h in range(2):
            quant("c", 128 * h, 128, view("ct", 512 * h, 512 * h + 512))

    def sort(partners=True):
        if OPT["rhalf"]:
            for h in range(2):
                mm(RANKS[h], 128, ("k", 0, "c", 128 * h))
                to_list("rl", bank(RANKS[h], 0, 128), "sf32", short[h], 128 * h, 128 * h + 128)
            for h in range(2):
                move("v", by(view("orow"), view("rl", 8 * h, 8 * h + 8)), view("iot", 128 * h, 128 * h + 128))
        else:
            mm(RANKS[0], C, ("k", 0, "c", 0))
            scan(view("sf32"), view("m16"), bank(RANKS[0]))
            for a, b in ((0, C),) if short[0] == short[1] else ((0, 128), (128, C)):
                ts(view("rl", a // 16, b // 16), view("sf32", a + 15, b, 16), short[a // 128], None, A.add)
            move("v", by(view("orow"), view("rl")), view("iot"))
        for h in range(2):
            move(OPT["swap"][h], view("oswp", h, C, 2), view("orow", 1 - h, C, 2))
        if partners:
            halves(OPT["m"], "mrow", view("oswp"), "rl")

    def unpack():
        for b in range(4):
            mm(UNPACK[b], C, ("e", 128 * b, "h", 0))
            for h in range(2):
                tt(view("st", 512 * h + b, 512 * h + 512, 4), bank(UNPACK[b], 128 * h, 128 * h + 128), view("ft", 512 * h + b, 512 * h + 512, 4), A.add)

    def steps():
        tt(view("dcum", 0, 9), bank(COUNTS, 0, 72, 8), view("dcum", 0, 9), A.add)

    def turn():
        ts(view("o6"), view("lj", 112, 128), bank(COUNTS, 56, 57), 256.0, A.add, A.add)
        ts(view("o2"), view("lj", 48, 64), bank(COUNTS, 24, 25), 256.0, A.add, A.add)
        for e in range(2):
            tt(view("li", e, 144, 2), bank(COUNTS, 0, 72), view("lj", e, 144, 2), A.add)
        steps()
        ts(view("lj"), view("li"), 255, None, A.bitwise_and)
        move("v", view("off"), view("lj"))
        ts(col("dcol", 0), col("lj", 64), c16, None, A.add)
        left = ((view("s3"), view("o6")), (view("ta"), lists(6)), (view("tb"), lists(5)))
        for s, to in enumerate((view("ta"), view("tb"), view("tl", 0, C))):
            move(OPT["left"][s], to, by(*left[s]))
        if OPT["skew"]:
            ts(view("ei"), by(view("skew", 0, C), col("off", 0)), col("dcum", 1), None, A.add)
            ts(view("ej"), view("ei"), 255, None, A.bitwise_and)
            move("v", view("o0"), view("ej"))
            right = ((view("r3"), view("o2")), (view("ra"), lists(2)), (view("rb"), view("o0")))
            for s, to in enumerate((view("ra"), view("rb"), view("rc"))):
                move(OPT["right"][s], to, by(*right[s]))
        else:
            right = ((view("r3"), view("o2")), (view("ra"), lists(2)), (view("rb"), lists(1)), (view("ra"), lists(0)))
            for s, to in enumerate((view("ra"), view("rb"), view("ra"), view("rc"))):
                move(OPT["right"][s], to, by(*right[s]))
        move(OPT["dbl"], view("tl", C, 2 * C), view("tl", 0, C))
        to_list("jl", view("rc"), "sr", col("dcol", 0))
        halves(OPT["join"], "erow", view("tl"), "jl")
        for h in range(2):
            scan(view("se2", 128 * h, 128 * h + 128), view("m16", 0, 128), view("erow", 128 * h, 128 * h + 128))
            ts(view("el", 8 * h, 8 * h + 8), view("se2", 128 * h + 15, 128 * h + 128, 16), -1.0, mirror, A.mult, A.add)
        sort()
        unpack()
        move("v", by(view("me"), lists(8)), view("mrow"))
        halves(OPT["crow"], "crow", view("me"), "el")
        move("v", view("lj", 128, 144), view("el"))

    def inverse(tripled):
        to_list("ul", view("erow"), "se2", c16)
        n = 16 // OPT["pieces"]
        for a in range(0, 16, n):
            move("v", by(mid("s3"), view("ul", a, a + n)), view("iot", 16 * a, 16 * (a + n)))
        if tripled:
            for a in (0, 2 * C):
                move(OPT["triple"], view("s3", a, a + C), mid("s3"))
        else:
            to_list("il", mid("s3"), "sa", c16)

    def folded(i):
        ts(view("o6"), view("lj", 128, 144), bank(COUNTS, 64, 65), 256.0, A.add, A.add)
        ts(view("o2"), view("lj", 48, 64), bank(COUNTS, 24, 25), 256.0, A.add, A.add)
        for e in range(2):
            tt(view("li", e, 144, 2), bank(COUNTS, 0, 72), view("lj", e, 144, 2), A.add)
        steps()
        ts(view("lj"), view("li"), 255, None, A.bitwise_and)
        move("v", view("off"), view("lj"))
        ts(col("dcol", 0), col("lj", 64), c16, None, A.add)
        left = ((view("s3"), view("o6")), (view("ta"), lists(7)), (view("tb"), lists(6)), (view("ta"), lists(5)))
        for s, to in enumerate((view("ta"), view("tb"), view("ta"), view("tl", 0, C))):
            move(OPT["fleft"][s], to, by(*left[s]))
        if OPT["skew"]:
            ts(view("ei"), by(view("skew", 0, C), col("off", 0)), col("dcum", 1), None, A.add)
            ts(view("ej"), view("ei"), 255, None, A.bitwise_and)
            move("v", view("o0"), view("ej"))
            right = ((view("r3"), view("o2")), (view("ra"), lists(2)), (view("rb"), view("o0")))
            for s, to in enumerate((view("ra"), view("rb"), view("rc"))):
                move(OPT["right"][s], to, by(*right[s]))
        else:
            right = ((view("r3"), view("o2")), (view("ra"), lists(2)), (view("rb"), lists(1)), (view("ra"), lists(0)))
            for s, to in enumerate((view("ra"), view("rb"), view("ra"), view("rc"))):
                move(OPT["right"][s], to, by(*right[s]))
        to_list("el", view("tl", 0, C), "sa", c16)
        to_list("jl", view("rc"), "sr", col("dcol", 0))
        sort()
        unpack()
        for h in range(2):
            move(OPT["ml"][h], view("ml", C * h, C * h + C), by(view("mrow"), view("el")))
        halves(OPT["crow"], "crow", view("ml"), "jl")
        move(OPT["dbl"], view("tl", C, 2 * C), view("tl", 0, C))
        halves("a", "brow", view("tl"), "jl")
        to_list("bl", view("brow"), "sr", c16)
        move("a", view("me"), view("erow")) if 0 else None
        move("a", view(("me", "erow")[i]), by(view(("erow", "me")[i]), view("bl")))
        if i == 0:
            to_list("ul", view("me"), "se2", c16)
            n = 16 // OPT["pieces"]
            for a in range(0, 16, n):
                move("v", by(mid("s3"), view("ul", a, a + n)), view("iot", 16 * a, 16 * (a + n)))
            for a in (0, 2 * C):
                move(OPT["triple"], view("s3", a, a + C), mid("s3"))
        else:
            inverse(False)

    def last():
        if OPT["fold"]:
            move("v", view("ej"), view("ul"))
        else:
            unfolded()
        finish()

    def unfolded():
        ts(col("dcol", 1), col("dcum", 8), 255.0, None, A.add)
        ts(view("ei"), view("lj", 128, 144), -1.0, col("dcol", 1), A.mult, A.add)
        ts(view("ej"), view("ei"), 255, None, A.bitwise_and)
        move("v", view("ul"), view("ej"))
        if OPT["last"] != "scatter":
            n = 16 // OPT["pieces"]
            for a in range(0, 16, n):
                move("v", by(view("einv"), view("ul", a, a + n)), view("iot", 16 * a, 16 * (a + n)))
            to_list("il", view("einv"), "sa", c16)

    def finish():
        scan(view("acum", 0, 9), view("keep", 0, 9), view("dcum", 0, 9), A.mult, A.add)
        ts(view("ek"), view("ej"), col("acum", 8), None, A.subtract)
        ts(view("em"), view("ek"), 255, None, A.bitwise_and)
        scan(view("acol", 0, 9), view("keep", 0, 9), bank(COUNTS, 0, 72, 8), A.mult, A.add)
        ts(view("jl"), view("em"), col("acol", 8), None, A.subtract)
        move("a", view("optab"), by(view("wrap"), view("jl")))
        if OPT["last"] == "ranks":
            sort(False)
            mm(SIGNS[1], C, ("k", 0, "c", 0))
            for h in range(2):
                op({"a": length("a", view("ta", 0, 128))},
                   lambda q, h=h: S.activation(T.ta[:, 128 * h:128 * h + 128], ap(bank(SIGNS[1], 128 * h, 128 * h + 128)), IDENT, bias=64.0 if short[h] == c80 else 128.0),
                   [bank(SIGNS[1])], [view("ta", 128 * h, 128 * h + 128)])
            move("a", view("tb"), by(view("ta"), view("il")))
            to_list("el", view("tb"), "sr", c16)
            unpack()
            halves(OPT["crow"], "crow", view("oswp"), "el")
        else:
            sort()
            unpack()
            if OPT["last"] == "scatter":
                move("v", by(view("crow"), view("ul")), view("mrow"))
            else:
                halves(OPT["crow"], "crow", view("mrow"), "il")
        gather(False, "crow", "x")
        to_list("cl", view("crow"), "sa", c16)
        move("a", view("oprow"), by(view("optab"), view("cl")))
        for h in range(2):
            mm(3 + 4 * h, 128, ("v", 0, "x", 128 * h))
            move("va", view("yb", 128 * h, 128 * h + 128), bank(3 + 4 * h, 0, 128))
        dma("sa", T.oc[:], T.qx[:].bitcast(dt.uint8), [view("qx")], (), "outs", late=500)
        for k in range(4):
            dma("sa", T.osc[4 * k:4 * k + 4, :], T.sx[32 * k:32 * k + 4, :], [view("sx")], (), "outs")
        for h in range(2):
            dma("sa", T.y[:, 128 * h:128 * h + 128], T.yb[:, 128 * h:128 * h + 128], [view("yb", 128 * h, 128 * h + 128)], (), "outs", late=300)
        dma("sa", T.op[:], T.oprow[0:128:16, :], [view("oprow")], (), "outs")

    for i in range(3):
        gather(i == 0, "crow" if i else "erow", "f")
        if i == 0:
            inverse(True) if OPT["fold"] else path_list()
        layer(i)
        if i < 2:
            folded(i) if OPT["fold"] else turn()
        else:
            last()

    if "order" not in PLAN:
        PLAN["order"] = plan(calls)
    known = {q: {} for q in Q}
    count = {}
    touched = {}
    for sem, (n, views) in landed.items():
        count[sem] = n
        for x in views:
            touched.setdefault(x[0], []).append((marks(x), True, (sem, n, {sem: n}, 0, "x")))
    for serial, (k, q) in enumerate(PLAN["order"]):
        c = calls[k]
        mine = [(x, False) for x in c["r"]] + [(x, True) for x in c["w"] if c["inc"]]
        evs = [ev for x, writes in mine for y, wrote, ev in touched.get(x[0], [])
               if meet(x, y) and (writes or wrote or (x[0] == "ps" and ev[4] != q))
               and not (OPT["inorder"] and writes and ev[0] == "c" + q and not c["sem"] and q in "va")]
        for ev in sorted(evs, key=lambda e: -e[3]):
            if known[q].get(ev[0], 0) < ev[1]:
                Q[q].wait_ge(T.sem[ev[0]], ev[1])
                for s, n in ev[2].items():
                    known[q][s] = max(known[q].get(s, 0), n)
        ins = c["make"](q)
        sem = c["sem"] or "c" + q
        count[sem] = count.get(sem, 0) + c["n"]
        if c["inc"]:
            ins.then_inc(T.sem[sem], c["n"])
        clock = dict(known[q])
        clock[sem] = c["upto"] or count[sem]
        for x, writes in mine:
            touched.setdefault(x[0], []).append((x, writes, (sem, clock[sem], clock, serial + 1, q)))
    for s in SEMAPHORES:
        if known["g"].get(s, 0) < count.get(s, 0):
            g.wait_ge(T.sem[s], count[s])
